import numpy as np
import ml_dtypes


def mxq(x, axis, fmt="e4m3"):
    dtype, down = {"e4m3": (ml_dtypes.float8_e4m3fn, 7), "e5m2": (ml_dtypes.float8_e5m2, 14)}[fmt]
    v = np.moveaxis(np.asarray(x, np.float32).astype(ml_dtypes.bfloat16).astype(np.float64), axis, -1)
    blocks = v.reshape(v.shape[:-1] + (-1, 32))
    amax = np.abs(blocks).max(-1, keepdims=True)
    byte = np.maximum(np.where(amax > 0, np.frexp(amax)[1] - 1 + 127, 0) - down, 1)
    scale = np.exp2(byte - 127.0)
    codes = (blocks / scale).astype(np.float32).astype(dtype).astype(np.float64)
    return np.moveaxis((codes * scale).reshape(v.shape), -1, axis)


WIDE = False


def mx_kscale(k):
    if not WIDE:
        return np.ones(k)
    levels = np.array([10, -10, 5, -5, 0])
    if k % 512:
        return np.exp2(np.random.permutation(np.resize(levels, k // 32))).repeat(32)
    a = np.empty((k // 512, 16))
    for p in range(k // 512):
        a[p, :8] = np.random.permutation(np.resize(levels, 8))
        for g in range(8):
            far = levels[np.abs(levels - a[p, g]) >= 10]
            a[p, g + 8] = far[np.random.randint(len(far))]
    return np.exp2(a.ravel()).repeat(32)


def f64(x):
    return np.asarray(x).astype(np.float64)


def striped(idx):
    return np.tile(idx.reshape(-1, 16).T, (8, 1)).astype(np.uint16)


def unstriped(offs):
    return offs[:16].T.reshape(-1).astype(np.int64)


E2M1 = np.array([0.0, 0.5, 1.0, 1.5, 2.0, 3.0, 4.0, 6.0, -0.0, -0.5, -1.0, -1.5, -2.0, -3.0, -4.0, -6.0])


def pack_weight(w, fmt):
    k, n = w.shape
    w = f64(np.asarray(w, np.float32).astype(ml_dtypes.bfloat16)).reshape(k // 32, 32, n)
    amax = np.abs(w).max(1)
    if fmt == "e4m3":
        byte = np.frexp(amax)[1] - 1 + 127 - 7
    else:
        mant, ex = np.frexp(amax / 6.0)
        byte = np.where(mant > 0.5, ex, ex - 1) + 127
    byte = np.clip(np.where(amax > 0, byte, 1), 1, 254)
    scaled = (w * np.exp2(127.0 - byte)[:, None, :]).reshape(k, n).astype(np.float32)
    by_word = np.ascontiguousarray(scaled.reshape(k // 512, 128, 4, n).transpose(0, 1, 3, 2))
    if fmt == "e4m3":
        words = by_word.astype(ml_dtypes.float8_e4m3fn).view(np.uint8)
    else:
        c = by_word.astype(ml_dtypes.float4_e2m1fn).view(np.uint8) & 0xF
        words = (c[..., 0::2] | (c[..., 1::2] << 4)).reshape(k // 512, 128, 2 * n)
    return np.ascontiguousarray(words), np.ascontiguousarray(byte.astype(np.uint8).reshape(k // 512, 16, n))


def unpack_weight(words, scales, fmt):
    g, _, n = scales.shape
    words = np.ascontiguousarray(words).reshape(g, 128, n, -1)
    if fmt == "e4m3":
        vals = words.view(ml_dtypes.float8_e4m3fn).astype(np.float64)
    else:
        nib = np.empty((g, 128, n, 4), np.uint8)
        nib[..., 0::2] = words & 0xF
        nib[..., 1::2] = words >> 4
        vals = E2M1[nib]
    vals = vals * np.repeat(np.exp2(scales.astype(np.float64) - 127.0), 8, axis=1)[..., None]
    return vals.transpose(0, 1, 3, 2).reshape(g * 512, n)


def gelu(v):
    return 0.5 * v * (1.0 + np.tanh(np.sqrt(2.0 / np.pi) * (v + 0.044715 * v**3)))


def striped8(idx):
    return np.concatenate([v.reshape(-1, 16).T for v in idx]).astype(np.uint16)


def unstriped8(offs):
    return np.stack([offs[16 * g:16 * g + 16].T.reshape(-1) for g in range(8)]).astype(np.int64)


def runs(v, idx8):
    k = np.arange(v.shape[0])
    return v[k[:, None], idx8[k % 512 // 64]]


K, K2, H, T, S = 1024, 512, 512, 2048, 1024


def setup_inputs():
    n = np.random.standard_normal
    s = mx_kscale(K)[:, None]
    s2 = mx_kscale(K2)[:, None]
    u = mx_kscale(H)[:, None]
    tab_words, tab_scales = pack_weight(n((K, T)) * s, "e4m3")
    tab2_words, tab2_scales = pack_weight(n((K2, T)) * s2, "e4m3")
    wr_words, wr_scales = pack_weight(n((K2, H)) / np.sqrt(K2) / s2, "e4m3")
    wp_words, wp_scales = pack_weight(n((K, K)) / np.sqrt(K) / s, "e2m1")
    w = n((K, H)) / np.sqrt(K)
    return {
        "tab_words": tab_words, "tab_scales": tab_scales,
        "offs": striped8(np.stack([np.random.permutation(T)[:S] for _ in range(8)])),
        "tab2_words": tab2_words, "tab2_scales": tab2_scales,
        "offs2": striped(np.random.permutation(T)[:S]),
        "w1": (w / s).astype(np.float32),
        "wr_words": wr_words, "wr_scales": wr_scales,
        "rho": np.random.uniform(0.5, 1.5, H).astype(np.float32),
        "gain": (np.random.uniform(0.5, 2.0, H) * u[:, 0]).astype(np.float32),
        "wb": (w.T / u).astype(np.float32),
        "wp_words": wp_words, "wp_scales": wp_scales,
    }


def reference(tab_words, tab_scales, offs, tab2_words, tab2_scales, offs2, w1,
              wr_words, wr_scales, rho, gain, wb, wp_words, wp_scales):
    v = runs(unpack_weight(tab_words, tab_scales, "e4m3"), unstriped8(offs))
    v2 = unpack_weight(tab2_words, tab2_scales, "e4m3")[:, unstriped(offs2)]
    wr = unpack_weight(wr_words, wr_scales, "e4m3")
    wp = unpack_weight(wp_words, wp_scales, "e2m1")
    a = mxq(f64(w1), 0, "e4m3").T @ v
    b = wr.T @ v2
    d = a - f64(rho)[:, None] * b
    z = np.tanh(d) * f64(gain)[:, None]
    x = wp.T @ v
    e = mxq(f64(wb), 0, "e4m3").T @ mxq(z, 0, "e4m3")
    return x - e

@@ -1,0 +1,299 @@
+from contextlib import ExitStack
+
+import concourse.mybir as mybir
+
+K, K2, H, T, S = 1024, 512, 512, 2048, 1024
+FLOPS = 2 * S * (K * H + K2 * H + K * K + H * K)
+
+F32 = mybir.dt.float32
+BF16 = mybir.dt.bfloat16
+I32 = mybir.dt.int32
+U32 = mybir.dt.uint32
+U16 = mybir.dt.uint16
+U8 = mybir.dt.uint8
+FP8X4 = mybir.dt.float8_e4m3fn_x4
+FP4X4 = mybir.dt.float4_e2m1fn_x4
+ACT = mybir.ActivationFunctionType
+ALU = mybir.AluOpType
+
+P = 128
+PACK = 4
+HALF = 512
+CHUNK = 256
+PER_COL = 16
+
+
+def tile_list_wafer_drift_correction_kernel(
+    tc, tab_words, tab_scales, offs, tab2_words, tab2_scales, offs2, w1,
+    wr_words, wr_scales, rho, gain, wb, wp_words, wp_scales, out,
+):
+    nc = tc.nc
+    with ExitStack() as ctx:
+        keep = ctx.enter_context(tc.tile_pool(name="keep", bufs=1))
+        ring = ctx.enter_context(tc.tile_pool(name="ring", bufs=2))
+        psum = ctx.enter_context(tc.psum_pool(name="psum", bufs=1))
+
+        def held(name, shape, dtype):
+            return keep.tile(shape, dtype, name=name, align_bytes=64)
+
+        def bank(index, shape, name):
+            return psum.tile(shape, F32, name=name, tag="bank%d" % index)
+
+        def as_words(packed):
+            return packed.rearrange("p c i -> p (c i)").bitcast(I32)
+
+        def load_plane(queue, plane, rows):
+            for r in range(PACK):
+                queue.dma_start(out=plane[:].bitcast(I32)[r:P:32], in_=rows[r].bitcast(I32))
+
+        def load_quadrant(plane, rows, d):
+            four = rows[4 * d:4 * d + 4, :].bitcast(I32)
+            nc.sync.dma_start(
+                out=plane[:].bitcast(I32)[32 * d:32 * d + 32, :],
+                in_=four.unsqueeze(0).to_broadcast([8, 4, four.shape[1]]),
+            )
+
+        def gather(dst, window, lists, first, count):
+            cols = slice(first // PER_COL, (first + count) // PER_COL)
+            nc.vector.tensor_copy(dst, window[:].indirect(lists[:, cols]))
+
+        lists = keep.tile([P, S // PER_COL], U16, name="lists")
+        lists2 = keep.tile([P, S // PER_COL], U16, name="lists2")
+        sc_win = held("sc_win", [P, T], U8)
+        sc2_win = held("sc2_win", [P, T], U8)
+        wr_sc_raw = held("wr_sc_raw", [P, H], U8)
+        wp_sc = held("wp_sc", [P, 2, K], U8)
+        v_sc = [held("v_sc%d" % a, [P, S], U8) for a in range(2)]
+        warm = held("warm", [P, 2], F32)
+
+        nc.gpsimd.memset(wp_sc[:].bitcast(I32), 0)
+        load_plane(nc.gpsimd, wp_sc, wp_scales.rearrange("a (d r) c -> r d a c", r=PACK))
+        nc.vector.memset(warm[:, 0:1], 0.0)
+        nc.vector.memset(v_sc[0][:].bitcast(I32), 0)
+        nc.vector.memset(v_sc[1][:].bitcast(I32), 0)
+        nc.scalar.activation(warm[:, 1:2], warm[:, 0:1], ACT.Tanh)
+
+        nc.sync.dma_start(lists[:], offs)
+        for a in range(2):
+            nc.sync.dma_start(
+                out=sc_win[:].bitcast(I32)[a:P:2],
+                in_=tab_scales[a].bitcast(I32).unsqueeze(1).to_broadcast([16, 4, T // 4]),
+            )
+        rho_t = held("rho_t", [P, PACK], F32)
+        gain_t = held("gain_t", [P, PACK], F32)
+
+        w1_raw = [held("w1_raw%d" % a, [P, PACK, H], F32) for a in range(2)]
+        tab = [held("tab%d" % a, [P, T], U32) for a in range(2)]
+        tab2 = held("tab2", [P, T], U32)
+        wr_raw = held("wr_raw", [P, H], U32)
+        wp = [held("wp%d" % a, [P, 2 * K], U8) for a in range(2)]
+        wb_raw = [held("wb_raw%d" % h, [P, PACK, HALF], F32) for h in range(2)]
+
+        def load_w1(a):
+            rows = w1[a * 512:(a + 1) * 512, :]
+            nc.sync.dma_start(out=w1_raw[a][:], in_=rows.rearrange("(p j) r -> p j r", j=PACK))
+
+        def load_tab(a):
+            nc.sync.dma_start(out=tab[a][:].bitcast(I32), in_=as_words(tab_words[a]))
+
+        nc.sync.dma_start(out=tab2[:].bitcast(I32), in_=as_words(tab2_words[0]))
+        nc.sync.dma_start(lists2[:], offs2)
+        for d in range(4):
+            load_quadrant(sc2_win, tab2_scales[0], d)
+        nc.sync.dma_start(out=wr_raw[:].bitcast(I32), in_=as_words(wr_words[0]))
+        load_w1(0)
+        for d in range(4):
+            load_quadrant(wr_sc_raw, wr_scales[0], d)
+        nc.sync.dma_start(out=rho_t[:], in_=rho.rearrange("(p t) -> p t", t=PACK))
+        load_w1(1)
+        load_tab(0)
+        load_tab(1)
+        nc.sync.dma_start(out=gain_t[:], in_=gain.rearrange("(p t) -> p t", t=PACK))
+        for a in range(2):
+            nc.sync.dma_start(out=wp[a][:].bitcast(I32), in_=wp_words[a].bitcast(I32))
+        for h in range(2):
+            cols = wb[:, h * HALF:(h + 1) * HALF]
+            nc.sync.dma_start(out=wb_raw[h][:], in_=cols.rearrange("(p j) n -> p j n", j=PACK))
+
+        sc_picked = held("sc_picked", [P, S], U8)
+        gather(sc_picked[:], sc_win, lists, 0, S)
+        for a in range(2):
+            for r in range(PACK):
+                nc.gpsimd.dma_start(
+                    out=v_sc[a][:].bitcast(I32)[r:P:32],
+                    in_=sc_picked[:].bitcast(I32)[8 * r + a:P:32],
+                )
+        v2_sc = held("v2_sc", [P, S], U8)
+
+        w1_bf = [held("w1_bf%d" % a, [P, PACK * H], BF16) for a in range(2)]
+        w1_q = [held("w1_q%d" % a, [P, H], U32) for a in range(2)]
+        w1_sc = [held("w1_sc%d" % a, [P, H], U8) for a in range(2)]
+
+        def round_w1(a):
+            nc.scalar.copy(
+                w1_bf[a][:].rearrange("p (t m j) -> p m j t", t=PACK, j=PACK),
+                w1_raw[a][:].rearrange("p j (m t) -> p m j t", t=PACK),
+            )
+
+        def quantize_w1(a):
+            nc.vector.quantize_mx(out=w1_q[a][:].bitcast(FP8X4), scales=w1_sc[a][:], in_=w1_bf[a][:])
+
+        round_w1(0)
+        v2 = [held("v2_%d" % h, [P, HALF], U32) for h in range(2)]
+        gather(v2[0][:], tab2, lists2, 0, HALF)
+        gather(v2_sc[:], sc2_win, lists2, 0, S)
+        wr_q = held("wr_q", [P, H], U32)
+        wr_sc = held("wr_sc", [P, H], U8)
+        nc.vector.tensor_copy(
+            wr_q[:].bitcast(I32).rearrange("p (t m) -> p t m", t=PACK),
+            wr_raw[:].bitcast(I32).rearrange("p (m t) -> p t m", t=PACK),
+        )
+        nc.vector.tensor_copy(
+            wr_sc[:].rearrange("p (t m) -> p t m", t=PACK),
+            wr_sc_raw[:].rearrange("p (m t) -> p t m", t=PACK),
+        )
+        gather(v2[1][:], tab2, lists2, HALF, HALF)
+
+        rho_b = [held("rho_b%d" % h, [P, 2, PACK, CHUNK], F32) for h in range(2)]
+
+        def reference_product(h):
+            for t in range(PACK):
+                b_ps = bank(4 * h + t, [P, HALF], "b_ps")
+                rows = slice(t * P, (t + 1) * P)
+                nc.tensor.matmul_mx(
+                    out=b_ps[:], lhsT=wr_q[:, rows].bitcast(FP8X4), lhsT_scale=wr_sc[:, rows],
+                    rhs=v2[h][:].bitcast(FP8X4), rhs_scale=v2_sc[:, h * HALF:(h + 1) * HALF],
+                    start=True, stop=True,
+                )
+                nc.scalar.activation(
+                    rho_b[h][:, :, t, :], b_ps[:].rearrange("p (c j) -> p c j", c=2),
+                    ACT.Copy, scale=rho_t[:, t:t + 1],
+                )
+
+        reference_product(0)
+        quantize_w1(0)
+        round_w1(1)
+        v = [[held("v%d_%d" % (a, h), [P, HALF], U32) for h in range(2)] for a in range(2)]
+        gather(v[0][0][:], tab[0], lists, 0, HALF)
+        quantize_w1(1)
+        reference_product(1)
+        gather(v[0][1][:], tab[0], lists, HALF, HALF)
+
+        z_q = [held("z_q%d" % c, [P, CHUNK], U32) for c in range(4)]
+        z_sc = [held("z_sc%d" % c, [P, CHUNK], U8) for c in range(4)]
+        z_bf = {}
+        bounded = {}
+
+        def gather_second_pass(c):
+            h, inner = divmod(c, 2)
+            gather(v[1][h][:, inner * CHUNK:(inner + 1) * CHUNK], tab[1], lists, c * CHUNK, CHUNK)
+
+        def residual(c):
+            h, inner = divmod(c, 2)
+            cols = slice(inner * CHUNK, (inner + 1) * CHUNK)
+            resid = ring.tile([P, PACK, CHUNK], F32, name="resid")
+            for pair in range(2):
+                a_ps = bank(2 * inner + pair, [P, 2, CHUNK], "a_ps")
+                for a in range(2):
+                    for u in range(2):
+                        rows = slice((2 * pair + u) * P, (2 * pair + u + 1) * P)
+                        nc.tensor.matmul_mx(
+                            out=a_ps[:, u, :], lhsT=w1_q[a][:, rows].bitcast(FP8X4), lhsT_scale=w1_sc[a][:, rows],
+                            rhs=v[a][h][:, cols].bitcast(FP8X4), rhs_scale=v_sc[a][:, c * CHUNK:(c + 1) * CHUNK],
+                            start=(a == 0 and u == 0), stop=(a == 1 and u == 1),
+                        )
+                nc.vector.tensor_tensor(
+                    resid[:, 2 * pair:2 * pair + 2, :], rho_b[h][:, inner, 2 * pair:2 * pair + 2, :], a_ps[:],
+                    ALU.subtract,
+                )
+            bounded[c] = ring.tile([P, CHUNK, PACK], F32, name="bounded")
+            nc.scalar.activation(
+                bounded[c][:].rearrange("p (g i) t -> p g t i", i=4),
+                resid[:].rearrange("p t (g i) -> p g t i", i=4),
+                ACT.Tanh,
+            )
+
+        def weigh(c):
+            z_bf[c] = ring.tile([P, CHUNK, PACK], BF16, name="z_bf", align_bytes=64)
+            nc.vector.tensor_tensor(
+                z_bf[c][:], bounded[c][:], gain_t[:].unsqueeze(1).to_broadcast([P, CHUNK, PACK]), ALU.mult,
+            )
+
+        def quantize_z(c):
+            nc.vector.quantize_mx(
+                out=z_q[c][:].bitcast(FP8X4), scales=z_sc[c][:], in_=z_bf[c][:].rearrange("p j t -> p (j t)"),
+            )
+
+        wb_bf = [held("wb_bf%d" % g, [P, CHUNK, PACK], BF16) for g in range(4)]
+        wb_q = [held("wb_q%d" % g, [P, CHUNK], U32) for g in range(4)]
+        wb_sc = [held("wb_sc%d" % g, [P, CHUNK], U8) for g in range(4)]
+
+        def round_wb(g):
+            cols = slice((g % 2) * CHUNK, (g % 2 + 1) * CHUNK)
+            nc.scalar.copy(
+                wb_bf[g][:].rearrange("p (g i) j -> p g j i", i=4),
+                wb_raw[g // 2][:, :, cols].rearrange("p j (g i) -> p g j i", i=4),
+            )
+
+        def quantize_wb(g):
+            nc.vector.quantize_mx(
+                out=wb_q[g][:].bitcast(FP8X4), scales=wb_sc[g][:], in_=wb_bf[g][:].rearrange("p n j -> p (n j)"),
+            )
+
+        def output_tile(h, n, index, on_vector):
+            o_ps = bank(index, [P, HALF], "o_ps")
+            for a in range(2):
+                nc.tensor.matmul_mx(
+                    out=o_ps[:], lhsT=wp[a][:, 2 * n * P:2 * (n + 1) * P].bitcast(FP4X4),
+                    lhsT_scale=wp_sc[:, a, n * P:(n + 1) * P],
+                    rhs=v[a][h][:].bitcast(FP8X4), rhs_scale=v_sc[a][:, h * HALF:(h + 1) * HALF],
+                    start=(a == 0), stop=False,
+                )
+            part, rows = n // 2, slice((n % 2) * P, (n % 2 + 1) * P)
+            for inner in range(2):
+                c = 2 * h + inner
+                nc.tensor.matmul_mx(
+                    out=o_ps[:, inner * CHUNK:(inner + 1) * CHUNK],
+                    lhsT=wb_q[part][:, rows].bitcast(FP8X4), lhsT_scale=wb_sc[part][:, rows],
+                    rhs=z_q[c][:].bitcast(FP8X4), rhs_scale=z_sc[c][:],
+                    start=False, stop=(inner == 1),
+                )
+            result = held("result%d_%d" % (h, n), [P, HALF], F32)
+            if on_vector:
+                nc.vector.tensor_copy(result[:], o_ps[:])
+            else:
+                nc.scalar.copy(result[:], o_ps[:])
+            nc.sync.dma_start(out=out[n * P:(n + 1) * P, h * HALF:(h + 1) * HALF], in_=result[:])
+
+        gather_second_pass(0)
+        gather_second_pass(1)
+        residual(0)
+        round_wb(0)
+        gather_second_pass(2)
+        residual(1)
+        round_wb(1)
+        weigh(0)
+        gather_second_pass(3)
+        quantize_z(0)
+        weigh(1)
+        quantize_wb(0)
+        quantize_z(1)
+        round_wb(2)
+        quantize_wb(1)
+        residual(2)
+        for n in range(2):
+            output_tile(0, n, 4 + n, False)
+        round_wb(3)
+        residual(3)
+        quantize_wb(2)
+        for n in range(2, 4):
+            output_tile(0, n, 4 + n, False)
+        weigh(2)
+        quantize_wb(3)
+        quantize_z(2)
+        weigh(3)
+        for n in range(4, 8):
+            output_tile(0, n, n, False)
+        quantize_z(3)
+        for n in range(8):
+            output_tile(1, n, n, n % 2 == 0)

@@ -33,8 +33,8 @@ def tile_list_wafer_drift_correction_kernel(
         ring = ctx.enter_context(tc.tile_pool(name="ring", bufs=2))
         psum = ctx.enter_context(tc.psum_pool(name="psum", bufs=1))
 
-        def held(name, shape, dtype):
-            return keep.tile(shape, dtype, name=name, align_bytes=64)
+        def held(name, shape, dtype, tag=None):
+            return keep.tile(shape, dtype, name=name, tag=tag or name, align_bytes=64)
 
         def bank(index, shape, name):
             return psum.tile(shape, F32, name=name, tag="bank%d" % index)
@@ -42,16 +42,9 @@ def tile_list_wafer_drift_correction_kernel(
         def as_words(packed):
             return packed.rearrange("p c i -> p (c i)").bitcast(I32)
 
-        def load_plane(queue, plane, rows):
-            for r in range(PACK):
-                queue.dma_start(out=plane[:].bitcast(I32)[r:P:32], in_=rows[r].bitcast(I32))
-
-        def load_quadrant(plane, rows, d):
-            four = rows[4 * d:4 * d + 4, :].bitcast(I32)
-            nc.sync.dma_start(
-                out=plane[:].bitcast(I32)[32 * d:32 * d + 32, :],
-                in_=four.unsqueeze(0).to_broadcast([8, 4, four.shape[1]]),
-            )
+        def load_plane(plane, rows, which=range(PACK)):
+            for r in which:
+                nc.sync.dma_start(out=plane[:].bitcast(I32)[r:P:32], in_=rows[r].bitcast(I32))
 
         def gather(dst, window, lists, first, count):
             cols = slice(first // PER_COL, (first + count) // PER_COL)
@@ -66,19 +59,21 @@ def tile_list_wafer_drift_correction_kernel(
         v_sc = [held("v_sc%d" % a, [P, S], U8) for a in range(2)]
         warm = held("warm", [P, 2], F32)
 
-        nc.gpsimd.memset(wp_sc[:].bitcast(I32), 0)
-        load_plane(nc.gpsimd, wp_sc, wp_scales.rearrange("a (d r) c -> r d a c", r=PACK))
+        nc.gpsimd.memset(sc_win[:].bitcast(I32), 0)
+        nc.vector.memset(sc2_win[:].bitcast(I32), 0)
         nc.vector.memset(warm[:, 0:1], 0.0)
+        nc.vector.memset(wr_sc_raw[:].bitcast(I32), 0)
+        nc.vector.memset(wp_sc[:].bitcast(I32), 0)
         nc.vector.memset(v_sc[0][:].bitcast(I32), 0)
         nc.vector.memset(v_sc[1][:].bitcast(I32), 0)
         nc.scalar.activation(warm[:, 1:2], warm[:, 0:1], ACT.Tanh)
 
         nc.sync.dma_start(lists[:], offs)
-        for a in range(2):
-            nc.sync.dma_start(
-                out=sc_win[:].bitcast(I32)[a:P:2],
-                in_=tab_scales[a].bitcast(I32).unsqueeze(1).to_broadcast([16, 4, T // 4]),
-            )
+        nc.sync.dma_start(lists2[:], offs2)
+        nc.sync.dma_start(
+            out=sc_win[:].bitcast(I32)[0:P:4, :],
+            in_=tab_scales.rearrange("a q t -> q a t").bitcast(I32),
+        )
         rho_t = held("rho_t", [P, PACK], F32)
         gain_t = held("gain_t", [P, PACK], F32)
 
@@ -86,8 +81,6 @@ def tile_list_wafer_drift_correction_kernel(
         tab = [held("tab%d" % a, [P, T], U32) for a in range(2)]
         tab2 = held("tab2", [P, T], U32)
         wr_raw = held("wr_raw", [P, H], U32)
-        wp = [held("wp%d" % a, [P, 2 * K], U8) for a in range(2)]
-        wb_raw = [held("wb_raw%d" % h, [P, PACK, HALF], F32) for h in range(2)]
 
         def load_w1(a):
             rows = w1[a * 512:(a + 1) * 512, :]
@@ -97,32 +90,39 @@ def tile_list_wafer_drift_correction_kernel(
             nc.sync.dma_start(out=tab[a][:].bitcast(I32), in_=as_words(tab_words[a]))
 
         nc.sync.dma_start(out=tab2[:].bitcast(I32), in_=as_words(tab2_words[0]))
-        nc.sync.dma_start(lists2[:], offs2)
-        for d in range(4):
-            load_quadrant(sc2_win, tab2_scales[0], d)
-        nc.sync.dma_start(out=wr_raw[:].bitcast(I32), in_=as_words(wr_words[0]))
+        load_plane(sc2_win, tab2_scales[0].rearrange("(d r) t -> r d t", r=PACK))
         load_w1(0)
-        for d in range(4):
-            load_quadrant(wr_sc_raw, wr_scales[0], d)
+        nc.sync.dma_start(out=wr_raw[:].bitcast(I32), in_=as_words(wr_words[0]))
+        load_plane(wr_sc_raw, wr_scales[0].rearrange("(d r) c -> r d c", r=PACK))
         nc.sync.dma_start(out=rho_t[:], in_=rho.rearrange("(p t) -> p t", t=PACK))
         load_w1(1)
+        load_plane(wp_sc, wp_scales.rearrange("a (d r) c -> r d a c", r=PACK))
         load_tab(0)
-        load_tab(1)
         nc.sync.dma_start(out=gain_t[:], in_=gain.rearrange("(p t) -> p t", t=PACK))
-        for a in range(2):
-            nc.sync.dma_start(out=wp[a][:].bitcast(I32), in_=wp_words[a].bitcast(I32))
-        for h in range(2):
-            cols = wb[:, h * HALF:(h + 1) * HALF]
-            nc.sync.dma_start(out=wb_raw[h][:], in_=cols.rearrange("(p j) n -> p j n", j=PACK))
 
         sc_picked = held("sc_picked", [P, S], U8)
         gather(sc_picked[:], sc_win, lists, 0, S)
-        for a in range(2):
+
+        def place_scales(a):
             for r in range(PACK):
-                nc.gpsimd.dma_start(
+                nc.sync.dma_start(
                     out=v_sc[a][:].bitcast(I32)[r:P:32],
-                    in_=sc_picked[:].bitcast(I32)[8 * r + a:P:32],
+                    in_=sc_picked[:].bitcast(I32)[8 * r + 4 * a:P:32],
                 )
+
+        wp = held("wp", [P, 2, 2 * K], U8)
+        wb_raw = [held("wb_raw%d" % h, [P, PACK, HALF], F32) for h in range(2)]
+
+        def load_wb(h):
+            cols = wb[:, h * HALF:(h + 1) * HALF]
+            nc.sync.dma_start(out=wb_raw[h][:], in_=cols.rearrange("(p j) n -> p j n", j=PACK))
+
+        place_scales(0)
+        load_tab(1)
+        place_scales(1)
+        nc.sync.dma_start(out=wp[:].bitcast(I32), in_=wp_words.rearrange("a p c -> p a c").bitcast(I32))
+        load_wb(0)
+        load_wb(1)
         v2_sc = held("v2_sc", [P, S], U8)
 
         w1_bf = [held("w1_bf%d" % a, [P, PACK * H], BF16) for a in range(2)]
@@ -141,6 +141,7 @@ def tile_list_wafer_drift_correction_kernel(
         round_w1(0)
         v2 = [held("v2_%d" % h, [P, HALF], U32) for h in range(2)]
         gather(v2[0][:], tab2, lists2, 0, HALF)
+        gather(v2[1][:], tab2, lists2, HALF, HALF)
         gather(v2_sc[:], sc2_win, lists2, 0, S)
         wr_q = held("wr_q", [P, H], U32)
         wr_sc = held("wr_sc", [P, H], U8)
@@ -152,11 +153,11 @@ def tile_list_wafer_drift_correction_kernel(
             wr_sc[:].rearrange("p (t m) -> p t m", t=PACK),
             wr_sc_raw[:].rearrange("p (m t) -> p t m", t=PACK),
         )
-        gather(v2[1][:], tab2, lists2, HALF, HALF)
 
-        rho_b = [held("rho_b%d" % h, [P, 2, PACK, CHUNK], F32) for h in range(2)]
+        rho_b = []
 
         def reference_product(h):
+            rho_b.append(held("rho_b%d" % h, [P, 2, PACK, CHUNK], F32, tag=("w1_raw1", "w1_bf1")[h]))
             for t in range(PACK):
                 b_ps = bank(4 * h + t, [P, HALF], "b_ps")
                 rows = slice(t * P, (t + 1) * P)
@@ -170,14 +171,14 @@ def tile_list_wafer_drift_correction_kernel(
                     ACT.Copy, scale=rho_t[:, t:t + 1],
                 )
 
+        v = [[held("v0_%d" % h, [P, HALF], U32) for h in range(2)], [held("v1_0", [P, HALF], U32)]]
+        round_w1(1)
         reference_product(0)
         quantize_w1(0)
-        round_w1(1)
-        v = [[held("v%d_%d" % (a, h), [P, HALF], U32) for h in range(2)] for a in range(2)]
-        gather(v[0][0][:], tab[0], lists, 0, HALF)
         quantize_w1(1)
-        reference_product(1)
+        gather(v[0][0][:], tab[0], lists, 0, HALF)
         gather(v[0][1][:], tab[0], lists, HALF, HALF)
+        reference_product(1)
 
         z_q = [held("z_q%d" % c, [P, CHUNK], U32) for c in range(4)]
         z_sc = [held("z_sc%d" % c, [P, CHUNK], U8) for c in range(4)]
@@ -187,6 +188,10 @@ def tile_list_wafer_drift_correction_kernel(
         def gather_second_pass(c):
             h, inner = divmod(c, 2)
             gather(v[1][h][:, inner * CHUNK:(inner + 1) * CHUNK], tab[1], lists, c * CHUNK, CHUNK)
+
+        def gather_late_half():
+            v[1].append(held("v1_1", [P, HALF], U32, tag="w1_raw1"))
+            gather(v[1][1][:], tab[1], lists, HALF, HALF)
 
         def residual(c):
             h, inner = divmod(c, 2)
@@ -228,9 +233,9 @@ def tile_list_wafer_drift_correction_kernel(
         wb_q = [held("wb_q%d" % g, [P, CHUNK], U32) for g in range(4)]
         wb_sc = [held("wb_sc%d" % g, [P, CHUNK], U8) for g in range(4)]
 
-        def round_wb(g):
+        def round_wb(g, on_vector=False):
             cols = slice((g % 2) * CHUNK, (g % 2 + 1) * CHUNK)
-            nc.scalar.copy(
+            (nc.vector.tensor_copy if on_vector else nc.scalar.copy)(
                 wb_bf[g][:].rearrange("p (g i) j -> p g j i", i=4),
                 wb_raw[g // 2][:, :, cols].rearrange("p j (g i) -> p g j i", i=4),
             )
@@ -244,7 +249,7 @@ def tile_list_wafer_drift_correction_kernel(
             o_ps = bank(index, [P, HALF], "o_ps")
             for a in range(2):
                 nc.tensor.matmul_mx(
-                    out=o_ps[:], lhsT=wp[a][:, 2 * n * P:2 * (n + 1) * P].bitcast(FP4X4),
+                    out=o_ps[:], lhsT=wp[:, a, 2 * n * P:2 * (n + 1) * P].bitcast(FP4X4),
                     lhsT_scale=wp_sc[:, a, n * P:(n + 1) * P],
                     rhs=v[a][h][:].bitcast(FP8X4), rhs_scale=v_sc[a][:, h * HALF:(h + 1) * HALF],
                     start=(a == 0), stop=False,
@@ -265,35 +270,71 @@ def tile_list_wafer_drift_correction_kernel(
                 nc.scalar.copy(result[:], o_ps[:])
             nc.sync.dma_start(out=out[n * P:(n + 1) * P, h * HALF:(h + 1) * HALF], in_=result[:])
 
+        def output_pair(c, pair, index, on_vector):
+            h, inner = divmod(c, 2)
+            o_ps = bank(index, [P, 2, CHUNK], "o_ps")
+            for u in range(2):
+                n = 2 * pair + u
+                for a in range(2):
+                    for s in range(CHUNK // P):
+                        first = inner * CHUNK + s * P
+                        nc.tensor.matmul_mx(
+                            out=o_ps[:, u, s * P:(s + 1) * P], lhsT=wp[:, a, 2 * n * P:2 * (n + 1) * P].bitcast(FP4X4),
+                            lhsT_scale=wp_sc[:, a, n * P:(n + 1) * P],
+                            rhs=v[a][h][:, first:first + P].bitcast(FP8X4),
+                            rhs_scale=v_sc[a][:, c * CHUNK + s * P:c * CHUNK + (s + 1) * P],
+                            start=(u == 0 and a == 0 and s == 0), stop=False,
+                        )
+            for u in range(2):
+                rows = slice(u * P, (u + 1) * P)
+                nc.tensor.matmul_mx(
+                    out=o_ps[:, u, :], lhsT=wb_q[pair][:, rows].bitcast(FP8X4), lhsT_scale=wb_sc[pair][:, rows],
+                    rhs=z_q[c][:].bitcast(FP8X4), rhs_scale=z_sc[c][:], start=False, stop=(u == 1),
+                )
+            result = held("result_c%d_%d" % (c, pair), [P, 2, CHUNK], F32)
+            if on_vector:
+                nc.vector.tensor_copy(result[:], o_ps[:])
+            else:
+                nc.scalar.copy(result[:], o_ps[:])
+            rows = out[2 * pair * P:2 * (pair + 1) * P, c * CHUNK:(c + 1) * CHUNK]
+            nc.sync.dma_start(out=rows.rearrange("(u p) j -> p u j", u=2), in_=result[:])
+
         gather_second_pass(0)
         gather_second_pass(1)
         residual(0)
-        round_wb(0)
-        gather_second_pass(2)
         residual(1)
-        round_wb(1)
+        round_wb(0, False)
+        gather_late_half()
         weigh(0)
-        gather_second_pass(3)
+        round_wb(1, False)
         quantize_z(0)
         weigh(1)
         quantize_wb(0)
         quantize_z(1)
-        round_wb(2)
         quantize_wb(1)
         residual(2)
-        for n in range(2):
-            output_tile(0, n, 4 + n, False)
-        round_wb(3)
         residual(3)
+        output_tile(0, 0, 4, False)
+        output_tile(0, 1, 5, False)
+        output_tile(0, 2, 6, False)
+        output_tile(0, 3, 7, False)
+        round_wb(2, False)
+        round_wb(3, True)
         quantize_wb(2)
-        for n in range(2, 4):
-            output_tile(0, n, 4 + n, False)
-        weigh(2)
         quantize_wb(3)
+        weigh(2)
+        output_tile(0, 4, 4, False)
+        output_tile(0, 5, 5, False)
+        output_tile(0, 6, 6, False)
+        output_tile(0, 7, 7, False)
         quantize_z(2)
         weigh(3)
-        for n in range(4, 8):
-            output_tile(0, n, n, False)
         quantize_z(3)
-        for n in range(8):
-            output_tile(1, n, n, n % 2 == 0)
+        output_tile(1, 0, 0, True)
+        output_tile(1, 1, 1, True)
+        output_tile(1, 2, 2, True)
+        output_tile(1, 3, 3, False)
+        output_tile(1, 4, 4, True)
+        output_tile(1, 5, 5, False)
+        output_tile(1, 6, 6, True)
+        output_tile(1, 7, 7, False)

@@ -42,9 +42,9 @@ def tile_list_wafer_drift_correction_kernel(
         def as_words(packed):
             return packed.rearrange("p c i -> p (c i)").bitcast(I32)
 
-        def load_plane(plane, rows, which=range(PACK)):
+        def load_plane(plane, rows, first=0, which=range(PACK)):
             for r in which:
-                nc.sync.dma_start(out=plane[:].bitcast(I32)[r:P:32], in_=rows[r].bitcast(I32))
+                nc.sync.dma_start(out=plane[:].bitcast(I32)[first + r:P:32], in_=rows[r].bitcast(I32))
 
         def gather(dst, window, lists, first, count):
             cols = slice(first // PER_COL, (first + count) // PER_COL)
@@ -90,58 +90,61 @@ def tile_list_wafer_drift_correction_kernel(
             nc.sync.dma_start(out=tab[a][:].bitcast(I32), in_=as_words(tab_words[a]))
 
         nc.sync.dma_start(out=tab2[:].bitcast(I32), in_=as_words(tab2_words[0]))
-        load_plane(sc2_win, tab2_scales[0].rearrange("(d r) t -> r d t", r=PACK))
-        load_w1(0)
+        load_plane(sc2_win, tab2_scales[0].rearrange("(d r) t -> r d t", r=PACK), 8)
         nc.sync.dma_start(out=wr_raw[:].bitcast(I32), in_=as_words(wr_words[0]))
-        load_plane(wr_sc_raw, wr_scales[0].rearrange("(d r) c -> r d c", r=PACK))
+        load_plane(wr_sc_raw, wr_scales[0].rearrange("(d r) c -> r d c", r=PACK), 12, range(1))
+        load_w1(0)
+        load_plane(wr_sc_raw, wr_scales[0].rearrange("(d r) c -> r d c", r=PACK), 12, range(1, 4))
         nc.sync.dma_start(out=rho_t[:], in_=rho.rearrange("(p t) -> p t", t=PACK))
-        load_w1(1)
-        load_plane(wp_sc, wp_scales.rearrange("a (d r) c -> r d a c", r=PACK))
         load_tab(0)
+        load_plane(wp_sc, wp_scales.rearrange("a (d r) c -> r d a c", r=PACK))
+        load_w1(1)
         nc.sync.dma_start(out=gain_t[:], in_=gain.rearrange("(p t) -> p t", t=PACK))
 
         sc_picked = held("sc_picked", [P, S], U8)
         gather(sc_picked[:], sc_win, lists, 0, S)
 
-        def place_scales(a):
-            for r in range(PACK):
+        def place_scales(a, rows=range(PACK)):
+            for r in rows:
                 nc.sync.dma_start(
                     out=v_sc[a][:].bitcast(I32)[r:P:32],
                     in_=sc_picked[:].bitcast(I32)[8 * r + 4 * a:P:32],
                 )
 
         wp = held("wp", [P, 2, 2 * K], U8)
-        wb_raw = [held("wb_raw%d" % h, [P, PACK, HALF], F32) for h in range(2)]
+        wb_raw = [held("wb_raw%d" % g, [P, PACK, CHUNK], F32) for g in range(4)]
 
-        def load_wb(h):
-            cols = wb[:, h * HALF:(h + 1) * HALF]
-            nc.sync.dma_start(out=wb_raw[h][:], in_=cols.rearrange("(p j) n -> p j n", j=PACK))
+        def load_wb(g):
+            cols = wb[:, g * CHUNK:(g + 1) * CHUNK]
+            nc.sync.dma_start(out=wb_raw[g][:], in_=cols.rearrange("(p j) n -> p j n", j=PACK))
 
         place_scales(0)
         load_tab(1)
         place_scales(1)
-        nc.sync.dma_start(out=wp[:].bitcast(I32), in_=wp_words.rearrange("a p c -> p a c").bitcast(I32))
         load_wb(0)
+        nc.sync.dma_start(out=wp[:].bitcast(I32), in_=wp_words.rearrange("a p c -> p a c").bitcast(I32))
         load_wb(1)
+        load_wb(2)
+        load_wb(3)
         v2_sc = held("v2_sc", [P, S], U8)
 
         w1_bf = [held("w1_bf%d" % a, [P, PACK * H], BF16) for a in range(2)]
         w1_q = [held("w1_q%d" % a, [P, H], U32) for a in range(2)]
         w1_sc = [held("w1_sc%d" % a, [P, H], U8) for a in range(2)]
 
-        def round_w1(a):
-            nc.scalar.copy(
-                w1_bf[a][:].rearrange("p (t m j) -> p m j t", t=PACK, j=PACK),
-                w1_raw[a][:].rearrange("p j (m t) -> p m j t", t=PACK),
-            )
+        def round_w1(a, on_scalar):
+            dst = w1_bf[a][:].rearrange("p (t m j) -> p m j t", t=PACK, j=PACK)
+            src = w1_raw[a][:].rearrange("p j (m t) -> p m j t", t=PACK)
+            nc.scalar.copy(dst[:, 0:on_scalar], src[:, 0:on_scalar])
+            if on_scalar < P:
+                nc.vector.tensor_copy(dst[:, on_scalar:P], src[:, on_scalar:P])
 
         def quantize_w1(a):
             nc.vector.quantize_mx(out=w1_q[a][:].bitcast(FP8X4), scales=w1_sc[a][:], in_=w1_bf[a][:])
 
-        round_w1(0)
-        v2 = [held("v2_%d" % h, [P, HALF], U32) for h in range(2)]
+        round_w1(0, P)
+        v2 = [held("v2_0", [P, HALF], U32)]
         gather(v2[0][:], tab2, lists2, 0, HALF)
-        gather(v2[1][:], tab2, lists2, HALF, HALF)
         gather(v2_sc[:], sc2_win, lists2, 0, S)
         wr_q = held("wr_q", [P, H], U32)
         wr_sc = held("wr_sc", [P, H], U8)
@@ -154,16 +157,19 @@ def tile_list_wafer_drift_correction_kernel(
             wr_sc_raw[:].rearrange("p (m t) -> p t m", t=PACK),
         )
 
+        v2.append(held("v2_1", [P, HALF], U32, tag="wr_sc_raw"))
+        gather(v2[1][:], tab2, lists2, HALF, HALF)
+
         rho_b = []
 
         def reference_product(h):
-            rho_b.append(held("rho_b%d" % h, [P, 2, PACK, CHUNK], F32, tag=("w1_raw1", "w1_bf1")[h]))
+            rho_b.append(held("rho_b%d" % h, [P, 2, PACK, CHUNK], F32, tag=("rho_b0", "w1_raw1")[h]))
             for t in range(PACK):
                 b_ps = bank(4 * h + t, [P, HALF], "b_ps")
                 rows = slice(t * P, (t + 1) * P)
                 nc.tensor.matmul_mx(
-                    out=b_ps[:], lhsT=wr_q[:, rows].bitcast(FP8X4), lhsT_scale=wr_sc[:, rows],
-                    rhs=v2[h][:].bitcast(FP8X4), rhs_scale=v2_sc[:, h * HALF:(h + 1) * HALF],
+                    out=b_ps[:], lhsT=wr_q[:, rows].bitcast(FP8X4), lhsT_scale=wr_sc[12:P, rows],
+                    rhs=v2[h][:].bitcast(FP8X4), rhs_scale=v2_sc[8:P, h * HALF:(h + 1) * HALF],
                     start=True, stop=True,
                 )
                 nc.scalar.activation(
@@ -172,12 +178,16 @@ def tile_list_wafer_drift_correction_kernel(
                 )
 
         v = [[held("v0_%d" % h, [P, HALF], U32) for h in range(2)], [held("v1_0", [P, HALF], U32)]]
-        round_w1(1)
+
+        def picked(a, first, count):
+            return v[a][first // HALF][:, first % HALF:first % HALF + count]
+
         reference_product(0)
         quantize_w1(0)
+        gather(picked(0, 0, HALF), tab[0], lists, 0, HALF)
+        gather(picked(0, HALF, HALF), tab[0], lists, HALF, HALF)
+        round_w1(1, 64)
         quantize_w1(1)
-        gather(v[0][0][:], tab[0], lists, 0, HALF)
-        gather(v[0][1][:], tab[0], lists, HALF, HALF)
         reference_product(1)
 
         z_q = [held("z_q%d" % c, [P, CHUNK], U32) for c in range(4)]
@@ -186,25 +196,23 @@ def tile_list_wafer_drift_correction_kernel(
         bounded = {}
 
         def gather_second_pass(c):
-            h, inner = divmod(c, 2)
-            gather(v[1][h][:, inner * CHUNK:(inner + 1) * CHUNK], tab[1], lists, c * CHUNK, CHUNK)
+            gather(picked(1, c * CHUNK, CHUNK), tab[1], lists, c * CHUNK, CHUNK)
 
         def gather_late_half():
-            v[1].append(held("v1_1", [P, HALF], U32, tag="w1_raw1"))
+            v[1].append(held("v1_1", [P, HALF], U32, tag="rho_b0"))
             gather(v[1][1][:], tab[1], lists, HALF, HALF)
 
-        def residual(c):
+        def residual(c, first_bank):
             h, inner = divmod(c, 2)
-            cols = slice(inner * CHUNK, (inner + 1) * CHUNK)
             resid = ring.tile([P, PACK, CHUNK], F32, name="resid")
             for pair in range(2):
-                a_ps = bank(2 * inner + pair, [P, 2, CHUNK], "a_ps")
+                a_ps = bank(first_bank + pair, [P, 2, CHUNK], "a_ps")
                 for a in range(2):
                     for u in range(2):
                         rows = slice((2 * pair + u) * P, (2 * pair + u + 1) * P)
                         nc.tensor.matmul_mx(
                             out=a_ps[:, u, :], lhsT=w1_q[a][:, rows].bitcast(FP8X4), lhsT_scale=w1_sc[a][:, rows],
-                            rhs=v[a][h][:, cols].bitcast(FP8X4), rhs_scale=v_sc[a][:, c * CHUNK:(c + 1) * CHUNK],
+                            rhs=picked(a, c * CHUNK, CHUNK).bitcast(FP8X4), rhs_scale=v_sc[a][:, c * CHUNK:(c + 1) * CHUNK],
                             start=(a == 0 and u == 0), stop=(a == 1 and u == 1),
                         )
                 nc.vector.tensor_tensor(
@@ -219,7 +227,7 @@ def tile_list_wafer_drift_correction_kernel(
             )
 
         def weigh(c):
-            z_bf[c] = ring.tile([P, CHUNK, PACK], BF16, name="z_bf", align_bytes=64)
+            z_bf[c] = held("z_bf%d" % c, [P, CHUNK, PACK], BF16)
             nc.vector.tensor_tensor(
                 z_bf[c][:], bounded[c][:], gain_t[:].unsqueeze(1).to_broadcast([P, CHUNK, PACK]), ALU.mult,
             )
@@ -234,10 +242,9 @@ def tile_list_wafer_drift_correction_kernel(
         wb_sc = [held("wb_sc%d" % g, [P, CHUNK], U8) for g in range(4)]
 
         def round_wb(g, on_vector=False):
-            cols = slice((g % 2) * CHUNK, (g % 2 + 1) * CHUNK)
             (nc.vector.tensor_copy if on_vector else nc.scalar.copy)(
                 wb_bf[g][:].rearrange("p (g i) j -> p g j i", i=4),
-                wb_raw[g // 2][:, :, cols].rearrange("p j (g i) -> p g j i", i=4),
+                wb_raw[g][:].rearrange("p j (g i) -> p g j i", i=4),
             )
 
         def quantize_wb(g):
@@ -245,43 +252,43 @@ def tile_list_wafer_drift_correction_kernel(
                 out=wb_q[g][:].bitcast(FP8X4), scales=wb_sc[g][:], in_=wb_bf[g][:].rearrange("p n j -> p (n j)"),
             )
 
-        def output_tile(h, n, index, on_vector):
+        def output_tile(c0, n, index, on_vector):
+            first = c0 * CHUNK
             o_ps = bank(index, [P, HALF], "o_ps")
             for a in range(2):
                 nc.tensor.matmul_mx(
                     out=o_ps[:], lhsT=wp[:, a, 2 * n * P:2 * (n + 1) * P].bitcast(FP4X4),
                     lhsT_scale=wp_sc[:, a, n * P:(n + 1) * P],
-                    rhs=v[a][h][:].bitcast(FP8X4), rhs_scale=v_sc[a][:, h * HALF:(h + 1) * HALF],
+                    rhs=picked(a, first, HALF).bitcast(FP8X4), rhs_scale=v_sc[a][:, first:first + HALF],
                     start=(a == 0), stop=False,
                 )
             part, rows = n // 2, slice((n % 2) * P, (n % 2 + 1) * P)
             for inner in range(2):
-                c = 2 * h + inner
+                c = c0 + inner
                 nc.tensor.matmul_mx(
                     out=o_ps[:, inner * CHUNK:(inner + 1) * CHUNK],
                     lhsT=wb_q[part][:, rows].bitcast(FP8X4), lhsT_scale=wb_sc[part][:, rows],
                     rhs=z_q[c][:].bitcast(FP8X4), rhs_scale=z_sc[c][:],
                     start=False, stop=(inner == 1),
                 )
-            result = held("result%d_%d" % (h, n), [P, HALF], F32)
+            result = held("result%d_%d" % (c0, n), [P, HALF], F32)
             if on_vector:
                 nc.vector.tensor_copy(result[:], o_ps[:])
             else:
                 nc.scalar.copy(result[:], o_ps[:])
-            nc.sync.dma_start(out=out[n * P:(n + 1) * P, h * HALF:(h + 1) * HALF], in_=result[:])
+            nc.sync.dma_start(out=out[n * P:(n + 1) * P, first:first + HALF], in_=result[:])
 
         def output_pair(c, pair, index, on_vector):
-            h, inner = divmod(c, 2)
             o_ps = bank(index, [P, 2, CHUNK], "o_ps")
             for u in range(2):
                 n = 2 * pair + u
                 for a in range(2):
                     for s in range(CHUNK // P):
-                        first = inner * CHUNK + s * P
+                        first = c * CHUNK + s * P
                         nc.tensor.matmul_mx(
                             out=o_ps[:, u, s * P:(s + 1) * P], lhsT=wp[:, a, 2 * n * P:2 * (n + 1) * P].bitcast(FP4X4),
                             lhsT_scale=wp_sc[:, a, n * P:(n + 1) * P],
-                            rhs=v[a][h][:, first:first + P].bitcast(FP8X4),
+                            rhs=picked(a, first, P).bitcast(FP8X4),
                             rhs_scale=v_sc[a][:, c * CHUNK + s * P:c * CHUNK + (s + 1) * P],
                             start=(u == 0 and a == 0 and s == 0), stop=False,
                         )
@@ -301,40 +308,40 @@ def tile_list_wafer_drift_correction_kernel(
 
         gather_second_pass(0)
         gather_second_pass(1)
-        residual(0)
-        residual(1)
         round_wb(0, False)
-        gather_late_half()
-        weigh(0)
+        residual(0, 0)
+        residual(1, 2)
+        quantize_wb(0)
         round_wb(1, False)
+        round_wb(2, False)
+        weigh(0)
         quantize_z(0)
         weigh(1)
-        quantize_wb(0)
         quantize_z(1)
         quantize_wb(1)
-        residual(2)
-        residual(3)
+        gather_late_half()
+        quantize_wb(2)
         output_tile(0, 0, 4, False)
         output_tile(0, 1, 5, False)
         output_tile(0, 2, 6, False)
         output_tile(0, 3, 7, False)
-        round_wb(2, False)
+        residual(2, 0)
         round_wb(3, True)
-        quantize_wb(2)
+        residual(3, 2)
         quantize_wb(3)
         weigh(2)
+        quantize_z(2)
+        weigh(3)
+        quantize_z(3)
         output_tile(0, 4, 4, False)
         output_tile(0, 5, 5, False)
         output_tile(0, 6, 6, False)
         output_tile(0, 7, 7, False)
-        quantize_z(2)
-        weigh(3)
-        quantize_z(3)
-        output_tile(1, 0, 0, True)
-        output_tile(1, 1, 1, True)
-        output_tile(1, 2, 2, True)
-        output_tile(1, 3, 3, False)
-        output_tile(1, 4, 4, True)
-        output_tile(1, 5, 5, False)
-        output_tile(1, 6, 6, True)
-        output_tile(1, 7, 7, False)
+        output_tile(2, 0, 0, True)
+        output_tile(2, 1, 1, False)
+        output_tile(2, 2, 2, True)
+        output_tile(2, 3, 3, False)
+        output_tile(2, 4, 4, True)
+        output_tile(2, 5, 5, False)
+        output_tile(2, 6, 6, True)
+        output_tile(2, 7, 7, False)

@@ -18,9 +18,16 @@ ALU = mybir.AluOpType
 
 P = 128
 PACK = 4
+QUADRANT = 32
+K_PASS = P * PACK
 HALF = 512
 CHUNK = 256
-PER_COL = 16
+LIST_ROWS = 16
+LINE = 4
+PASSES, HALVES, CHUNKS, PARTS, TILES = K // K_PASS, S // HALF, S // CHUNK, K // CHUNK, K // P
+V2_FIRST, WR_FIRST = 8, 12
+W1_ON_SCALAR = 64
+OUT_BANK = 4
 
 
 def tile_list_wafer_drift_correction_kernel(
@@ -39,34 +46,31 @@ def tile_list_wafer_drift_correction_kernel(
         def bank(index, shape, name):
             return psum.tile(shape, F32, name=name, tag="bank%d" % index)
 
-        def as_words(packed):
-            return packed.rearrange("p c i -> p (c i)").bitcast(I32)
+        def load_words(tile, packed):
+            nc.sync.dma_start(out=tile[:].bitcast(I32), in_=packed.rearrange("p c i -> p (c i)").bitcast(I32))
 
         def load_plane(plane, rows, first=0, which=range(PACK)):
             for r in which:
-                nc.sync.dma_start(out=plane[:].bitcast(I32)[first + r:P:32], in_=rows[r].bitcast(I32))
+                nc.sync.dma_start(out=plane[:].bitcast(I32)[first + r:P:QUADRANT], in_=rows[r].bitcast(I32))
 
-        def gather(dst, window, lists, first, count):
-            cols = slice(first // PER_COL, (first + count) // PER_COL)
-            nc.vector.tensor_copy(dst, window[:].indirect(lists[:, cols]))
+        def gather(dst, window, offsets, entry, count):
+            cols = slice(entry // LIST_ROWS, (entry + count) // LIST_ROWS)
+            nc.vector.tensor_copy(dst, window[:].indirect(offsets[:, cols]))
 
-        lists = keep.tile([P, S // PER_COL], U16, name="lists")
-        lists2 = keep.tile([P, S // PER_COL], U16, name="lists2")
+        lists = keep.tile([P, S // LIST_ROWS], U16, name="lists")
+        lists2 = keep.tile([P, S // LIST_ROWS], U16, name="lists2")
         sc_win = held("sc_win", [P, T], U8)
         sc2_win = held("sc2_win", [P, T], U8)
         wr_sc_raw = held("wr_sc_raw", [P, H], U8)
-        wp_sc = held("wp_sc", [P, 2, K], U8)
-        v_sc = [held("v_sc%d" % a, [P, S], U8) for a in range(2)]
-        warm = held("warm", [P, 2], F32)
+        wp_sc = held("wp_sc", [P, PASSES, K], U8)
+        v_sc = [held("v_sc%d" % a, [P, S], U8) for a in range(PASSES)]
 
         nc.gpsimd.memset(sc_win[:].bitcast(I32), 0)
         nc.vector.memset(sc2_win[:].bitcast(I32), 0)
-        nc.vector.memset(warm[:, 0:1], 0.0)
         nc.vector.memset(wr_sc_raw[:].bitcast(I32), 0)
         nc.vector.memset(wp_sc[:].bitcast(I32), 0)
-        nc.vector.memset(v_sc[0][:].bitcast(I32), 0)
-        nc.vector.memset(v_sc[1][:].bitcast(I32), 0)
-        nc.scalar.activation(warm[:, 1:2], warm[:, 0:1], ACT.Tanh)
+        for a in range(PASSES):
+            nc.vector.memset(v_sc[a][:].bitcast(I32), 0)
 
         nc.sync.dma_start(lists[:], offs)
         nc.sync.dma_start(lists2[:], offs2)
@@ -76,27 +80,24 @@ def tile_list_wafer_drift_correction_kernel(
         )
         rho_t = held("rho_t", [P, PACK], F32)
         gain_t = held("gain_t", [P, PACK], F32)
-
-        w1_raw = [held("w1_raw%d" % a, [P, PACK, H], F32) for a in range(2)]
-        tab = [held("tab%d" % a, [P, T], U32) for a in range(2)]
+        w1_raw = [held("w1_raw%d" % a, [P, PACK, H], F32) for a in range(PASSES)]
+        tab = [held("tab%d" % a, [P, T], U32) for a in range(PASSES)]
         tab2 = held("tab2", [P, T], U32)
         wr_raw = held("wr_raw", [P, H], U32)
 
         def load_w1(a):
-            rows = w1[a * 512:(a + 1) * 512, :]
+            rows = w1[a * K_PASS:(a + 1) * K_PASS, :]
             nc.sync.dma_start(out=w1_raw[a][:], in_=rows.rearrange("(p j) r -> p j r", j=PACK))
 
-        def load_tab(a):
-            nc.sync.dma_start(out=tab[a][:].bitcast(I32), in_=as_words(tab_words[a]))
-
-        nc.sync.dma_start(out=tab2[:].bitcast(I32), in_=as_words(tab2_words[0]))
-        load_plane(sc2_win, tab2_scales[0].rearrange("(d r) t -> r d t", r=PACK), 8)
-        nc.sync.dma_start(out=wr_raw[:].bitcast(I32), in_=as_words(wr_words[0]))
-        load_plane(wr_sc_raw, wr_scales[0].rearrange("(d r) c -> r d c", r=PACK), 12, range(1))
+        wr_rows = wr_scales[0].rearrange("(d r) c -> r d c", r=PACK)
+        load_words(tab2, tab2_words[0])
+        load_plane(sc2_win, tab2_scales[0].rearrange("(d r) t -> r d t", r=PACK), V2_FIRST)
+        load_words(wr_raw, wr_words[0])
+        load_plane(wr_sc_raw, wr_rows, WR_FIRST, range(1))
         load_w1(0)
-        load_plane(wr_sc_raw, wr_scales[0].rearrange("(d r) c -> r d c", r=PACK), 12, range(1, 4))
+        load_plane(wr_sc_raw, wr_rows, WR_FIRST, range(1, PACK))
         nc.sync.dma_start(out=rho_t[:], in_=rho.rearrange("(p t) -> p t", t=PACK))
-        load_tab(0)
+        load_words(tab[0], tab_words[0])
         load_plane(wp_sc, wp_scales.rearrange("a (d r) c -> r d a c", r=PACK))
         load_w1(1)
         nc.sync.dma_start(out=gain_t[:], in_=gain.rearrange("(p t) -> p t", t=PACK))
@@ -104,40 +105,39 @@ def tile_list_wafer_drift_correction_kernel(
         sc_picked = held("sc_picked", [P, S], U8)
         gather(sc_picked[:], sc_win, lists, 0, S)
 
-        def place_scales(a, rows=range(PACK)):
-            for r in rows:
+        def place_scales(a):
+            for r in range(PACK):
                 nc.sync.dma_start(
-                    out=v_sc[a][:].bitcast(I32)[r:P:32],
-                    in_=sc_picked[:].bitcast(I32)[8 * r + 4 * a:P:32],
+                    out=v_sc[a][:].bitcast(I32)[r:P:QUADRANT],
+                    in_=sc_picked[:].bitcast(I32)[8 * r + 4 * a:P:QUADRANT],
                 )
 
-        wp = held("wp", [P, 2, 2 * K], U8)
-        wb_raw = [held("wb_raw%d" % g, [P, PACK, CHUNK], F32) for g in range(4)]
+        wp = held("wp", [P, PASSES, 2 * K], U8)
+        wb_raw = [held("wb_raw%d" % g, [P, PACK, CHUNK], F32) for g in range(PARTS)]
 
         def load_wb(g):
             cols = wb[:, g * CHUNK:(g + 1) * CHUNK]
             nc.sync.dma_start(out=wb_raw[g][:], in_=cols.rearrange("(p j) n -> p j n", j=PACK))
 
         place_scales(0)
-        load_tab(1)
+        load_words(tab[1], tab_words[1])
         place_scales(1)
         load_wb(0)
         nc.sync.dma_start(out=wp[:].bitcast(I32), in_=wp_words.rearrange("a p c -> p a c").bitcast(I32))
-        load_wb(1)
-        load_wb(2)
-        load_wb(3)
+        for g in range(1, PARTS):
+            load_wb(g)
+
         v2_sc = held("v2_sc", [P, S], U8)
+        w1_bf = [held("w1_bf%d" % a, [P, PACK * H], BF16) for a in range(PASSES)]
+        w1_q = [held("w1_q%d" % a, [P, H], U32) for a in range(PASSES)]
+        w1_sc = [held("w1_sc%d" % a, [P, H], U8) for a in range(PASSES)]
 
-        w1_bf = [held("w1_bf%d" % a, [P, PACK * H], BF16) for a in range(2)]
-        w1_q = [held("w1_q%d" % a, [P, H], U32) for a in range(2)]
-        w1_sc = [held("w1_sc%d" % a, [P, H], U8) for a in range(2)]
-
-        def round_w1(a, on_scalar):
+        def round_w1(a, split):
             dst = w1_bf[a][:].rearrange("p (t m j) -> p m j t", t=PACK, j=PACK)
             src = w1_raw[a][:].rearrange("p j (m t) -> p m j t", t=PACK)
-            nc.scalar.copy(dst[:, 0:on_scalar], src[:, 0:on_scalar])
-            if on_scalar < P:
-                nc.vector.tensor_copy(dst[:, on_scalar:P], src[:, on_scalar:P])
+            nc.scalar.copy(dst[:, 0:split], src[:, 0:split])
+            if split < P:
+                nc.vector.tensor_copy(dst[:, split:P], src[:, split:P])
 
         def quantize_w1(a):
             nc.vector.quantize_mx(out=w1_q[a][:].bitcast(FP8X4), scales=w1_sc[a][:], in_=w1_bf[a][:])
@@ -156,20 +156,19 @@ def tile_list_wafer_drift_correction_kernel(
             wr_sc[:].rearrange("p (t m) -> p t m", t=PACK),
             wr_sc_raw[:].rearrange("p (m t) -> p t m", t=PACK),
         )
-
         v2.append(held("v2_1", [P, HALF], U32, tag="wr_sc_raw"))
         gather(v2[1][:], tab2, lists2, HALF, HALF)
 
         rho_b = []
 
-        def reference_product(h):
-            rho_b.append(held("rho_b%d" % h, [P, 2, PACK, CHUNK], F32, tag=("rho_b0", "w1_raw1")[h]))
+        def reference_product(h, tag):
+            rho_b.append(held("rho_b%d" % h, [P, 2, PACK, CHUNK], F32, tag=tag))
             for t in range(PACK):
-                b_ps = bank(4 * h + t, [P, HALF], "b_ps")
+                b_ps = bank(PACK * h + t, [P, HALF], "b_ps")
                 rows = slice(t * P, (t + 1) * P)
                 nc.tensor.matmul_mx(
-                    out=b_ps[:], lhsT=wr_q[:, rows].bitcast(FP8X4), lhsT_scale=wr_sc[12:P, rows],
-                    rhs=v2[h][:].bitcast(FP8X4), rhs_scale=v2_sc[8:P, h * HALF:(h + 1) * HALF],
+                    out=b_ps[:], lhsT=wr_q[:, rows].bitcast(FP8X4), lhsT_scale=wr_sc[WR_FIRST:P, rows],
+                    rhs=v2[h][:].bitcast(FP8X4), rhs_scale=v2_sc[V2_FIRST:P, h * HALF:(h + 1) * HALF],
                     start=True, stop=True,
                 )
                 nc.scalar.activation(
@@ -177,43 +176,37 @@ def tile_list_wafer_drift_correction_kernel(
                     ACT.Copy, scale=rho_t[:, t:t + 1],
                 )
 
-        v = [[held("v0_%d" % h, [P, HALF], U32) for h in range(2)], [held("v1_0", [P, HALF], U32)]]
+        v = [[held("v0_%d" % h, [P, HALF], U32) for h in range(HALVES)], [held("v1_0", [P, HALF], U32)]]
 
-        def picked(a, first, count):
-            return v[a][first // HALF][:, first % HALF:first % HALF + count]
+        def picked(a, entry, count):
+            return v[a][entry // HALF][:, entry % HALF:entry % HALF + count]
 
-        reference_product(0)
+        reference_product(0, "rho_b0")
         quantize_w1(0)
-        gather(picked(0, 0, HALF), tab[0], lists, 0, HALF)
-        gather(picked(0, HALF, HALF), tab[0], lists, HALF, HALF)
-        round_w1(1, 64)
+        for h in range(HALVES):
+            gather(picked(0, h * HALF, HALF), tab[0], lists, h * HALF, HALF)
+        round_w1(1, W1_ON_SCALAR)
         quantize_w1(1)
-        reference_product(1)
+        reference_product(1, "w1_raw1")
 
-        z_q = [held("z_q%d" % c, [P, CHUNK], U32) for c in range(4)]
-        z_sc = [held("z_sc%d" % c, [P, CHUNK], U8) for c in range(4)]
+        z_q = [held("z_q%d" % c, [P, CHUNK], U32) for c in range(CHUNKS)]
+        z_sc = [held("z_sc%d" % c, [P, CHUNK], U8) for c in range(CHUNKS)]
         z_bf = {}
         bounded = {}
 
-        def gather_second_pass(c):
-            gather(picked(1, c * CHUNK, CHUNK), tab[1], lists, c * CHUNK, CHUNK)
-
-        def gather_late_half():
-            v[1].append(held("v1_1", [P, HALF], U32, tag="rho_b0"))
-            gather(v[1][1][:], tab[1], lists, HALF, HALF)
-
-        def residual(c, first_bank):
+        def residual(c):
             h, inner = divmod(c, 2)
             resid = ring.tile([P, PACK, CHUNK], F32, name="resid")
             for pair in range(2):
-                a_ps = bank(first_bank + pair, [P, 2, CHUNK], "a_ps")
-                for a in range(2):
+                a_ps = bank(2 * inner + pair, [P, 2, CHUNK], "a_ps")
+                for a in range(PASSES):
                     for u in range(2):
                         rows = slice((2 * pair + u) * P, (2 * pair + u + 1) * P)
                         nc.tensor.matmul_mx(
                             out=a_ps[:, u, :], lhsT=w1_q[a][:, rows].bitcast(FP8X4), lhsT_scale=w1_sc[a][:, rows],
-                            rhs=picked(a, c * CHUNK, CHUNK).bitcast(FP8X4), rhs_scale=v_sc[a][:, c * CHUNK:(c + 1) * CHUNK],
-                            start=(a == 0 and u == 0), stop=(a == 1 and u == 1),
+                            rhs=picked(a, c * CHUNK, CHUNK).bitcast(FP8X4),
+                            rhs_scale=v_sc[a][:, c * CHUNK:(c + 1) * CHUNK],
+                            start=(a == 0 and u == 0), stop=(a == PASSES - 1 and u == 1),
                         )
                 nc.vector.tensor_tensor(
                     resid[:, 2 * pair:2 * pair + 2, :], rho_b[h][:, inner, 2 * pair:2 * pair + 2, :], a_ps[:],
@@ -221,30 +214,28 @@ def tile_list_wafer_drift_correction_kernel(
                 )
             bounded[c] = ring.tile([P, CHUNK, PACK], F32, name="bounded")
             nc.scalar.activation(
-                bounded[c][:].rearrange("p (g i) t -> p g t i", i=4),
-                resid[:].rearrange("p t (g i) -> p g t i", i=4),
+                bounded[c][:].rearrange("p (g i) t -> p g t i", i=LINE),
+                resid[:].rearrange("p t (g i) -> p g t i", i=LINE),
                 ACT.Tanh,
             )
 
-        def weigh(c):
+        def make_z(c):
             z_bf[c] = held("z_bf%d" % c, [P, CHUNK, PACK], BF16)
             nc.vector.tensor_tensor(
                 z_bf[c][:], bounded[c][:], gain_t[:].unsqueeze(1).to_broadcast([P, CHUNK, PACK]), ALU.mult,
             )
-
-        def quantize_z(c):
             nc.vector.quantize_mx(
                 out=z_q[c][:].bitcast(FP8X4), scales=z_sc[c][:], in_=z_bf[c][:].rearrange("p j t -> p (j t)"),
             )
 
-        wb_bf = [held("wb_bf%d" % g, [P, CHUNK, PACK], BF16) for g in range(4)]
-        wb_q = [held("wb_q%d" % g, [P, CHUNK], U32) for g in range(4)]
-        wb_sc = [held("wb_sc%d" % g, [P, CHUNK], U8) for g in range(4)]
+        wb_bf = [held("wb_bf%d" % g, [P, CHUNK, PACK], BF16) for g in range(PARTS)]
+        wb_q = [held("wb_q%d" % g, [P, CHUNK], U32) for g in range(PARTS)]
+        wb_sc = [held("wb_sc%d" % g, [P, CHUNK], U8) for g in range(PARTS)]
 
-        def round_wb(g, on_vector=False):
-            (nc.vector.tensor_copy if on_vector else nc.scalar.copy)(
-                wb_bf[g][:].rearrange("p (g i) j -> p g j i", i=4),
-                wb_raw[g][:].rearrange("p j (g i) -> p g j i", i=4),
+        def round_wb(g, copy):
+            copy(
+                wb_bf[g][:].rearrange("p (g i) j -> p g j i", i=LINE),
+                wb_raw[g][:].rearrange("p j (g i) -> p g j i", i=LINE),
             )
 
         def quantize_wb(g):
@@ -252,96 +243,55 @@ def tile_list_wafer_drift_correction_kernel(
                 out=wb_q[g][:].bitcast(FP8X4), scales=wb_sc[g][:], in_=wb_bf[g][:].rearrange("p n j -> p (n j)"),
             )
 
-        def output_tile(c0, n, index, on_vector):
-            first = c0 * CHUNK
+        def output_tile(h, n, index, copy):
+            cols = slice(h * HALF, (h + 1) * HALF)
             o_ps = bank(index, [P, HALF], "o_ps")
-            for a in range(2):
+            for a in range(PASSES):
                 nc.tensor.matmul_mx(
                     out=o_ps[:], lhsT=wp[:, a, 2 * n * P:2 * (n + 1) * P].bitcast(FP4X4),
                     lhsT_scale=wp_sc[:, a, n * P:(n + 1) * P],
-                    rhs=picked(a, first, HALF).bitcast(FP8X4), rhs_scale=v_sc[a][:, first:first + HALF],
+                    rhs=picked(a, h * HALF, HALF).bitcast(FP8X4), rhs_scale=v_sc[a][:, cols],
                     start=(a == 0), stop=False,
                 )
-            part, rows = n // 2, slice((n % 2) * P, (n % 2 + 1) * P)
+            g, rows = n // 2, slice((n % 2) * P, (n % 2 + 1) * P)
             for inner in range(2):
-                c = c0 + inner
+                c = 2 * h + inner
                 nc.tensor.matmul_mx(
                     out=o_ps[:, inner * CHUNK:(inner + 1) * CHUNK],
-                    lhsT=wb_q[part][:, rows].bitcast(FP8X4), lhsT_scale=wb_sc[part][:, rows],
+                    lhsT=wb_q[g][:, rows].bitcast(FP8X4), lhsT_scale=wb_sc[g][:, rows],
                     rhs=z_q[c][:].bitcast(FP8X4), rhs_scale=z_sc[c][:],
                     start=False, stop=(inner == 1),
                 )
-            result = held("result%d_%d" % (c0, n), [P, HALF], F32)
-            if on_vector:
-                nc.vector.tensor_copy(result[:], o_ps[:])
-            else:
-                nc.scalar.copy(result[:], o_ps[:])
-            nc.sync.dma_start(out=out[n * P:(n + 1) * P, first:first + HALF], in_=result[:])
+            result = held("result%d_%d" % (2 * h, n), [P, HALF], F32)
+            copy(result[:], o_ps[:])
+            nc.sync.dma_start(out=out[n * P:(n + 1) * P, cols], in_=result[:])
 
-        def output_pair(c, pair, index, on_vector):
-            o_ps = bank(index, [P, 2, CHUNK], "o_ps")
-            for u in range(2):
-                n = 2 * pair + u
-                for a in range(2):
-                    for s in range(CHUNK // P):
-                        first = c * CHUNK + s * P
-                        nc.tensor.matmul_mx(
-                            out=o_ps[:, u, s * P:(s + 1) * P], lhsT=wp[:, a, 2 * n * P:2 * (n + 1) * P].bitcast(FP4X4),
-                            lhsT_scale=wp_sc[:, a, n * P:(n + 1) * P],
-                            rhs=picked(a, first, P).bitcast(FP8X4),
-                            rhs_scale=v_sc[a][:, c * CHUNK + s * P:c * CHUNK + (s + 1) * P],
-                            start=(u == 0 and a == 0 and s == 0), stop=False,
-                        )
-            for u in range(2):
-                rows = slice(u * P, (u + 1) * P)
-                nc.tensor.matmul_mx(
-                    out=o_ps[:, u, :], lhsT=wb_q[pair][:, rows].bitcast(FP8X4), lhsT_scale=wb_sc[pair][:, rows],
-                    rhs=z_q[c][:].bitcast(FP8X4), rhs_scale=z_sc[c][:], start=False, stop=(u == 1),
-                )
-            result = held("result_c%d_%d" % (c, pair), [P, 2, CHUNK], F32)
-            if on_vector:
-                nc.vector.tensor_copy(result[:], o_ps[:])
-            else:
-                nc.scalar.copy(result[:], o_ps[:])
-            rows = out[2 * pair * P:2 * (pair + 1) * P, c * CHUNK:(c + 1) * CHUNK]
-            nc.sync.dma_start(out=rows.rearrange("(u p) j -> p u j", u=2), in_=result[:])
+        on_scalar, on_vector = nc.scalar.copy, nc.vector.tensor_copy
 
-        gather_second_pass(0)
-        gather_second_pass(1)
-        round_wb(0, False)
-        residual(0, 0)
-        residual(1, 2)
+        for c in range(2):
+            gather(picked(1, c * CHUNK, CHUNK), tab[1], lists, c * CHUNK, CHUNK)
+        round_wb(0, on_scalar)
+        for c in range(2):
+            residual(c)
         quantize_wb(0)
-        round_wb(1, False)
-        round_wb(2, False)
-        weigh(0)
-        quantize_z(0)
-        weigh(1)
-        quantize_z(1)
+        for g in range(1, PARTS - 1):
+            round_wb(g, on_scalar)
+        for c in range(2):
+            make_z(c)
         quantize_wb(1)
-        gather_late_half()
+        v[1].append(held("v1_1", [P, HALF], U32, tag="rho_b0"))
+        gather(v[1][1][:], tab[1], lists, HALF, HALF)
         quantize_wb(2)
-        output_tile(0, 0, 4, False)
-        output_tile(0, 1, 5, False)
-        output_tile(0, 2, 6, False)
-        output_tile(0, 3, 7, False)
-        residual(2, 0)
-        round_wb(3, True)
-        residual(3, 2)
-        quantize_wb(3)
-        weigh(2)
-        quantize_z(2)
-        weigh(3)
-        quantize_z(3)
-        output_tile(0, 4, 4, False)
-        output_tile(0, 5, 5, False)
-        output_tile(0, 6, 6, False)
-        output_tile(0, 7, 7, False)
-        output_tile(2, 0, 0, True)
-        output_tile(2, 1, 1, False)
-        output_tile(2, 2, 2, True)
-        output_tile(2, 3, 3, False)
-        output_tile(2, 4, 4, True)
-        output_tile(2, 5, 5, False)
-        output_tile(2, 6, 6, True)
-        output_tile(2, 7, 7, False)
+        for n in range(TILES // 2):
+            output_tile(0, n, OUT_BANK + n, on_scalar)
+
+        residual(2)
+        round_wb(PARTS - 1, on_vector)
+        residual(3)
+        quantize_wb(PARTS - 1)
+        for c in range(2, CHUNKS):
+            make_z(c)
+        for n in range(TILES // 2, TILES):
+            output_tile(0, n, n, on_scalar)
+        for n in range(TILES):
+            output_tile(1, n, n, on_vector if n % 2 == 0 else on_scalar)

@@ -26,8 +26,7 @@ LIST_ROWS = 16
 LINE = 4
 PASSES, HALVES, CHUNKS, PARTS, TILES = K // K_PASS, S // HALF, S // CHUNK, K // CHUNK, K // P
 V2_FIRST, WR_FIRST = 8, 12
-W1_ON_SCALAR = 64
-OUT_BANK = 4
+W1_ON_SCALAR = 80
 
 
 def tile_list_wafer_drift_correction_kernel(
@@ -49,9 +48,9 @@ def tile_list_wafer_drift_correction_kernel(
         def load_words(tile, packed):
             nc.sync.dma_start(out=tile[:].bitcast(I32), in_=packed.rearrange("p c i -> p (c i)").bitcast(I32))
 
-        def load_plane(plane, rows, first=0, which=range(PACK)):
+        def load_plane(queue, plane, rows, first=0, which=range(PACK)):
             for r in which:
-                nc.sync.dma_start(out=plane[:].bitcast(I32)[first + r:P:QUADRANT], in_=rows[r].bitcast(I32))
+                queue.dma_start(out=plane[:].bitcast(I32)[first + r:P:QUADRANT], in_=rows[r].bitcast(I32))
 
         def gather(dst, window, offsets, entry, count):
             cols = slice(entry // LIST_ROWS, (entry + count) // LIST_ROWS)
@@ -64,107 +63,121 @@ def tile_list_wafer_drift_correction_kernel(
         wr_sc_raw = held("wr_sc_raw", [P, H], U8)
         wp_sc = held("wp_sc", [P, PASSES, K], U8)
         v_sc = [held("v_sc%d" % a, [P, S], U8) for a in range(PASSES)]
-
-        nc.gpsimd.memset(sc_win[:].bitcast(I32), 0)
-        nc.vector.memset(sc2_win[:].bitcast(I32), 0)
-        nc.vector.memset(wr_sc_raw[:].bitcast(I32), 0)
-        nc.vector.memset(wp_sc[:].bitcast(I32), 0)
-        for a in range(PASSES):
-            nc.vector.memset(v_sc[a][:].bitcast(I32), 0)
-
-        nc.sync.dma_start(lists[:], offs)
-        nc.sync.dma_start(lists2[:], offs2)
-        nc.sync.dma_start(
-            out=sc_win[:].bitcast(I32)[0:P:4, :],
-            in_=tab_scales.rearrange("a q t -> q a t").bitcast(I32),
-        )
         rho_t = held("rho_t", [P, PACK], F32)
         gain_t = held("gain_t", [P, PACK], F32)
         w1_raw = [held("w1_raw%d" % a, [P, PACK, H], F32) for a in range(PASSES)]
         tab = [held("tab%d" % a, [P, T], U32) for a in range(PASSES)]
         tab2 = held("tab2", [P, T], U32)
         wr_raw = held("wr_raw", [P, H], U32)
+        wp = [held("wp%d" % a, [P, 2 * K], U8) for a in range(PASSES)]
+        wb_raw = [held("wb_raw%d" % g, [P, PACK, CHUNK], F32) for g in range(PARTS)]
+        sc_picked = held("sc_picked", [P, S], U8)
+        v2_sc = held("v2_sc", [P, S], U8)
+        w1_bf = [held("w1_bf%d" % a, [P, PACK * H], BF16) for a in range(PASSES)]
+        w1_q = [held("w1_q%d" % a, [P, H], U32) for a in range(PASSES)]
+        w1_sc = [held("w1_sc%d" % a, [P, H], U8) for a in range(PASSES)]
+        wr_q = held("wr_q", [P, H], U32)
+        wr_sc = held("wr_sc", [P, H], U8)
+        z_q = [held("z_q%d" % c, [P, CHUNK], U32) for c in range(CHUNKS)]
+        z_sc = [held("z_sc%d" % c, [P, CHUNK], U8) for c in range(CHUNKS)]
+        wb_bf = {}
+        wb_q = [held("wb_q%d" % g, [P, CHUNK], U32) for g in range(PARTS)]
+        wb_sc = [held("wb_sc%d" % g, [P, CHUNK], U8) for g in range(PARTS)]
+        v, v2, rho_b, a_ps, resid, bounded, z_bf, units = {}, {}, {}, {}, {}, {}, {}, {}
+        wr_rows = wr_scales[0].rearrange("(d r) c -> r d c", r=PACK)
+        v2_rows = tab2_scales[0].rearrange("(d r) t -> r d t", r=PACK)
+        wp_rows = wp_scales.rearrange("a (d r) c -> r d a c", r=PACK)
+        on_scalar, on_vector = nc.scalar.copy, nc.vector.tensor_copy
+
+        def on_gpsimd(dst, src):
+            nc.gpsimd.tensor_scalar(dst, src, 1.0, 0.0, ALU.mult, ALU.add)
+
+        def load_sc_win(queue=nc.sync):
+            queue.dma_start(
+                out=sc_win[:].bitcast(I32)[0:P:4, :],
+                in_=tab_scales.rearrange("a q t -> q a t").bitcast(I32),
+            )
 
         def load_w1(a):
             rows = w1[a * K_PASS:(a + 1) * K_PASS, :]
             nc.sync.dma_start(out=w1_raw[a][:], in_=rows.rearrange("(p j) r -> p j r", j=PACK))
 
-        wr_rows = wr_scales[0].rearrange("(d r) c -> r d c", r=PACK)
-        load_words(tab2, tab2_words[0])
-        load_plane(sc2_win, tab2_scales[0].rearrange("(d r) t -> r d t", r=PACK), V2_FIRST)
-        load_words(wr_raw, wr_words[0])
-        load_plane(wr_sc_raw, wr_rows, WR_FIRST, range(1))
-        load_w1(0)
-        load_plane(wr_sc_raw, wr_rows, WR_FIRST, range(1, PACK))
-        nc.sync.dma_start(out=rho_t[:], in_=rho.rearrange("(p t) -> p t", t=PACK))
-        load_words(tab[0], tab_words[0])
-        load_plane(wp_sc, wp_scales.rearrange("a (d r) c -> r d a c", r=PACK))
-        load_w1(1)
-        nc.sync.dma_start(out=gain_t[:], in_=gain.rearrange("(p t) -> p t", t=PACK))
+        w1_half = [held("w1_half%d" % i, [P, PACK, H // 2], F32) for i in range(2)]
 
-        sc_picked = held("sc_picked", [P, S], U8)
-        gather(sc_picked[:], sc_win, lists, 0, S)
+        def load_w1_half(i):
+            rows = w1[K_PASS:2 * K_PASS, i * H // 2:(i + 1) * H // 2]
+            nc.sync.dma_start(out=w1_half[i][:], in_=rows.rearrange("(p j) r -> p j r", j=PACK))
 
-        def place_scales(a):
-            for r in range(PACK):
-                nc.sync.dma_start(
-                    out=v_sc[a][:].bitcast(I32)[r:P:QUADRANT],
-                    in_=sc_picked[:].bitcast(I32)[8 * r + 4 * a:P:QUADRANT],
-                )
+        def round_w1_half(i, copy):
+            dst = w1_bf[1][:].rearrange("p (t m j) -> p m j t", t=PACK, j=PACK)
+            src = w1_half[i][:].rearrange("p j (m t) -> p m j t", t=PACK)
+            copy(dst[:, i * P // 2:(i + 1) * P // 2], src)
 
-        wp = held("wp", [P, PASSES, 2 * K], U8)
-        wb_raw = [held("wb_raw%d" % g, [P, PACK, CHUNK], F32) for g in range(PARTS)]
+        def load_wp(a):
+            nc.sync.dma_start(out=wp[a][:].bitcast(I32), in_=wp_words[a].bitcast(I32))
 
         def load_wb(g):
             cols = wb[:, g * CHUNK:(g + 1) * CHUNK]
             nc.sync.dma_start(out=wb_raw[g][:], in_=cols.rearrange("(p j) n -> p j n", j=PACK))
 
-        place_scales(0)
-        load_words(tab[1], tab_words[1])
-        place_scales(1)
-        load_wb(0)
-        nc.sync.dma_start(out=wp[:].bitcast(I32), in_=wp_words.rearrange("a p c -> p a c").bitcast(I32))
-        for g in range(1, PARTS):
-            load_wb(g)
+        def load_vec(queue, tile, vec):
+            queue.dma_start(out=tile[:], in_=vec.rearrange("(p t) -> p t", t=PACK))
 
-        v2_sc = held("v2_sc", [P, S], U8)
-        w1_bf = [held("w1_bf%d" % a, [P, PACK * H], BF16) for a in range(PASSES)]
-        w1_q = [held("w1_q%d" % a, [P, H], U32) for a in range(PASSES)]
-        w1_sc = [held("w1_sc%d" % a, [P, H], U8) for a in range(PASSES)]
+        def place_scales(a, queue=nc.sync):
+            for r in range(PACK):
+                queue.dma_start(
+                    out=v_sc[a][:].bitcast(I32)[r:P:QUADRANT],
+                    in_=sc_picked[:].bitcast(I32)[8 * r + 4 * a:P:QUADRANT],
+                )
 
         def round_w1(a, split):
             dst = w1_bf[a][:].rearrange("p (t m j) -> p m j t", t=PACK, j=PACK)
             src = w1_raw[a][:].rearrange("p j (m t) -> p m j t", t=PACK)
-            nc.scalar.copy(dst[:, 0:split], src[:, 0:split])
+            if split > 0:
+                nc.scalar.copy(dst[:, 0:split], src[:, 0:split])
             if split < P:
                 nc.vector.tensor_copy(dst[:, split:P], src[:, split:P])
 
         def quantize_w1(a):
             nc.vector.quantize_mx(out=w1_q[a][:].bitcast(FP8X4), scales=w1_sc[a][:], in_=w1_bf[a][:])
 
-        round_w1(0, P)
-        v2 = [held("v2_0", [P, HALF], U32)]
-        gather(v2[0][:], tab2, lists2, 0, HALF)
-        gather(v2_sc[:], sc2_win, lists2, 0, S)
-        wr_q = held("wr_q", [P, H], U32)
-        wr_sc = held("wr_sc", [P, H], U8)
-        nc.vector.tensor_copy(
-            wr_q[:].bitcast(I32).rearrange("p (t m) -> p t m", t=PACK),
-            wr_raw[:].bitcast(I32).rearrange("p (m t) -> p t m", t=PACK),
-        )
-        nc.vector.tensor_copy(
-            wr_sc[:].rearrange("p (t m) -> p t m", t=PACK),
-            wr_sc_raw[:].rearrange("p (m t) -> p t m", t=PACK),
-        )
-        v2.append(held("v2_1", [P, HALF], U32, tag="wr_sc_raw"))
-        gather(v2[1][:], tab2, lists2, HALF, HALF)
+        def order_wr():
+            nc.vector.tensor_copy(
+                wr_q[:].bitcast(I32).rearrange("p (t m) -> p m t", t=PACK),
+                wr_raw[:].bitcast(I32).rearrange("p (m t) -> p m t", t=PACK),
+            )
+            nc.vector.tensor_copy(
+                wr_sc[:].rearrange("p (t m) -> p t m", t=PACK),
+                wr_sc_raw[:].rearrange("p (m t) -> p t m", t=PACK),
+            )
 
-        rho_b = []
+        def order_wr_on_gpsimd():
+            nc.gpsimd.tensor_copy(
+                wr_sc[:].rearrange("p (t m) -> p t m", t=PACK),
+                wr_sc_raw[:].rearrange("p (m t) -> p t m", t=PACK),
+            )
+            nc.gpsimd.tensor_copy(
+                wr_q[:].bitcast(I32).rearrange("p (t m) -> p t m", t=PACK),
+                wr_raw[:].bitcast(I32).rearrange("p (m t) -> p t m", t=PACK),
+            )
 
-        def reference_product(h, tag):
-            rho_b.append(held("rho_b%d" % h, [P, 2, PACK, CHUNK], F32, tag=tag))
+        def pick2(h, tag=None):
+            v2[h] = held("v2_%d" % h, [P, HALF], U32, tag=tag)
+            gather(v2[h][:], tab2, lists2, h * HALF, HALF)
+
+        def picked(a, entry, count):
+            return v[a, entry // HALF][:, entry % HALF:entry % HALF + count]
+
+        def pick(a, entry, count, tag=None):
+            h = entry // HALF
+            if (a, h) not in v:
+                v[a, h] = held("v%d_%d" % (a, h), [P, HALF], U32, tag=tag)
+            gather(picked(a, entry, count), tab[a], lists, entry, count)
+
+        def reference_product(h, banks, tag=None):
+            rho_b[h] = held("rho_b%d" % h, [P, 2, PACK, CHUNK], F32, tag=tag)
             for t in range(PACK):
-                b_ps = bank(PACK * h + t, [P, HALF], "b_ps")
+                b_ps = bank(banks[t], [P, HALF], "b_ps")
                 rows = slice(t * P, (t + 1) * P)
                 nc.tensor.matmul_mx(
                     out=b_ps[:], lhsT=wr_q[:, rows].bitcast(FP8X4), lhsT_scale=wr_sc[WR_FIRST:P, rows],
@@ -176,63 +189,55 @@ def tile_list_wafer_drift_correction_kernel(
                     ACT.Copy, scale=rho_t[:, t:t + 1],
                 )
 
-        v = [[held("v0_%d" % h, [P, HALF], U32) for h in range(HALVES)], [held("v1_0", [P, HALF], U32)]]
-
-        def picked(a, entry, count):
-            return v[a][entry // HALF][:, entry % HALF:entry % HALF + count]
-
-        reference_product(0, "rho_b0")
-        quantize_w1(0)
-        for h in range(HALVES):
-            gather(picked(0, h * HALF, HALF), tab[0], lists, h * HALF, HALF)
-        round_w1(1, W1_ON_SCALAR)
-        quantize_w1(1)
-        reference_product(1, "w1_raw1")
-
-        z_q = [held("z_q%d" % c, [P, CHUNK], U32) for c in range(CHUNKS)]
-        z_sc = [held("z_sc%d" % c, [P, CHUNK], U8) for c in range(CHUNKS)]
-        z_bf = {}
-        bounded = {}
-
-        def residual(c):
-            h, inner = divmod(c, 2)
-            resid = ring.tile([P, PACK, CHUNK], F32, name="resid")
-            for pair in range(2):
-                a_ps = bank(2 * inner + pair, [P, 2, CHUNK], "a_ps")
-                for a in range(PASSES):
-                    for u in range(2):
-                        rows = slice((2 * pair + u) * P, (2 * pair + u + 1) * P)
-                        nc.tensor.matmul_mx(
-                            out=a_ps[:, u, :], lhsT=w1_q[a][:, rows].bitcast(FP8X4), lhsT_scale=w1_sc[a][:, rows],
-                            rhs=picked(a, c * CHUNK, CHUNK).bitcast(FP8X4),
-                            rhs_scale=v_sc[a][:, c * CHUNK:(c + 1) * CHUNK],
-                            start=(a == 0 and u == 0), stop=(a == PASSES - 1 and u == 1),
-                        )
-                nc.vector.tensor_tensor(
-                    resid[:, 2 * pair:2 * pair + 2, :], rho_b[h][:, inner, 2 * pair:2 * pair + 2, :], a_ps[:],
-                    ALU.subtract,
+        def a_pass(c, pair, a, index):
+            if a == 0:
+                a_ps[c, pair] = bank(index, [P, 2, CHUNK], "a_ps")
+            for u in range(2):
+                rows = slice((2 * pair + u) * P, (2 * pair + u + 1) * P)
+                nc.tensor.matmul_mx(
+                    out=a_ps[c, pair][:, u, :], lhsT=w1_q[a][:, rows].bitcast(FP8X4), lhsT_scale=w1_sc[a][:, rows],
+                    rhs=picked(a, c * CHUNK, CHUNK).bitcast(FP8X4),
+                    rhs_scale=v_sc[a][:, c * CHUNK:(c + 1) * CHUNK],
+                    start=(a == 0 and u == 0), stop=(a == PASSES - 1 and u == 1),
                 )
-            bounded[c] = ring.tile([P, CHUNK, PACK], F32, name="bounded")
+
+        def subtract(c, pair):
+            h, inner = divmod(c, 2)
+            if pair == 0:
+                resid[c] = held("resid%d" % c, [P, PACK, CHUNK], F32)
+            nc.vector.tensor_tensor(
+                resid[c][:, 2 * pair:2 * pair + 2, :], rho_b[h][:, inner, 2 * pair:2 * pair + 2, :], a_ps[c, pair][:],
+                ALU.subtract,
+            )
+
+        def bound(c):
+            bounded[c] = held("bounded%d" % c, [P, CHUNK, PACK], F32)
             nc.scalar.activation(
                 bounded[c][:].rearrange("p (g i) t -> p g t i", i=LINE),
-                resid[:].rearrange("p t (g i) -> p g t i", i=LINE),
+                resid[c][:].rearrange("p t (g i) -> p g t i", i=LINE),
                 ACT.Tanh,
             )
 
-        def make_z(c):
+        def residual(c, banks, passes=range(PASSES)):
+            for pair in range(2):
+                for a in passes:
+                    a_pass(c, pair, a, banks[pair])
+                subtract(c, pair)
+            bound(c)
+
+        def weigh(c):
             z_bf[c] = held("z_bf%d" % c, [P, CHUNK, PACK], BF16)
             nc.vector.tensor_tensor(
                 z_bf[c][:], bounded[c][:], gain_t[:].unsqueeze(1).to_broadcast([P, CHUNK, PACK]), ALU.mult,
             )
+
+        def quantize_z(c):
             nc.vector.quantize_mx(
                 out=z_q[c][:].bitcast(FP8X4), scales=z_sc[c][:], in_=z_bf[c][:].rearrange("p j t -> p (j t)"),
             )
 
-        wb_bf = [held("wb_bf%d" % g, [P, CHUNK, PACK], BF16) for g in range(PARTS)]
-        wb_q = [held("wb_q%d" % g, [P, CHUNK], U32) for g in range(PARTS)]
-        wb_sc = [held("wb_sc%d" % g, [P, CHUNK], U8) for g in range(PARTS)]
-
-        def round_wb(g, copy):
+        def round_wb(g, copy, tag=None):
+            wb_bf[g] = held("wb_bf%d" % g, [P, CHUNK, PACK], BF16, tag=tag)
             copy(
                 wb_bf[g][:].rearrange("p (g i) j -> p g j i", i=LINE),
                 wb_raw[g][:].rearrange("p j (g i) -> p g j i", i=LINE),
@@ -243,55 +248,165 @@ def tile_list_wafer_drift_correction_kernel(
                 out=wb_q[g][:].bitcast(FP8X4), scales=wb_sc[g][:], in_=wb_bf[g][:].rearrange("p n j -> p (n j)"),
             )
 
-        def output_tile(h, n, index, copy):
-            cols = slice(h * HALF, (h + 1) * HALF)
-            o_ps = bank(index, [P, HALF], "o_ps")
-            for a in range(PASSES):
+        def x_pass(unit, a, index=None):
+            col, width, first = unit
+            count = HALF // width
+            if index is not None:
+                units[unit] = bank(index, [P, count, width], "o_ps")
+            step = HALF if width == HALF else P
+            for u in range(count):
+                n = first + u
+                for s in range(0, width, step):
+                    nc.tensor.matmul_mx(
+                        out=units[unit][:, u, s:s + step], lhsT=wp[a][:, 2 * n * P:2 * (n + 1) * P].bitcast(FP4X4),
+                        lhsT_scale=wp_sc[:, a, n * P:(n + 1) * P],
+                        rhs=picked(a, col + s, step).bitcast(FP8X4), rhs_scale=v_sc[a][:, col + s:col + s + step],
+                        start=(index is not None and u == 0 and s == 0), stop=False,
+                    )
+
+        def e_pass(unit, c):
+            col, width, first = unit
+            count = HALF // width
+            s = c * CHUNK - col
+            for u in range(count):
+                n = first + u
+                g, rows = n // 2, slice((n % 2) * P, (n % 2 + 1) * P)
                 nc.tensor.matmul_mx(
-                    out=o_ps[:], lhsT=wp[:, a, 2 * n * P:2 * (n + 1) * P].bitcast(FP4X4),
-                    lhsT_scale=wp_sc[:, a, n * P:(n + 1) * P],
-                    rhs=picked(a, h * HALF, HALF).bitcast(FP8X4), rhs_scale=v_sc[a][:, cols],
-                    start=(a == 0), stop=False,
-                )
-            g, rows = n // 2, slice((n % 2) * P, (n % 2 + 1) * P)
-            for inner in range(2):
-                c = 2 * h + inner
-                nc.tensor.matmul_mx(
-                    out=o_ps[:, inner * CHUNK:(inner + 1) * CHUNK],
+                    out=units[unit][:, u, s:s + CHUNK],
                     lhsT=wb_q[g][:, rows].bitcast(FP8X4), lhsT_scale=wb_sc[g][:, rows],
                     rhs=z_q[c][:].bitcast(FP8X4), rhs_scale=z_sc[c][:],
-                    start=False, stop=(inner == 1),
+                    start=False, stop=(u == count - 1 and s + CHUNK == width),
                 )
-            result = held("result%d_%d" % (2 * h, n), [P, HALF], F32)
-            copy(result[:], o_ps[:])
-            nc.sync.dma_start(out=out[n * P:(n + 1) * P, cols], in_=result[:])
 
-        on_scalar, on_vector = nc.scalar.copy, nc.vector.tensor_copy
+        results = {}
+
+        def finish(unit, copy):
+            col, width, first = unit
+            count = HALF // width
+            result = held("result%d_%d" % (col, first), [P, count, width], F32)
+            results[unit] = result
+            copy(result[:], units[unit][:])
+            rows = out[first * P:(first + count) * P, col:col + width]
+            nc.sync.dma_start(out=rows.rearrange("(u p) c -> p u c", p=P), in_=result[:])
+
+
+        nc.vector.memset(sc_win[:].bitcast(I32), 0)
+        nc.vector.memset(sc2_win[:].bitcast(I32), 0)
+        nc.gpsimd.memset(wp_sc[:].bitcast(I32), 0)
+        nc.vector.memset(wr_sc_raw[:].bitcast(I32), 0)
+        for a in range(PASSES):
+            nc.vector.memset(v_sc[a][:].bitcast(I32), 0)
+        nc.sync.dma_start(lists[:], offs)
+        nc.sync.dma_start(lists2[:], offs2)
+        load_sc_win()
+        load_plane(nc.scalar, sc2_win, v2_rows, V2_FIRST)
+        load_plane(nc.gpsimd, wp_sc, wp_rows)
+        load_vec(nc.gpsimd, gain_t, gain)
+        load_w1(0)
+        load_words(tab2, tab2_words[0])
+        load_words(wr_raw, wr_words[0])
+        load_plane(nc.sync, wr_sc_raw, wr_rows, WR_FIRST)
+        load_vec(nc.sync, rho_t, rho)
+        load_w1(1)
+        load_words(tab[0], tab_words[0])
+        gather(sc_picked[:], sc_win, lists, 0, S)
+        place_scales(0)
+        load_words(tab[1], tab_words[1])
+        place_scales(1)
+        load_wb(0)
+        load_wp(0)
+        load_wp(1)
+        for g in range(1, PARTS):
+            load_wb(g)
+        gather(v2_sc[:], sc2_win, lists2, 0, S)
+        round_w1(0, P)
+        quantize_w1(0)
+        pick2(0)
+        pick2(1)
+        order_wr()
+        round_w1(1, 64)
+        reference_product(0, [0, 1, 2, 3], tag="w1_raw1")
+        quantize_w1(1)
+        reference_product(1, [4, 5, 6, 7], tag="w1_bf1")
+        pick(0, 0, HALF)
+        pick(0, HALF, HALF)
+
+        h0 = [(0, HALF, n) for n in range(TILES)]
+        h1 = [(HALF, HALF, n) for n in range(TILES)]
+
+        def a_chunk(c, pair, index):
+            for a in range(PASSES):
+                a_pass(c, pair, a, index)
+
+        def x_both(unit, index):
+            x_pass(unit, 0, index)
+            x_pass(unit, 1)
+
+        def e_both(unit):
+            for inner in range(2):
+                e_pass(unit, unit[0] // CHUNK + inner)
 
         for c in range(2):
-            gather(picked(1, c * CHUNK, CHUNK), tab[1], lists, c * CHUNK, CHUNK)
+            for pair in range(2):
+                a_pass(c, pair, 0, 2 * c + pair)
+        pick(1, 0, CHUNK)
+        pick(1, CHUNK, CHUNK)
         round_wb(0, on_scalar)
         for c in range(2):
-            residual(c)
+            for pair in range(2):
+                a_pass(c, pair, 1, 2 * c + pair)
+            for pair in range(2):
+                subtract(c, pair)
+            bound(c)
         quantize_wb(0)
-        for g in range(1, PARTS - 1):
-            round_wb(g, on_scalar)
-        for c in range(2):
-            make_z(c)
+        pick(1, HALF, HALF, tag="w1_raw1")
+        for n in range(4):
+            x_both(h0[n], 4 + n)
+        for n in range(4, 6):
+            x_both(h0[n], n - 4)
+        for pair in range(2):
+            a_chunk(2, pair, 2 + pair)
+        weigh(0)
+        weigh(1)
+        quantize_z(0)
+        quantize_z(1)
+        round_wb(1, on_scalar, tag="resid1")
+        round_wb(2, on_scalar)
+        round_wb(3, on_scalar)
         quantize_wb(1)
-        v[1].append(held("v1_1", [P, HALF], U32, tag="rho_b0"))
-        gather(v[1][1][:], tab[1], lists, HALF, HALF)
+        for n in range(4):
+            e_both(h0[n])
+        subtract(2, 0)
+        subtract(2, 1)
+        bound(2)
         quantize_wb(2)
-        for n in range(TILES // 2):
-            output_tile(0, n, OUT_BANK + n, on_scalar)
-
-        residual(2)
-        round_wb(PARTS - 1, on_vector)
-        residual(3)
-        quantize_wb(PARTS - 1)
-        for c in range(2, CHUNKS):
-            make_z(c)
-        for n in range(TILES // 2, TILES):
-            output_tile(0, n, n, on_scalar)
+        a_chunk(3, 0, 2)
+        e_both(h0[4])
+        e_both(h0[5])
+        a_chunk(3, 1, 3)
+        finish(h0[0], on_vector)
+        quantize_wb(3)
+        finish(h0[1], on_scalar)
+        finish(h0[2], on_scalar)
+        subtract(3, 0)
+        subtract(3, 1)
+        bound(3)
+        x_both(h0[6], 4)
+        e_both(h0[6])
+        x_both(h0[7], 5)
+        e_both(h0[7])
+        weigh(2)
+        finish(h0[3], on_vector)
+        quantize_z(2)
+        for n in range(4, 8):
+            finish(h0[n], on_scalar)
+        weigh(3)
+        quantize_z(3)
+        order = [2, 3, 6, 7, 0, 1, 4, 5]
+        for n in range(5):
+            x_both(h1[n], order[n])
         for n in range(TILES):
-            output_tile(1, n, n, on_vector if n % 2 == 0 else on_scalar)
+            if n >= 5:
+                x_both(h1[n], order[n])
+            e_both(h1[n])
+            finish(h1[n], on_vector if n % 2 == 0 else on_scalar)

@@ -143,8 +143,8 @@ def tile_list_wafer_drift_correction_kernel(
 
         def order_wr():
             nc.vector.tensor_copy(
-                wr_q[:].bitcast(I32).rearrange("p (t m) -> p m t", t=PACK),
-                wr_raw[:].bitcast(I32).rearrange("p (m t) -> p m t", t=PACK),
+                wr_q[:].bitcast(I32).rearrange("p (t m) -> p t m", t=PACK),
+                wr_raw[:].bitcast(I32).rearrange("p (m t) -> p t m", t=PACK),
             )
             nc.vector.tensor_copy(
                 wr_sc[:].rearrange("p (t m) -> p t m", t=PACK),
@@ -290,40 +290,42 @@ def tile_list_wafer_drift_correction_kernel(
             nc.sync.dma_start(out=rows.rearrange("(u p) c -> p u c", p=P), in_=result[:])
 
 
-        nc.vector.memset(sc_win[:].bitcast(I32), 0)
+        nc.gpsimd.memset(sc_win[:].bitcast(I32), 0)
         nc.vector.memset(sc2_win[:].bitcast(I32), 0)
-        nc.gpsimd.memset(wp_sc[:].bitcast(I32), 0)
         nc.vector.memset(wr_sc_raw[:].bitcast(I32), 0)
+        nc.vector.memset(wp_sc[:].bitcast(I32), 0)
         for a in range(PASSES):
             nc.vector.memset(v_sc[a][:].bitcast(I32), 0)
         nc.sync.dma_start(lists[:], offs)
         nc.sync.dma_start(lists2[:], offs2)
         load_sc_win()
-        load_plane(nc.scalar, sc2_win, v2_rows, V2_FIRST)
-        load_plane(nc.gpsimd, wp_sc, wp_rows)
-        load_vec(nc.gpsimd, gain_t, gain)
-        load_w1(0)
         load_words(tab2, tab2_words[0])
+        load_plane(nc.sync, sc2_win, v2_rows, V2_FIRST)
         load_words(wr_raw, wr_words[0])
-        load_plane(nc.sync, wr_sc_raw, wr_rows, WR_FIRST)
+        load_plane(nc.sync, wr_sc_raw, wr_rows, WR_FIRST, range(1))
+        load_w1(0)
+        load_plane(nc.sync, wr_sc_raw, wr_rows, WR_FIRST, range(1, PACK))
         load_vec(nc.sync, rho_t, rho)
+        load_vec(nc.sync, gain_t, gain)
         load_w1(1)
+        load_plane(nc.sync, wp_sc, wp_rows, 0, range(2))
         load_words(tab[0], tab_words[0])
         gather(sc_picked[:], sc_win, lists, 0, S)
         place_scales(0)
         load_words(tab[1], tab_words[1])
         place_scales(1)
         load_wb(0)
+        load_plane(nc.sync, wp_sc, wp_rows, 0, range(2, PACK))
         load_wp(0)
         load_wp(1)
         for g in range(1, PARTS):
             load_wb(g)
-        gather(v2_sc[:], sc2_win, lists2, 0, S)
-        round_w1(0, P)
-        quantize_w1(0)
         pick2(0)
         pick2(1)
+        gather(v2_sc[:], sc2_win, lists2, 0, S)
         order_wr()
+        round_w1(0, P)
+        quantize_w1(0)
         round_w1(1, 64)
         reference_product(0, [0, 1, 2, 3], tag="w1_raw1")
         quantize_w1(1)

@@ -23,7 +23,7 @@ K_PASS = P * PACK
 HALF = 512
 CHUNK = 256
 LIST_ROWS = 16
-LINE = 4
+LINE = 2
 PASSES, HALVES, CHUNKS, PARTS, TILES = K // K_PASS, S // HALF, S // CHUNK, K // CHUNK, K // P
 V2_FIRST, WR_FIRST = 8, 12
 W1_ON_SCALAR = 80
@@ -133,10 +133,8 @@ def tile_list_wafer_drift_correction_kernel(
         def round_w1(a, split):
             dst = w1_bf[a][:].rearrange("p (t m j) -> p m j t", t=PACK, j=PACK)
             src = w1_raw[a][:].rearrange("p j (m t) -> p m j t", t=PACK)
-            if split > 0:
-                nc.scalar.copy(dst[:, 0:split], src[:, 0:split])
-            if split < P:
-                nc.vector.tensor_copy(dst[:, split:P], src[:, split:P])
+            nc.scalar.copy(dst[:, :, :, 0:2], src[:, :, :, 0:2])
+            (nc.scalar.copy if split == P else nc.vector.tensor_copy)(dst[:, :, :, 2:4], src[:, :, :, 2:4])
 
         def quantize_w1(a):
             nc.vector.quantize_mx(out=w1_q[a][:].bitcast(FP8X4), scales=w1_sc[a][:], in_=w1_bf[a][:])
@@ -249,8 +247,7 @@ def tile_list_wafer_drift_correction_kernel(
             )
 
         def x_pass(unit, a, index=None):
-            col, width, first = unit
-            count = HALF // width
+            col, width, first, count = unit
             if index is not None:
                 units[unit] = bank(index, [P, count, width], "o_ps")
             step = HALF if width == HALF else P
@@ -265,8 +262,7 @@ def tile_list_wafer_drift_correction_kernel(
                     )
 
         def e_pass(unit, c):
-            col, width, first = unit
-            count = HALF // width
+            col, width, first, count = unit
             s = c * CHUNK - col
             for u in range(count):
                 n = first + u
@@ -281,8 +277,7 @@ def tile_list_wafer_drift_correction_kernel(
         results = {}
 
         def finish(unit, copy):
-            col, width, first = unit
-            count = HALF // width
+            col, width, first, count = unit
             result = held("result%d_%d" % (col, first), [P, count, width], F32)
             results[unit] = result
             copy(result[:], units[unit][:])
@@ -297,16 +292,16 @@ def tile_list_wafer_drift_correction_kernel(
         for a in range(PASSES):
             nc.vector.memset(v_sc[a][:].bitcast(I32), 0)
         nc.sync.dma_start(lists[:], offs)
+        load_words(wr_raw, wr_words[0])
+        load_vec(nc.sync, rho_t, rho)
+        load_vec(nc.sync, gain_t, gain)
         nc.sync.dma_start(lists2[:], offs2)
         load_sc_win()
         load_words(tab2, tab2_words[0])
         load_plane(nc.sync, sc2_win, v2_rows, V2_FIRST)
-        load_words(wr_raw, wr_words[0])
         load_plane(nc.sync, wr_sc_raw, wr_rows, WR_FIRST, range(1))
         load_w1(0)
         load_plane(nc.sync, wr_sc_raw, wr_rows, WR_FIRST, range(1, PACK))
-        load_vec(nc.sync, rho_t, rho)
-        load_vec(nc.sync, gain_t, gain)
         load_w1(1)
         load_plane(nc.sync, wp_sc, wp_rows, 0, range(2))
         load_words(tab[0], tab_words[0])
@@ -333,8 +328,8 @@ def tile_list_wafer_drift_correction_kernel(
         pick(0, 0, HALF)
         pick(0, HALF, HALF)
 
-        h0 = [(0, HALF, n) for n in range(TILES)]
-        h1 = [(HALF, HALF, n) for n in range(TILES)]
+        h0 = [(0, HALF, n, 1) for n in range(TILES)]
+        h1 = [(HALF, HALF, n, 1) for n in range(TILES)]
 
         def a_chunk(c, pair, index):
             for a in range(PASSES):

@@ -23,10 +23,10 @@ K_PASS = P * PACK
 HALF = 512
 CHUNK = 256
 LIST_ROWS = 16
-LINE = 2
-PASSES, HALVES, CHUNKS, PARTS, TILES = K // K_PASS, S // HALF, S // CHUNK, K // CHUNK, K // P
+PAIR = 2
+PASSES, CHUNKS, PARTS, TILES = K // K_PASS, S // CHUNK, K // CHUNK, K // P
+BANKS = 8
 V2_FIRST, WR_FIRST = 8, 12
-W1_ON_SCALAR = 80
 
 
 def tile_list_wafer_drift_correction_kernel(
@@ -36,25 +36,14 @@ def tile_list_wafer_drift_correction_kernel(
     nc = tc.nc
     with ExitStack() as ctx:
         keep = ctx.enter_context(tc.tile_pool(name="keep", bufs=1))
-        ring = ctx.enter_context(tc.tile_pool(name="ring", bufs=2))
         psum = ctx.enter_context(tc.psum_pool(name="psum", bufs=1))
+        on_scalar, on_vector = nc.scalar.copy, nc.vector.tensor_copy
 
         def held(name, shape, dtype, tag=None):
             return keep.tile(shape, dtype, name=name, tag=tag or name, align_bytes=64)
 
         def bank(index, shape, name):
             return psum.tile(shape, F32, name=name, tag="bank%d" % index)
-
-        def load_words(tile, packed):
-            nc.sync.dma_start(out=tile[:].bitcast(I32), in_=packed.rearrange("p c i -> p (c i)").bitcast(I32))
-
-        def load_plane(queue, plane, rows, first=0, which=range(PACK)):
-            for r in which:
-                queue.dma_start(out=plane[:].bitcast(I32)[first + r:P:QUADRANT], in_=rows[r].bitcast(I32))
-
-        def gather(dst, window, offsets, entry, count):
-            cols = slice(entry // LIST_ROWS, (entry + count) // LIST_ROWS)
-            nc.vector.tensor_copy(dst, window[:].indirect(offsets[:, cols]))
 
         lists = keep.tile([P, S // LIST_ROWS], U16, name="lists")
         lists2 = keep.tile([P, S // LIST_ROWS], U16, name="lists2")
@@ -80,38 +69,23 @@ def tile_list_wafer_drift_correction_kernel(
         wr_sc = held("wr_sc", [P, H], U8)
         z_q = [held("z_q%d" % c, [P, CHUNK], U32) for c in range(CHUNKS)]
         z_sc = [held("z_sc%d" % c, [P, CHUNK], U8) for c in range(CHUNKS)]
-        wb_bf = {}
         wb_q = [held("wb_q%d" % g, [P, CHUNK], U32) for g in range(PARTS)]
         wb_sc = [held("wb_sc%d" % g, [P, CHUNK], U8) for g in range(PARTS)]
-        v, v2, rho_b, a_ps, resid, bounded, z_bf, units = {}, {}, {}, {}, {}, {}, {}, {}
-        wr_rows = wr_scales[0].rearrange("(d r) c -> r d c", r=PACK)
-        v2_rows = tab2_scales[0].rearrange("(d r) t -> r d t", r=PACK)
-        wp_rows = wp_scales.rearrange("a (d r) c -> r d a c", r=PACK)
-        on_scalar, on_vector = nc.scalar.copy, nc.vector.tensor_copy
+        v, v2, rho_b, a_ps, resid, bounded, z_bf, wb_bf, o_ps = {}, {}, {}, {}, {}, {}, {}, {}, {}
 
-        def on_gpsimd(dst, src):
-            nc.gpsimd.tensor_scalar(dst, src, 1.0, 0.0, ALU.mult, ALU.add)
+        def load_words(tile, packed):
+            nc.sync.dma_start(out=tile[:].bitcast(I32), in_=packed.rearrange("p c i -> p (c i)").bitcast(I32))
 
-        def load_sc_win(queue=nc.sync):
-            queue.dma_start(
-                out=sc_win[:].bitcast(I32)[0:P:4, :],
-                in_=tab_scales.rearrange("a q t -> q a t").bitcast(I32),
-            )
+        def load_plane(plane, rows, first, which):
+            for r in which:
+                nc.sync.dma_start(out=plane[:].bitcast(I32)[first + r:P:QUADRANT], in_=rows[r].bitcast(I32))
+
+        def load_by_slice(tile, vec):
+            nc.sync.dma_start(out=tile[:], in_=vec.rearrange("(p t) -> p t", t=PACK))
 
         def load_w1(a):
             rows = w1[a * K_PASS:(a + 1) * K_PASS, :]
             nc.sync.dma_start(out=w1_raw[a][:], in_=rows.rearrange("(p j) r -> p j r", j=PACK))
-
-        w1_half = [held("w1_half%d" % i, [P, PACK, H // 2], F32) for i in range(2)]
-
-        def load_w1_half(i):
-            rows = w1[K_PASS:2 * K_PASS, i * H // 2:(i + 1) * H // 2]
-            nc.sync.dma_start(out=w1_half[i][:], in_=rows.rearrange("(p j) r -> p j r", j=PACK))
-
-        def round_w1_half(i, copy):
-            dst = w1_bf[1][:].rearrange("p (t m j) -> p m j t", t=PACK, j=PACK)
-            src = w1_half[i][:].rearrange("p j (m t) -> p m j t", t=PACK)
-            copy(dst[:, i * P // 2:(i + 1) * P // 2], src)
 
         def load_wp(a):
             nc.sync.dma_start(out=wp[a][:].bitcast(I32), in_=wp_words[a].bitcast(I32))
@@ -120,62 +94,48 @@ def tile_list_wafer_drift_correction_kernel(
             cols = wb[:, g * CHUNK:(g + 1) * CHUNK]
             nc.sync.dma_start(out=wb_raw[g][:], in_=cols.rearrange("(p j) n -> p j n", j=PACK))
 
-        def load_vec(queue, tile, vec):
-            queue.dma_start(out=tile[:], in_=vec.rearrange("(p t) -> p t", t=PACK))
-
-        def place_scales(a, queue=nc.sync):
+        def place_scales(a):
             for r in range(PACK):
-                queue.dma_start(
+                nc.sync.dma_start(
                     out=v_sc[a][:].bitcast(I32)[r:P:QUADRANT],
                     in_=sc_picked[:].bitcast(I32)[8 * r + 4 * a:P:QUADRANT],
                 )
 
-        def round_w1(a, split):
-            dst = w1_bf[a][:].rearrange("p (t m j) -> p m j t", t=PACK, j=PACK)
-            src = w1_raw[a][:].rearrange("p j (m t) -> p m j t", t=PACK)
-            nc.scalar.copy(dst[:, :, :, 0:2], src[:, :, :, 0:2])
-            (nc.scalar.copy if split == P else nc.vector.tensor_copy)(dst[:, :, :, 2:4], src[:, :, :, 2:4])
-
-        def quantize_w1(a):
-            nc.vector.quantize_mx(out=w1_q[a][:].bitcast(FP8X4), scales=w1_sc[a][:], in_=w1_bf[a][:])
-
-        def order_wr():
-            nc.vector.tensor_copy(
-                wr_q[:].bitcast(I32).rearrange("p (t m) -> p t m", t=PACK),
-                wr_raw[:].bitcast(I32).rearrange("p (m t) -> p t m", t=PACK),
-            )
-            nc.vector.tensor_copy(
-                wr_sc[:].rearrange("p (t m) -> p t m", t=PACK),
-                wr_sc_raw[:].rearrange("p (m t) -> p t m", t=PACK),
-            )
-
-        def order_wr_on_gpsimd():
-            nc.gpsimd.tensor_copy(
-                wr_sc[:].rearrange("p (t m) -> p t m", t=PACK),
-                wr_sc_raw[:].rearrange("p (m t) -> p t m", t=PACK),
-            )
-            nc.gpsimd.tensor_copy(
-                wr_q[:].bitcast(I32).rearrange("p (t m) -> p t m", t=PACK),
-                wr_raw[:].bitcast(I32).rearrange("p (m t) -> p t m", t=PACK),
-            )
-
-        def pick2(h, tag=None):
-            v2[h] = held("v2_%d" % h, [P, HALF], U32, tag=tag)
-            gather(v2[h][:], tab2, lists2, h * HALF, HALF)
+        def gather(dst, window, offsets, entry, count):
+            cols = slice(entry // LIST_ROWS, (entry + count) // LIST_ROWS)
+            nc.vector.tensor_copy(dst, window[:].indirect(offsets[:, cols]))
 
         def picked(a, entry, count):
             return v[a, entry // HALF][:, entry % HALF:entry % HALF + count]
 
-        def pick(a, entry, count, tag=None):
-            h = entry // HALF
-            if (a, h) not in v:
-                v[a, h] = held("v%d_%d" % (a, h), [P, HALF], U32, tag=tag)
+        def pick(a, entry, count):
             gather(picked(a, entry, count), tab[a], lists, entry, count)
 
-        def reference_product(h, banks, tag=None):
+        def round_w1(a, upper):
+            dst = w1_bf[a][:].rearrange("p (t m j) -> p m j t", t=PACK, j=PACK)
+            src = w1_raw[a][:].rearrange("p j (m t) -> p m j t", t=PACK)
+            on_scalar(dst[:, :, :, 0:PAIR], src[:, :, :, 0:PAIR])
+            upper(dst[:, :, :, PAIR:PACK], src[:, :, :, PAIR:PACK])
+
+        def quantize_w1(a):
+            nc.vector.quantize_mx(out=w1_q[a][:].bitcast(FP8X4), scales=w1_sc[a][:], in_=w1_bf[a][:])
+
+        def round_wb(g, copy, tag=None):
+            wb_bf[g] = held("wb_bf%d" % g, [P, CHUNK, PACK], BF16, tag=tag)
+            copy(
+                wb_bf[g][:].rearrange("p (g i) j -> p g j i", i=PAIR),
+                wb_raw[g][:].rearrange("p j (g i) -> p g j i", i=PAIR),
+            )
+
+        def quantize_wb(g):
+            nc.vector.quantize_mx(
+                out=wb_q[g][:].bitcast(FP8X4), scales=wb_sc[g][:], in_=wb_bf[g][:].rearrange("p n j -> p (n j)"),
+            )
+
+        def reference_product(h, first_bank, tag):
             rho_b[h] = held("rho_b%d" % h, [P, 2, PACK, CHUNK], F32, tag=tag)
             for t in range(PACK):
-                b_ps = bank(banks[t], [P, HALF], "b_ps")
+                b_ps = bank(first_bank + t, [P, HALF], "b_ps")
                 rows = slice(t * P, (t + 1) * P)
                 nc.tensor.matmul_mx(
                     out=b_ps[:], lhsT=wr_q[:, rows].bitcast(FP8X4), lhsT_scale=wr_sc[WR_FIRST:P, rows],
@@ -187,9 +147,7 @@ def tile_list_wafer_drift_correction_kernel(
                     ACT.Copy, scale=rho_t[:, t:t + 1],
                 )
 
-        def a_pass(c, pair, a, index):
-            if a == 0:
-                a_ps[c, pair] = bank(index, [P, 2, CHUNK], "a_ps")
+        def a_pass(c, pair, a):
             for u in range(2):
                 rows = slice((2 * pair + u) * P, (2 * pair + u + 1) * P)
                 nc.tensor.matmul_mx(
@@ -199,29 +157,23 @@ def tile_list_wafer_drift_correction_kernel(
                     start=(a == 0 and u == 0), stop=(a == PASSES - 1 and u == 1),
                 )
 
+        def a_product(c, pair, index):
+            a_ps[c, pair] = bank(index, [P, 2, CHUNK], "a_ps")
+            for a in range(PASSES):
+                a_pass(c, pair, a)
+
         def subtract(c, pair):
             h, inner = divmod(c, 2)
-            if pair == 0:
-                resid[c] = held("resid%d" % c, [P, PACK, CHUNK], F32)
-            nc.vector.tensor_tensor(
-                resid[c][:, 2 * pair:2 * pair + 2, :], rho_b[h][:, inner, 2 * pair:2 * pair + 2, :], a_ps[c, pair][:],
-                ALU.subtract,
-            )
+            two = slice(2 * pair, 2 * pair + 2)
+            nc.vector.tensor_tensor(resid[c][:, two, :], rho_b[h][:, inner, two, :], a_ps[c, pair][:], ALU.subtract)
 
         def bound(c):
             bounded[c] = held("bounded%d" % c, [P, CHUNK, PACK], F32)
             nc.scalar.activation(
-                bounded[c][:].rearrange("p (g i) t -> p g t i", i=LINE),
-                resid[c][:].rearrange("p t (g i) -> p g t i", i=LINE),
+                bounded[c][:].rearrange("p (g i) t -> p g t i", i=PAIR),
+                resid[c][:].rearrange("p t (g i) -> p g t i", i=PAIR),
                 ACT.Tanh,
             )
-
-        def residual(c, banks, passes=range(PASSES)):
-            for pair in range(2):
-                for a in passes:
-                    a_pass(c, pair, a, banks[pair])
-                subtract(c, pair)
-            bound(c)
 
         def weigh(c):
             z_bf[c] = held("z_bf%d" % c, [P, CHUNK, PACK], BF16)
@@ -234,56 +186,31 @@ def tile_list_wafer_drift_correction_kernel(
                 out=z_q[c][:].bitcast(FP8X4), scales=z_sc[c][:], in_=z_bf[c][:].rearrange("p j t -> p (j t)"),
             )
 
-        def round_wb(g, copy, tag=None):
-            wb_bf[g] = held("wb_bf%d" % g, [P, CHUNK, PACK], BF16, tag=tag)
-            copy(
-                wb_bf[g][:].rearrange("p (g i) j -> p g j i", i=LINE),
-                wb_raw[g][:].rearrange("p j (g i) -> p g j i", i=LINE),
-            )
-
-        def quantize_wb(g):
-            nc.vector.quantize_mx(
-                out=wb_q[g][:].bitcast(FP8X4), scales=wb_sc[g][:], in_=wb_bf[g][:].rearrange("p n j -> p (n j)"),
-            )
-
-        def x_pass(unit, a, index=None):
-            col, width, first, count = unit
-            if index is not None:
-                units[unit] = bank(index, [P, count, width], "o_ps")
-            step = HALF if width == HALF else P
-            for u in range(count):
-                n = first + u
-                for s in range(0, width, step):
-                    nc.tensor.matmul_mx(
-                        out=units[unit][:, u, s:s + step], lhsT=wp[a][:, 2 * n * P:2 * (n + 1) * P].bitcast(FP4X4),
-                        lhsT_scale=wp_sc[:, a, n * P:(n + 1) * P],
-                        rhs=picked(a, col + s, step).bitcast(FP8X4), rhs_scale=v_sc[a][:, col + s:col + s + step],
-                        start=(index is not None and u == 0 and s == 0), stop=False,
-                    )
-
-        def e_pass(unit, c):
-            col, width, first, count = unit
-            s = c * CHUNK - col
-            for u in range(count):
-                n = first + u
-                g, rows = n // 2, slice((n % 2) * P, (n % 2 + 1) * P)
+        def calibrate(h, n, index):
+            o_ps[h, n] = bank(index, [P, HALF], "o_ps")
+            for a in range(PASSES):
                 nc.tensor.matmul_mx(
-                    out=units[unit][:, u, s:s + CHUNK],
-                    lhsT=wb_q[g][:, rows].bitcast(FP8X4), lhsT_scale=wb_sc[g][:, rows],
-                    rhs=z_q[c][:].bitcast(FP8X4), rhs_scale=z_sc[c][:],
-                    start=False, stop=(u == count - 1 and s + CHUNK == width),
+                    out=o_ps[h, n][:], lhsT=wp[a][:, 2 * n * P:2 * (n + 1) * P].bitcast(FP4X4),
+                    lhsT_scale=wp_sc[:, a, n * P:(n + 1) * P],
+                    rhs=picked(a, h * HALF, HALF).bitcast(FP8X4), rhs_scale=v_sc[a][:, h * HALF:(h + 1) * HALF],
+                    start=(a == 0), stop=False,
                 )
 
-        results = {}
+        def correct(h, n):
+            g, rows = n // 2, slice((n % 2) * P, (n % 2 + 1) * P)
+            for inner in range(2):
+                c = 2 * h + inner
+                nc.tensor.matmul_mx(
+                    out=o_ps[h, n][:, inner * CHUNK:(inner + 1) * CHUNK],
+                    lhsT=wb_q[g][:, rows].bitcast(FP8X4), lhsT_scale=wb_sc[g][:, rows],
+                    rhs=z_q[c][:].bitcast(FP8X4), rhs_scale=z_sc[c][:],
+                    start=False, stop=(inner == 1),
+                )
 
-        def finish(unit, copy):
-            col, width, first, count = unit
-            result = held("result%d_%d" % (col, first), [P, count, width], F32)
-            results[unit] = result
-            copy(result[:], units[unit][:])
-            rows = out[first * P:(first + count) * P, col:col + width]
-            nc.sync.dma_start(out=rows.rearrange("(u p) c -> p u c", p=P), in_=result[:])
-
+        def finish(h, n, copy):
+            result = held("result%d_%d" % (h, n), [P, HALF], F32)
+            copy(result[:], o_ps[h, n][:])
+            nc.sync.dma_start(out=out[n * P:(n + 1) * P, h * HALF:(h + 1) * HALF], in_=result[:])
 
         nc.gpsimd.memset(sc_win[:].bitcast(I32), 0)
         nc.vector.memset(sc2_win[:].bitcast(I32), 0)
@@ -291,119 +218,118 @@ def tile_list_wafer_drift_correction_kernel(
         nc.vector.memset(wp_sc[:].bitcast(I32), 0)
         for a in range(PASSES):
             nc.vector.memset(v_sc[a][:].bitcast(I32), 0)
+
+        wr_rows = wr_scales[0].rearrange("(d r) c -> r d c", r=PACK)
+        wp_rows = wp_scales.rearrange("a (d r) c -> r d a c", r=PACK)
         nc.sync.dma_start(lists[:], offs)
         load_words(wr_raw, wr_words[0])
-        load_vec(nc.sync, rho_t, rho)
-        load_vec(nc.sync, gain_t, gain)
+        load_by_slice(rho_t, rho)
+        load_by_slice(gain_t, gain)
         nc.sync.dma_start(lists2[:], offs2)
-        load_sc_win()
+        nc.sync.dma_start(
+            out=sc_win[:].bitcast(I32)[0:P:4, :],
+            in_=tab_scales.rearrange("a q t -> q a t").bitcast(I32),
+        )
         load_words(tab2, tab2_words[0])
-        load_plane(nc.sync, sc2_win, v2_rows, V2_FIRST)
-        load_plane(nc.sync, wr_sc_raw, wr_rows, WR_FIRST, range(1))
+        load_plane(sc2_win, tab2_scales[0].rearrange("(d r) t -> r d t", r=PACK), V2_FIRST, range(PACK))
+        load_plane(wr_sc_raw, wr_rows, WR_FIRST, range(1))
         load_w1(0)
-        load_plane(nc.sync, wr_sc_raw, wr_rows, WR_FIRST, range(1, PACK))
+        load_plane(wr_sc_raw, wr_rows, WR_FIRST, range(1, PACK))
         load_w1(1)
-        load_plane(nc.sync, wp_sc, wp_rows, 0, range(2))
+        load_plane(wp_sc, wp_rows, 0, range(2))
         load_words(tab[0], tab_words[0])
         gather(sc_picked[:], sc_win, lists, 0, S)
         place_scales(0)
         load_words(tab[1], tab_words[1])
         place_scales(1)
         load_wb(0)
-        load_plane(nc.sync, wp_sc, wp_rows, 0, range(2, PACK))
+        load_plane(wp_sc, wp_rows, 0, range(2, PACK))
         load_wp(0)
         load_wp(1)
         for g in range(1, PARTS):
             load_wb(g)
-        pick2(0)
-        pick2(1)
+
+        for h in range(2):
+            v2[h] = held("v2_%d" % h, [P, HALF], U32)
+            gather(v2[h][:], tab2, lists2, h * HALF, HALF)
         gather(v2_sc[:], sc2_win, lists2, 0, S)
-        order_wr()
-        round_w1(0, P)
+        nc.vector.tensor_copy(
+            wr_q[:].bitcast(I32).rearrange("p (t m) -> p t m", t=PACK),
+            wr_raw[:].bitcast(I32).rearrange("p (m t) -> p t m", t=PACK),
+        )
+        nc.vector.tensor_copy(
+            wr_sc[:].rearrange("p (t m) -> p t m", t=PACK),
+            wr_sc_raw[:].rearrange("p (m t) -> p t m", t=PACK),
+        )
+        round_w1(0, on_scalar)
         quantize_w1(0)
-        round_w1(1, 64)
-        reference_product(0, [0, 1, 2, 3], tag="w1_raw1")
+        round_w1(1, on_vector)
+        reference_product(0, 0, "w1_raw1")
         quantize_w1(1)
-        reference_product(1, [4, 5, 6, 7], tag="w1_bf1")
-        pick(0, 0, HALF)
-        pick(0, HALF, HALF)
-
-        h0 = [(0, HALF, n, 1) for n in range(TILES)]
-        h1 = [(HALF, HALF, n, 1) for n in range(TILES)]
-
-        def a_chunk(c, pair, index):
-            for a in range(PASSES):
-                a_pass(c, pair, a, index)
-
-        def x_both(unit, index):
-            x_pass(unit, 0, index)
-            x_pass(unit, 1)
-
-        def e_both(unit):
-            for inner in range(2):
-                e_pass(unit, unit[0] // CHUNK + inner)
+        reference_product(1, PACK, "w1_bf1")
+        for h in range(2):
+            v[0, h] = held("v0_%d" % h, [P, HALF], U32)
+            pick(0, h * HALF, HALF)
 
         for c in range(2):
             for pair in range(2):
-                a_pass(c, pair, 0, 2 * c + pair)
-        pick(1, 0, CHUNK)
-        pick(1, CHUNK, CHUNK)
+                a_ps[c, pair] = bank(2 * c + pair, [P, 2, CHUNK], "a_ps")
+                a_pass(c, pair, 0)
+        v[1, 0] = held("v1_0", [P, HALF], U32)
+        for c in range(2):
+            pick(1, c * CHUNK, CHUNK)
         round_wb(0, on_scalar)
         for c in range(2):
             for pair in range(2):
-                a_pass(c, pair, 1, 2 * c + pair)
+                a_pass(c, pair, 1)
+            resid[c] = held("resid%d" % c, [P, PACK, CHUNK], F32)
             for pair in range(2):
                 subtract(c, pair)
             bound(c)
         quantize_wb(0)
-        pick(1, HALF, HALF, tag="w1_raw1")
+        v[1, 1] = held("v1_1", [P, HALF], U32, tag="w1_raw1")
+        pick(1, HALF, HALF)
         for n in range(4):
-            x_both(h0[n], 4 + n)
-        for n in range(4, 6):
-            x_both(h0[n], n - 4)
-        for pair in range(2):
-            a_chunk(2, pair, 2 + pair)
-        weigh(0)
-        weigh(1)
-        quantize_z(0)
-        quantize_z(1)
+            calibrate(0, n, 4 + n)
+        for c in range(2, CHUNKS):
+            for pair in range(2):
+                a_product(c, pair, 2 * (c - 2) + pair)
+        for c in range(2):
+            weigh(c)
+        for c in range(2):
+            quantize_z(c)
         round_wb(1, on_scalar, tag="resid1")
         round_wb(2, on_scalar)
         round_wb(3, on_scalar)
         quantize_wb(1)
         for n in range(4):
-            e_both(h0[n])
-        subtract(2, 0)
-        subtract(2, 1)
-        bound(2)
+            correct(0, n)
+
+        finish(0, 0, on_scalar)
+        for c in range(2, CHUNKS):
+            resid[c] = held("resid%d" % c, [P, PACK, CHUNK], F32)
+            for pair in range(2):
+                subtract(c, pair)
+            bound(c)
         quantize_wb(2)
-        a_chunk(3, 0, 2)
-        e_both(h0[4])
-        e_both(h0[5])
-        a_chunk(3, 1, 3)
-        finish(h0[0], on_vector)
         quantize_wb(3)
-        finish(h0[1], on_scalar)
-        finish(h0[2], on_scalar)
-        subtract(3, 0)
-        subtract(3, 1)
-        bound(3)
-        x_both(h0[6], 4)
-        e_both(h0[6])
-        x_both(h0[7], 5)
-        e_both(h0[7])
+        finish(0, 1, on_vector)
+        for n in range(4, 6):
+            calibrate(0, n, n - 4)
+            correct(0, n)
         weigh(2)
-        finish(h0[3], on_vector)
-        quantize_z(2)
-        for n in range(4, 8):
-            finish(h0[n], on_scalar)
+        for n in range(6, TILES):
+            calibrate(0, n, n - 4)
+            correct(0, n)
+        for n in range(2, 6):
+            finish(0, n, on_scalar)
         weigh(3)
+        quantize_z(2)
         quantize_z(3)
-        order = [2, 3, 6, 7, 0, 1, 4, 5]
-        for n in range(5):
-            x_both(h1[n], order[n])
+        finish(0, 6, on_vector)
+        finish(0, 7, on_scalar)
+
         for n in range(TILES):
-            if n >= 5:
-                x_both(h1[n], order[n])
-            e_both(h1[n])
-            finish(h1[n], on_vector if n % 2 == 0 else on_scalar)
+            calibrate(1, n, (4 + n) % BANKS)
+            correct(1, n)
+            finish(1, n, on_vector if n % 2 == 0 else on_scalar)

@@ -253,11 +253,11 @@ def tile_list_wafer_drift_correction_kernel(
             v2[h] = held("v2_%d" % h, [P, HALF], U32)
             gather(v2[h][:], tab2, lists2, h * HALF, HALF)
         gather(v2_sc[:], sc2_win, lists2, 0, S)
-        nc.vector.tensor_copy(
+        nc.gpsimd.tensor_copy(
             wr_q[:].bitcast(I32).rearrange("p (t m) -> p t m", t=PACK),
             wr_raw[:].bitcast(I32).rearrange("p (m t) -> p t m", t=PACK),
         )
-        nc.vector.tensor_copy(
+        nc.gpsimd.tensor_copy(
             wr_sc[:].rearrange("p (t m) -> p t m", t=PACK),
             wr_sc_raw[:].rearrange("p (m t) -> p t m", t=PACK),
         )

@@ -26,6 +26,7 @@ LIST_ROWS = 16
 PAIR = 2
 PASSES, CHUNKS, PARTS, TILES = K // K_PASS, S // CHUNK, K // CHUNK, K // P
 BANKS = 8
+WB_LOADS = {0: CHUNK, 1: CHUNK, 2: HALF}
 V2_FIRST, WR_FIRST = 8, 12
 
 
@@ -38,6 +39,9 @@ def tile_list_wafer_drift_correction_kernel(
         keep = ctx.enter_context(tc.tile_pool(name="keep", bufs=1))
         psum = ctx.enter_context(tc.psum_pool(name="psum", bufs=1))
         on_scalar, on_vector = nc.scalar.copy, nc.vector.tensor_copy
+
+        def on_gpsimd(dst, src):
+            nc.gpsimd.tensor_scalar(dst, src, 1.0, 0.0, ALU.mult, ALU.add)
 
         def held(name, shape, dtype, tag=None):
             return keep.tile(shape, dtype, name=name, tag=tag or name, align_bytes=64)
@@ -58,8 +62,8 @@ def tile_list_wafer_drift_correction_kernel(
         tab = [held("tab%d" % a, [P, T], U32) for a in range(PASSES)]
         tab2 = held("tab2", [P, T], U32)
         wr_raw = held("wr_raw", [P, H], U32)
-        wp = [held("wp%d" % a, [P, 2 * K], U8) for a in range(PASSES)]
-        wb_raw = [held("wb_raw%d" % g, [P, PACK, CHUNK], F32) for g in range(PARTS)]
+        wp = held("wp", [P, PASSES, 2 * K], U8)
+        wb_raw = {g: held("wb_raw%d" % g, [P, PACK, width], F32) for g, width in WB_LOADS.items()}
         sc_picked = held("sc_picked", [P, S], U8)
         v2_sc = held("v2_sc", [P, S], U8)
         w1_bf = [held("w1_bf%d" % a, [P, PACK * H], BF16) for a in range(PASSES)]
@@ -87,11 +91,8 @@ def tile_list_wafer_drift_correction_kernel(
             rows = w1[a * K_PASS:(a + 1) * K_PASS, :]
             nc.sync.dma_start(out=w1_raw[a][:], in_=rows.rearrange("(p j) r -> p j r", j=PACK))
 
-        def load_wp(a):
-            nc.sync.dma_start(out=wp[a][:].bitcast(I32), in_=wp_words[a].bitcast(I32))
-
         def load_wb(g):
-            cols = wb[:, g * CHUNK:(g + 1) * CHUNK]
+            cols = wb[:, g * CHUNK:g * CHUNK + WB_LOADS[g]]
             nc.sync.dma_start(out=wb_raw[g][:], in_=cols.rearrange("(p j) n -> p j n", j=PACK))
 
         def place_scales(a):
@@ -111,31 +112,41 @@ def tile_list_wafer_drift_correction_kernel(
         def pick(a, entry, count):
             gather(picked(a, entry, count), tab[a], lists, entry, count)
 
-        def round_w1(a, upper):
+        def round_w1(a, lower, upper):
             dst = w1_bf[a][:].rearrange("p (t m j) -> p m j t", t=PACK, j=PACK)
             src = w1_raw[a][:].rearrange("p j (m t) -> p m j t", t=PACK)
-            on_scalar(dst[:, :, :, 0:PAIR], src[:, :, :, 0:PAIR])
+            lower(dst[:, :, :, 0:PAIR], src[:, :, :, 0:PAIR])
             upper(dst[:, :, :, PAIR:PACK], src[:, :, :, PAIR:PACK])
 
         def quantize_w1(a):
             nc.vector.quantize_mx(out=w1_q[a][:].bitcast(FP8X4), scales=w1_sc[a][:], in_=w1_bf[a][:])
 
+        def wb_part(g):
+            first = min(g, 2)
+            return wb_raw[first][:, :, (g - first) * CHUNK:(g - first + 1) * CHUNK]
+
         def round_wb(g, copy, tag=None):
             wb_bf[g] = held("wb_bf%d" % g, [P, CHUNK, PACK], BF16, tag=tag)
             copy(
                 wb_bf[g][:].rearrange("p (g i) j -> p g j i", i=PAIR),
-                wb_raw[g][:].rearrange("p j (g i) -> p g j i", i=PAIR),
+                wb_part(g).rearrange("p j (g i) -> p g j i", i=PAIR),
             )
+
+        def round_wb_gpsimd(g, tag=None):
+            wb_bf[g] = held("wb_bf%d" % g, [P, CHUNK, PACK], BF16, tag=tag)
+            on_gpsimd(wb_bf[g][:], wb_part(g).rearrange("p j n -> p n j"))
 
         def quantize_wb(g):
             nc.vector.quantize_mx(
                 out=wb_q[g][:].bitcast(FP8X4), scales=wb_sc[g][:], in_=wb_bf[g][:].rearrange("p n j -> p (n j)"),
             )
 
-        def reference_product(h, first_bank, tag):
-            rho_b[h] = held("rho_b%d" % h, [P, 2, PACK, CHUNK], F32, tag=tag)
+        def reference_product(h, tags):
             for t in range(PACK):
-                b_ps = bank(first_bank + t, [P, HALF], "b_ps")
+                pair, u = divmod(t, 2)
+                if u == 0:
+                    rho_b[h, pair] = held("rho_b%d_%d" % (h, pair), [P, 2, 2, CHUNK], F32, tag=tags[pair])
+                b_ps = bank(PACK * h + t, [P, HALF], "b_ps")
                 rows = slice(t * P, (t + 1) * P)
                 nc.tensor.matmul_mx(
                     out=b_ps[:], lhsT=wr_q[:, rows].bitcast(FP8X4), lhsT_scale=wr_sc[WR_FIRST:P, rows],
@@ -143,7 +154,7 @@ def tile_list_wafer_drift_correction_kernel(
                     start=True, stop=True,
                 )
                 nc.scalar.activation(
-                    rho_b[h][:, :, t, :], b_ps[:].rearrange("p (c j) -> p c j", c=2),
+                    rho_b[h, pair][:, :, u, :], b_ps[:].rearrange("p (c j) -> p c j", c=2),
                     ACT.Copy, scale=rho_t[:, t:t + 1],
                 )
 
@@ -163,9 +174,8 @@ def tile_list_wafer_drift_correction_kernel(
                 a_pass(c, pair, a)
 
         def subtract(c, pair):
-            h, inner = divmod(c, 2)
             two = slice(2 * pair, 2 * pair + 2)
-            nc.vector.tensor_tensor(resid[c][:, two, :], rho_b[h][:, inner, two, :], a_ps[c, pair][:], ALU.subtract)
+            nc.vector.tensor_tensor(resid[c][:, two, :], rho_b[c // 2, pair][:, c % 2], a_ps[c, pair][:], ALU.subtract)
 
         def bound(c):
             bounded[c] = held("bounded%d" % c, [P, CHUNK, PACK], F32)
@@ -175,8 +185,8 @@ def tile_list_wafer_drift_correction_kernel(
                 ACT.Tanh,
             )
 
-        def weigh(c):
-            z_bf[c] = held("z_bf%d" % c, [P, CHUNK, PACK], BF16)
+        def weigh(c, tag=None):
+            z_bf[c] = held("z_bf%d" % c, [P, CHUNK, PACK], BF16, tag=tag)
             nc.vector.tensor_tensor(
                 z_bf[c][:], bounded[c][:], gain_t[:].unsqueeze(1).to_broadcast([P, CHUNK, PACK]), ALU.mult,
             )
@@ -186,11 +196,11 @@ def tile_list_wafer_drift_correction_kernel(
                 out=z_q[c][:].bitcast(FP8X4), scales=z_sc[c][:], in_=z_bf[c][:].rearrange("p j t -> p (j t)"),
             )
 
-        def calibrate(h, n, index):
-            o_ps[h, n] = bank(index, [P, HALF], "o_ps")
+        def calibrate(h, n):
+            o_ps[h, n] = bank((4 + n) % BANKS, [P, HALF], "o_ps")
             for a in range(PASSES):
                 nc.tensor.matmul_mx(
-                    out=o_ps[h, n][:], lhsT=wp[a][:, 2 * n * P:2 * (n + 1) * P].bitcast(FP4X4),
+                    out=o_ps[h, n][:], lhsT=wp[:, a, 2 * n * P:2 * (n + 1) * P].bitcast(FP4X4),
                     lhsT_scale=wp_sc[:, a, n * P:(n + 1) * P],
                     rhs=picked(a, h * HALF, HALF).bitcast(FP8X4), rhs_scale=v_sc[a][:, h * HALF:(h + 1) * HALF],
                     start=(a == 0), stop=False,
@@ -212,47 +222,66 @@ def tile_list_wafer_drift_correction_kernel(
             copy(result[:], o_ps[h, n][:])
             nc.sync.dma_start(out=out[n * P:(n + 1) * P, h * HALF:(h + 1) * HALF], in_=result[:])
 
+        def finish_pair(h, n):
+            result = held("result%d_%d" % (h, n), [P, 2, HALF], F32)
+            on_vector(result[:, 0, :], o_ps[h, n][:])
+            on_scalar(result[:, 1, :], o_ps[h, n + 1][:])
+            rows = out[n * P:(n + 2) * P, h * HALF:(h + 1) * HALF]
+            nc.sync.dma_start(out=rows.rearrange("(u p) j -> p u j", u=2), in_=result[:])
+
+        def residual(c):
+            for pair in range(2):
+                subtract(c, pair)
+
+        def a_first(c):
+            for pair in range(2):
+                a_ps[c, pair] = bank((2 * c + pair) % 4, [P, 2, CHUNK], "a_ps")
+                a_pass(c, pair, 0)
+
+        def a_second(c):
+            for pair in range(2):
+                a_pass(c, pair, 1)
+
         nc.gpsimd.memset(sc_win[:].bitcast(I32), 0)
         nc.vector.memset(sc2_win[:].bitcast(I32), 0)
         nc.vector.memset(wr_sc_raw[:].bitcast(I32), 0)
-        nc.vector.memset(wp_sc[:].bitcast(I32), 0)
         for a in range(PASSES):
             nc.vector.memset(v_sc[a][:].bitcast(I32), 0)
+        nc.vector.memset(wp_sc[:].bitcast(I32), 0)
 
         wr_rows = wr_scales[0].rearrange("(d r) c -> r d c", r=PACK)
         wp_rows = wp_scales.rearrange("a (d r) c -> r d a c", r=PACK)
         nc.sync.dma_start(lists[:], offs)
         load_words(wr_raw, wr_words[0])
         load_by_slice(rho_t, rho)
-        load_by_slice(gain_t, gain)
         nc.sync.dma_start(lists2[:], offs2)
         nc.sync.dma_start(
             out=sc_win[:].bitcast(I32)[0:P:4, :],
             in_=tab_scales.rearrange("a q t -> q a t").bitcast(I32),
         )
+        load_plane(sc2_win, tab2_scales[0].rearrange("(d r) t -> r d t", r=PACK), V2_FIRST, range(2))
         load_words(tab2, tab2_words[0])
-        load_plane(sc2_win, tab2_scales[0].rearrange("(d r) t -> r d t", r=PACK), V2_FIRST, range(PACK))
-        load_plane(wr_sc_raw, wr_rows, WR_FIRST, range(1))
+        load_plane(sc2_win, tab2_scales[0].rearrange("(d r) t -> r d t", r=PACK), V2_FIRST, range(2, PACK))
+        load_plane(wr_sc_raw, wr_rows, WR_FIRST, range(2))
         load_w1(0)
-        load_plane(wr_sc_raw, wr_rows, WR_FIRST, range(1, PACK))
+        load_plane(wr_sc_raw, wr_rows, WR_FIRST, range(2, PACK))
         load_w1(1)
-        load_plane(wp_sc, wp_rows, 0, range(2))
         load_words(tab[0], tab_words[0])
         gather(sc_picked[:], sc_win, lists, 0, S)
         place_scales(0)
         load_words(tab[1], tab_words[1])
         place_scales(1)
         load_wb(0)
-        load_plane(wp_sc, wp_rows, 0, range(2, PACK))
-        load_wp(0)
-        load_wp(1)
-        for g in range(1, PARTS):
-            load_wb(g)
+        load_by_slice(gain_t, gain)
+        nc.sync.dma_start(out=wp[:].bitcast(I32), in_=wp_words.rearrange("a p c -> p a c").bitcast(I32))
+        load_plane(wp_sc, wp_rows, 0, range(PACK))
+        load_wb(1)
+        load_wb(2)
 
+        gather(v2_sc[:], sc2_win, lists2, 0, S)
         for h in range(2):
             v2[h] = held("v2_%d" % h, [P, HALF], U32)
             gather(v2[h][:], tab2, lists2, h * HALF, HALF)
-        gather(v2_sc[:], sc2_win, lists2, 0, S)
         nc.gpsimd.tensor_copy(
             wr_q[:].bitcast(I32).rearrange("p (t m) -> p t m", t=PACK),
             wr_raw[:].bitcast(I32).rearrange("p (m t) -> p t m", t=PACK),
@@ -261,75 +290,82 @@ def tile_list_wafer_drift_correction_kernel(
             wr_sc[:].rearrange("p (t m) -> p t m", t=PACK),
             wr_sc_raw[:].rearrange("p (m t) -> p t m", t=PACK),
         )
-        round_w1(0, on_scalar)
+        round_w1(0, on_scalar, on_scalar)
         quantize_w1(0)
-        round_w1(1, on_vector)
-        reference_product(0, 0, "w1_raw1")
+        round_w1(1, on_scalar, on_vector)
         quantize_w1(1)
-        reference_product(1, PACK, "w1_bf1")
+        reference_product(0, ("w1_raw1", "w1_raw0"))
+        reference_product(1, ("w1_bf1", "w1_bf0"))
         for h in range(2):
             v[0, h] = held("v0_%d" % h, [P, HALF], U32)
             pick(0, h * HALF, HALF)
-
         for c in range(2):
-            for pair in range(2):
-                a_ps[c, pair] = bank(2 * c + pair, [P, 2, CHUNK], "a_ps")
-                a_pass(c, pair, 0)
+            a_first(c)
+
         v[1, 0] = held("v1_0", [P, HALF], U32)
         for c in range(2):
             pick(1, c * CHUNK, CHUNK)
-        round_wb(0, on_scalar)
+            a_second(c)
         for c in range(2):
-            for pair in range(2):
-                a_pass(c, pair, 1)
             resid[c] = held("resid%d" % c, [P, PACK, CHUNK], F32)
-            for pair in range(2):
-                subtract(c, pair)
+            residual(c)
             bound(c)
-        quantize_wb(0)
+        round_wb_gpsimd(0)
         v[1, 1] = held("v1_1", [P, HALF], U32, tag="w1_raw1")
         pick(1, HALF, HALF)
-        for n in range(4):
-            calibrate(0, n, 4 + n)
         for c in range(2, CHUNKS):
-            for pair in range(2):
-                a_product(c, pair, 2 * (c - 2) + pair)
-        for c in range(2):
-            weigh(c)
-        for c in range(2):
-            quantize_z(c)
+            a_first(c)
+        for n in range(4):
+            calibrate(0, n)
+        a_second(2)
+        a_second(3)
         round_wb(1, on_scalar, tag="resid1")
-        round_wb(2, on_scalar)
-        round_wb(3, on_scalar)
+        weigh(0)
+        quantize_wb(0)
+        weigh(1)
+        quantize_z(0)
+        quantize_z(1)
         quantize_wb(1)
+        late = held("late", [P, 2 * PACK * CHUNK + 2 * CHUNK], F32, tag="resid1")
+        wb_bf[2] = late[:, 2 * PACK * CHUNK:].bitcast(BF16).rearrange("p (n j) -> p n j", j=PACK)
+        on_gpsimd(wb_bf[2], wb_part(2).rearrange("p j n -> p n j"))
         for n in range(4):
             correct(0, n)
-
-        finish(0, 0, on_scalar)
         for c in range(2, CHUNKS):
-            resid[c] = held("resid%d" % c, [P, PACK, CHUNK], F32)
-            for pair in range(2):
-                subtract(c, pair)
-            bound(c)
+            resid[c] = late[:, (c - 2) * PACK * CHUNK:(c - 1) * PACK * CHUNK].rearrange("p (t j) -> p t j", t=PACK)
+        residual(2)
+        finish(0, 0, on_scalar)
+        finish(0, 1, on_scalar)
+        bound(2)
+
+        residual(3)
+        round_wb(3, on_vector, tag="w1_bf1")
         quantize_wb(2)
         quantize_wb(3)
-        finish(0, 1, on_vector)
-        for n in range(4, 6):
-            calibrate(0, n, n - 4)
+        calibrate(0, 4)
+        calibrate(0, 5)
+        calibrate(1, 0)
+        finish(0, 2, on_scalar)
+        bound(3)
+        calibrate(0, 6)
+        calibrate(0, 7)
+        for n in range(4, TILES):
             correct(0, n)
         weigh(2)
-        for n in range(6, TILES):
-            calibrate(0, n, n - 4)
-            correct(0, n)
-        for n in range(2, 6):
-            finish(0, n, on_scalar)
         weigh(3)
         quantize_z(2)
         quantize_z(3)
-        finish(0, 6, on_vector)
-        finish(0, 7, on_scalar)
-
-        for n in range(TILES):
-            calibrate(1, n, (4 + n) % BANKS)
+        for n in range(3, TILES):
+            finish(0, n, on_scalar)
+        for n in range(1, 4):
+            calibrate(1, n)
+        for n in range(4):
             correct(1, n)
-            finish(1, n, on_vector if n % 2 == 0 else on_scalar)
+        finish_pair(1, 0)
+        finish_pair(1, 2)
+        for n in range(4, TILES):
+            calibrate(1, n)
+            correct(1, n)
+        finish_pair(1, 4)
+        finish(1, 6, on_vector)
+        finish(1, 7, on_scalar)

@@ -62,7 +62,7 @@ def tile_list_wafer_drift_correction_kernel(
         tab = [held("tab%d" % a, [P, T], U32) for a in range(PASSES)]
         tab2 = held("tab2", [P, T], U32)
         wr_raw = held("wr_raw", [P, H], U32)
-        wp = held("wp", [P, PASSES, 2 * K], U8)
+        wp = [held("wp%d" % a, [P, 2 * K], U8) for a in range(PASSES)]
         wb_raw = {g: held("wb_raw%d" % g, [P, PACK, width], F32) for g, width in WB_LOADS.items()}
         sc_picked = held("sc_picked", [P, S], U8)
         v2_sc = held("v2_sc", [P, S], U8)
@@ -71,11 +71,10 @@ def tile_list_wafer_drift_correction_kernel(
         w1_sc = [held("w1_sc%d" % a, [P, H], U8) for a in range(PASSES)]
         wr_q = held("wr_q", [P, H], U32)
         wr_sc = held("wr_sc", [P, H], U8)
-        z_q = [held("z_q%d" % c, [P, CHUNK], U32) for c in range(CHUNKS)]
-        z_sc = [held("z_sc%d" % c, [P, CHUNK], U8) for c in range(CHUNKS)]
-        wb_q = [held("wb_q%d" % g, [P, CHUNK], U32) for g in range(PARTS)]
+        z_sc = [held("z_sc%d" % h, [P, HALF], U8) for h in range(2)]
         wb_sc = [held("wb_sc%d" % g, [P, CHUNK], U8) for g in range(PARTS)]
         v, v2, rho_b, a_ps, resid, bounded, z_bf, wb_bf, o_ps = {}, {}, {}, {}, {}, {}, {}, {}, {}
+        aside, z_q, wb_q = {}, {}, {}
 
         def load_words(tile, packed):
             nc.sync.dma_start(out=tile[:].bitcast(I32), in_=packed.rearrange("p c i -> p (c i)").bitcast(I32))
@@ -90,6 +89,9 @@ def tile_list_wafer_drift_correction_kernel(
         def load_w1(a):
             rows = w1[a * K_PASS:(a + 1) * K_PASS, :]
             nc.sync.dma_start(out=w1_raw[a][:], in_=rows.rearrange("(p j) r -> p j r", j=PACK))
+
+        def load_wp(a):
+            nc.sync.dma_start(out=wp[a][:].bitcast(I32), in_=wp_words[a].bitcast(I32))
 
         def load_wb(g):
             cols = wb[:, g * CHUNK:g * CHUNK + WB_LOADS[g]]
@@ -136,16 +138,15 @@ def tile_list_wafer_drift_correction_kernel(
             wb_bf[g] = held("wb_bf%d" % g, [P, CHUNK, PACK], BF16, tag=tag)
             on_gpsimd(wb_bf[g][:], wb_part(g).rearrange("p j n -> p n j"))
 
-        def quantize_wb(g):
+        def quantize_wb(g, tag=None):
+            wb_q[g] = held("wb_q%d" % g, [P, CHUNK], U32, tag=tag)
             nc.vector.quantize_mx(
                 out=wb_q[g][:].bitcast(FP8X4), scales=wb_sc[g][:], in_=wb_bf[g][:].rearrange("p n j -> p (n j)"),
             )
 
-        def reference_product(h, tags):
-            for t in range(PACK):
+        def reference_product(h, slices, tags):
+            for t in slices:
                 pair, u = divmod(t, 2)
-                if u == 0:
-                    rho_b[h, pair] = held("rho_b%d_%d" % (h, pair), [P, 2, 2, CHUNK], F32, tag=tags[pair])
                 b_ps = bank(PACK * h + t, [P, HALF], "b_ps")
                 rows = slice(t * P, (t + 1) * P)
                 nc.tensor.matmul_mx(
@@ -153,29 +154,36 @@ def tile_list_wafer_drift_correction_kernel(
                     rhs=v2[h][:].bitcast(FP8X4), rhs_scale=v2_sc[V2_FIRST:P, h * HALF:(h + 1) * HALF],
                     start=True, stop=True,
                 )
-                nc.scalar.activation(
-                    rho_b[h, pair][:, :, u, :], b_ps[:].rearrange("p (c j) -> p c j", c=2),
-                    ACT.Copy, scale=rho_t[:, t:t + 1],
-                )
+                if (h, pair) == (0, 0):
+                    for c in range(2):
+                        if u == 0:
+                            rho_b[c, pair] = held("rho_b%d_0" % c, [P, 2, CHUNK], F32)
+                        nc.scalar.activation(
+                            rho_b[c, pair][:, u, :], b_ps[:, c * CHUNK:(c + 1) * CHUNK],
+                            ACT.Copy, scale=rho_t[:, t:t + 1],
+                        )
+                else:
+                    if u == 0:
+                        both = held("rho_b_half%d_%d" % (h, pair), [P, 2, 2, CHUNK], F32, tag=tags[pair])
+                        for c in range(2):
+                            rho_b[2 * h + c, pair] = both[:, c]
+                    nc.scalar.activation(
+                        both[:, :, u, :], b_ps[:].rearrange("p (c j) -> p c j", c=2), ACT.Copy, scale=rho_t[:, t:t + 1],
+                    )
 
-        def a_pass(c, pair, a):
+        def a_pass(c, pair, a, opens):
             for u in range(2):
                 rows = slice((2 * pair + u) * P, (2 * pair + u + 1) * P)
                 nc.tensor.matmul_mx(
                     out=a_ps[c, pair][:, u, :], lhsT=w1_q[a][:, rows].bitcast(FP8X4), lhsT_scale=w1_sc[a][:, rows],
                     rhs=picked(a, c * CHUNK, CHUNK).bitcast(FP8X4),
                     rhs_scale=v_sc[a][:, c * CHUNK:(c + 1) * CHUNK],
-                    start=(a == 0 and u == 0), stop=(a == PASSES - 1 and u == 1),
+                    start=(opens and u == 0), stop=(not opens and u == 1),
                 )
-
-        def a_product(c, pair, index):
-            a_ps[c, pair] = bank(index, [P, 2, CHUNK], "a_ps")
-            for a in range(PASSES):
-                a_pass(c, pair, a)
 
         def subtract(c, pair):
             two = slice(2 * pair, 2 * pair + 2)
-            nc.vector.tensor_tensor(resid[c][:, two, :], rho_b[c // 2, pair][:, c % 2], a_ps[c, pair][:], ALU.subtract)
+            nc.vector.tensor_tensor(resid[c][:, two, :], rho_b[c, pair][:], a_ps[c, pair][:], ALU.subtract)
 
         def bound(c):
             bounded[c] = held("bounded%d" % c, [P, CHUNK, PACK], F32)
@@ -185,46 +193,55 @@ def tile_list_wafer_drift_correction_kernel(
                 ACT.Tanh,
             )
 
-        def weigh(c, tag=None):
+        def weigh(c, engine, tag=None):
             z_bf[c] = held("z_bf%d" % c, [P, CHUNK, PACK], BF16, tag=tag)
-            nc.vector.tensor_tensor(
+            engine.tensor_tensor(
                 z_bf[c][:], bounded[c][:], gain_t[:].unsqueeze(1).to_broadcast([P, CHUNK, PACK]), ALU.mult,
             )
 
-        def quantize_z(c):
+        def quantize_z(c, tag=None):
+            if c % 2 == 0:
+                z_q[c // 2] = held("z_q%d" % (c // 2), [P, HALF], U32, tag=tag)
+            cols = slice((c % 2) * CHUNK, (c % 2 + 1) * CHUNK)
             nc.vector.quantize_mx(
-                out=z_q[c][:].bitcast(FP8X4), scales=z_sc[c][:], in_=z_bf[c][:].rearrange("p j t -> p (j t)"),
+                out=z_q[c // 2][:, cols].bitcast(FP8X4), scales=z_sc[c // 2][:, cols],
+                in_=z_bf[c][:].rearrange("p j t -> p (j t)"),
             )
 
-        def calibrate(h, n):
-            o_ps[h, n] = bank((4 + n) % BANKS, [P, HALF], "o_ps")
+        def calibrate(h, n, index, closes=False):
+            o_ps[h, n] = bank(index, [P, HALF], "o_ps")
             for a in range(PASSES):
                 nc.tensor.matmul_mx(
-                    out=o_ps[h, n][:], lhsT=wp[:, a, 2 * n * P:2 * (n + 1) * P].bitcast(FP4X4),
+                    out=o_ps[h, n][:], lhsT=wp[a][:, 2 * n * P:2 * (n + 1) * P].bitcast(FP4X4),
                     lhsT_scale=wp_sc[:, a, n * P:(n + 1) * P],
                     rhs=picked(a, h * HALF, HALF).bitcast(FP8X4), rhs_scale=v_sc[a][:, h * HALF:(h + 1) * HALF],
-                    start=(a == 0), stop=False,
+                    start=(a == 0), stop=(closes and a == PASSES - 1),
                 )
 
-        def correct(h, n):
+        def correct(h, n, opens=False):
             g, rows = n // 2, slice((n % 2) * P, (n % 2 + 1) * P)
-            for inner in range(2):
-                c = 2 * h + inner
-                nc.tensor.matmul_mx(
-                    out=o_ps[h, n][:, inner * CHUNK:(inner + 1) * CHUNK],
-                    lhsT=wb_q[g][:, rows].bitcast(FP8X4), lhsT_scale=wb_sc[g][:, rows],
-                    rhs=z_q[c][:].bitcast(FP8X4), rhs_scale=z_sc[c][:],
-                    start=False, stop=(inner == 1),
-                )
+            nc.tensor.matmul_mx(
+                out=o_ps[h, n][:], lhsT=wb_q[g][:, rows].bitcast(FP8X4), lhsT_scale=wb_sc[g][:, rows],
+                rhs=z_q[h][:].bitcast(FP8X4), rhs_scale=z_sc[h][:], start=opens, stop=True,
+            )
 
         def finish(h, n, copy):
             result = held("result%d_%d" % (h, n), [P, HALF], F32)
             copy(result[:], o_ps[h, n][:])
             nc.sync.dma_start(out=out[n * P:(n + 1) * P, h * HALF:(h + 1) * HALF], in_=result[:])
 
-        def finish_pair(h, n):
+        def finish_last(h, n, copy):
+            for u in range(2):
+                cols = slice(u * CHUNK, (u + 1) * CHUNK)
+                result = held("result%d_%d_%d" % (h, n, u), [P, CHUNK], F32)
+                copy(result[:], o_ps[h, n][:, cols])
+                nc.sync.dma_start(
+                    out=out[n * P:(n + 1) * P, h * HALF + u * CHUNK:h * HALF + (u + 1) * CHUNK], in_=result[:],
+                )
+
+        def finish_pair(h, n, first):
             result = held("result%d_%d" % (h, n), [P, 2, HALF], F32)
-            on_vector(result[:, 0, :], o_ps[h, n][:])
+            first(result[:, 0, :], o_ps[h, n][:])
             on_scalar(result[:, 1, :], o_ps[h, n + 1][:])
             rows = out[n * P:(n + 2) * P, h * HALF:(h + 1) * HALF]
             nc.sync.dma_start(out=rows.rearrange("(u p) j -> p u j", u=2), in_=result[:])
@@ -233,14 +250,26 @@ def tile_list_wafer_drift_correction_kernel(
             for pair in range(2):
                 subtract(c, pair)
 
-        def a_first(c):
+        def a_first(c, a, index):
             for pair in range(2):
-                a_ps[c, pair] = bank((2 * c + pair) % 4, [P, 2, CHUNK], "a_ps")
-                a_pass(c, pair, 0)
+                a_ps[c, pair] = bank(index + pair, [P, 2, CHUNK], "a_ps")
+                a_pass(c, pair, a, True)
 
-        def a_second(c):
+        def a_second(c, a):
             for pair in range(2):
-                a_pass(c, pair, 1)
+                a_pass(c, pair, a, False)
+
+        def set_aside(n, index):
+            calibrate(1, n, index, True)
+            aside[n] = held("aside%d" % n, [P, HALF], F32)
+            on_scalar(aside[n][:], o_ps[1, n][:])
+
+        def finish_aside(n, index):
+            o_ps[1, n] = bank(index, [P, HALF], "o_ps")
+            correct(1, n, True)
+            result = held("result1_%d" % n, [P, HALF], F32)
+            nc.vector.tensor_tensor(result[:], o_ps[1, n][:], aside[n][:], ALU.add)
+            nc.sync.dma_start(out=out[n * P:(n + 1) * P, HALF:S], in_=result[:])
 
         nc.gpsimd.memset(sc_win[:].bitcast(I32), 0)
         nc.vector.memset(sc2_win[:].bitcast(I32), 0)
@@ -272,10 +301,11 @@ def tile_list_wafer_drift_correction_kernel(
         load_words(tab[1], tab_words[1])
         place_scales(1)
         load_wb(0)
-        load_by_slice(gain_t, gain)
-        nc.sync.dma_start(out=wp[:].bitcast(I32), in_=wp_words.rearrange("a p c -> p a c").bitcast(I32))
-        load_plane(wp_sc, wp_rows, 0, range(PACK))
         load_wb(1)
+        load_by_slice(gain_t, gain)
+        load_wp(0)
+        load_plane(wp_sc, wp_rows, 0, range(PACK))
+        load_wp(1)
         load_wb(2)
 
         gather(v2_sc[:], sc2_win, lists2, 0, S)
@@ -294,78 +324,70 @@ def tile_list_wafer_drift_correction_kernel(
         quantize_w1(0)
         round_w1(1, on_scalar, on_vector)
         quantize_w1(1)
-        reference_product(0, ("w1_raw1", "w1_raw0"))
-        reference_product(1, ("w1_bf1", "w1_bf0"))
+        reference_product(0, range(2), None)
+        reference_product(1, range(PACK), ("w1_raw1", "w1_raw0"))
+        reference_product(0, range(2, PACK), (None, "w1_bf1"))
         for h in range(2):
             v[0, h] = held("v0_%d" % h, [P, HALF], U32)
             pick(0, h * HALF, HALF)
-        for c in range(2):
-            a_first(c)
+        for c in (0, 2, 3):
+            a_first(c, 0, 2 * c)
 
         v[1, 0] = held("v1_0", [P, HALF], U32)
         for c in range(2):
             pick(1, c * CHUNK, CHUNK)
-            a_second(c)
-        for c in range(2):
+        a_second(0, 1)
+        a_first(1, 1, 2)
+        a_second(1, 0)
+        for c in range(CHUNKS):
             resid[c] = held("resid%d" % c, [P, PACK, CHUNK], F32)
+        round_wb_gpsimd(0)
+        residual(0)
+        bound(0)
+        weigh(0, nc.gpsimd, tag="wb_raw0")
+        round_wb(1, on_scalar, tag="resid0")
+        v[1, 1] = held("v1_1", [P, HALF], U32, tag="rho_b0_0")
+        for c in range(2, CHUNKS):
+            pick(1, c * CHUNK, CHUNK)
+            a_second(c, 1)
+        for c in range(1, CHUNKS):
             residual(c)
             bound(c)
-        round_wb_gpsimd(0)
-        v[1, 1] = held("v1_1", [P, HALF], U32, tag="w1_raw1")
-        pick(1, HALF, HALF)
-        for c in range(2, CHUNKS):
-            a_first(c)
-        for n in range(4):
-            calibrate(0, n)
-        a_second(2)
-        a_second(3)
-        round_wb(1, on_scalar, tag="resid1")
-        weigh(0)
-        quantize_wb(0)
-        weigh(1)
-        quantize_z(0)
+        for n in range(TILES):
+            calibrate(0, n, n)
+        quantize_wb(0, tag="w1_raw1")
+        weigh(1, nc.vector)
+        quantize_z(0, tag="w1_raw0")
         quantize_z(1)
-        quantize_wb(1)
-        late = held("late", [P, 2 * PACK * CHUNK + 2 * CHUNK], F32, tag="resid1")
-        wb_bf[2] = late[:, 2 * PACK * CHUNK:].bitcast(BF16).rearrange("p (n j) -> p n j", j=PACK)
-        on_gpsimd(wb_bf[2], wb_part(2).rearrange("p j n -> p n j"))
+        quantize_wb(1, tag="bounded1")
+        round_wb(2, on_vector, tag="z_bf1")
+        quantize_wb(2)
+        round_wb(3, on_vector, tag="resid0")
         for n in range(4):
             correct(0, n)
-        for c in range(2, CHUNKS):
-            resid[c] = late[:, (c - 2) * PACK * CHUNK:(c - 1) * PACK * CHUNK].rearrange("p (t j) -> p t j", t=PACK)
-        residual(2)
-        finish(0, 0, on_scalar)
-        finish(0, 1, on_scalar)
-        bound(2)
-
-        residual(3)
-        round_wb(3, on_vector, tag="w1_bf1")
-        quantize_wb(2)
+            finish(0, n, on_scalar)
         quantize_wb(3)
-        calibrate(0, 4)
-        calibrate(0, 5)
-        calibrate(1, 0)
-        finish(0, 2, on_scalar)
-        bound(3)
-        calibrate(0, 6)
-        calibrate(0, 7)
-        for n in range(4, TILES):
+        weigh(2, nc.vector, tag="z_bf1")
+        calibrate(1, 0, 0)
+        for n in range(4, 6):
             correct(0, n)
-        weigh(2)
-        weigh(3)
+        calibrate(1, 1, 1)
+        for n in range(6, TILES):
+            correct(0, n)
+        weigh(3, nc.vector, tag="resid0")
         quantize_z(2)
         quantize_z(3)
-        for n in range(3, TILES):
-            finish(0, n, on_scalar)
-        for n in range(1, 4):
-            calibrate(1, n)
+        for n in range(4, TILES, 2):
+            finish_pair(0, n, on_scalar)
+        for n in range(2, 4):
+            calibrate(1, n, n)
         for n in range(4):
             correct(1, n)
-        finish_pair(1, 0)
-        finish_pair(1, 2)
+        finish_pair(1, 0, on_vector)
+        finish_pair(1, 2, on_vector)
         for n in range(4, TILES):
-            calibrate(1, n)
+            calibrate(1, n, n)
             correct(1, n)
-        finish_pair(1, 4)
+        finish_pair(1, 4, on_vector)
         finish(1, 6, on_vector)
         finish(1, 7, on_scalar)

@@ -25,7 +25,7 @@ CHUNK = 256
 LIST_ROWS = 16
 PAIR = 2
 PASSES, CHUNKS, PARTS, TILES = K // K_PASS, S // CHUNK, K // CHUNK, K // P
-BANKS = 8
+FREED = (6, 7, 2, 3, 4, 5, 0, 1)
 WB_LOADS = {0: CHUNK, 1: CHUNK, 2: HALF}
 V2_FIRST, WR_FIRST = 8, 12
 
@@ -330,7 +330,7 @@ def tile_list_wafer_drift_correction_kernel(
         for h in range(2):
             v[0, h] = held("v0_%d" % h, [P, HALF], U32)
             pick(0, h * HALF, HALF)
-        for c in (0, 2, 3):
+        for c in (0, 2):
             a_first(c, 0, 2 * c)
 
         v[1, 0] = held("v1_0", [P, HALF], U32)
@@ -343,6 +343,7 @@ def tile_list_wafer_drift_correction_kernel(
             resid[c] = held("resid%d" % c, [P, PACK, CHUNK], F32)
         round_wb_gpsimd(0)
         residual(0)
+        a_first(3, 0, 0)
         bound(0)
         weigh(0, nc.gpsimd, tag="wb_raw0")
         round_wb(1, on_scalar, tag="resid0")
@@ -354,7 +355,7 @@ def tile_list_wafer_drift_correction_kernel(
             residual(c)
             bound(c)
         for n in range(TILES):
-            calibrate(0, n, n)
+            calibrate(0, n, FREED[n])
         quantize_wb(0, tag="w1_raw1")
         weigh(1, nc.vector)
         quantize_z(0, tag="w1_raw0")
@@ -368,10 +369,10 @@ def tile_list_wafer_drift_correction_kernel(
             finish(0, n, on_scalar)
         quantize_wb(3)
         weigh(2, nc.vector, tag="z_bf1")
-        calibrate(1, 0, 0)
+        calibrate(1, 0, FREED[0])
         for n in range(4, 6):
             correct(0, n)
-        calibrate(1, 1, 1)
+        calibrate(1, 1, FREED[1])
         for n in range(6, TILES):
             correct(0, n)
         weigh(3, nc.vector, tag="resid0")
@@ -380,13 +381,13 @@ def tile_list_wafer_drift_correction_kernel(
         for n in range(4, TILES, 2):
             finish_pair(0, n, on_scalar)
         for n in range(2, 4):
-            calibrate(1, n, n)
+            calibrate(1, n, FREED[n])
         for n in range(4):
             correct(1, n)
         finish_pair(1, 0, on_vector)
         finish_pair(1, 2, on_vector)
         for n in range(4, TILES):
-            calibrate(1, n, n)
+            calibrate(1, n, FREED[n])
             correct(1, n)
         finish_pair(1, 4, on_vector)
         finish(1, 6, on_vector)

@@ -44,7 +44,7 @@ def tile_list_wafer_drift_correction_kernel(
             nc.gpsimd.tensor_scalar(dst, src, 1.0, 0.0, ALU.mult, ALU.add)
 
         def held(name, shape, dtype, tag=None):
-            return keep.tile(shape, dtype, name=name, tag=tag or name, align_bytes=64)
+            return keep.tile(shape, dtype, name=name, tag=tag or name, align_bytes=256)
 
         def bank(index, shape, name):
             return psum.tile(shape, F32, name=name, tag="bank%d" % index)

@@ -66,7 +66,7 @@ def tile_list_wafer_drift_correction_kernel(
         wb_raw = {g: held("wb_raw%d" % g, [P, PACK, width], F32) for g, width in WB_LOADS.items()}
         sc_picked = held("sc_picked", [P, S], U8)
         v2_sc = held("v2_sc", [P, S], U8)
-        w1_bf = [held("w1_bf%d" % a, [P, PACK * H], BF16) for a in range(PASSES)]
+        w1_bf = {(a, pair): held("w1_bf%d_%d" % (a, pair), [P, PAIR * H], BF16) for a in range(PASSES) for pair in range(2)}
         w1_q = [held("w1_q%d" % a, [P, H], U32) for a in range(PASSES)]
         w1_sc = [held("w1_sc%d" % a, [P, H], U8) for a in range(PASSES)]
         wr_q = held("wr_q", [P, H], U32)
@@ -114,14 +114,18 @@ def tile_list_wafer_drift_correction_kernel(
         def pick(a, entry, count):
             gather(picked(a, entry, count), tab[a], lists, entry, count)
 
-        def round_w1(a, lower, upper):
-            dst = w1_bf[a][:].rearrange("p (t m j) -> p m j t", t=PACK, j=PACK)
+        def round_w1(a, pair, copy):
             src = w1_raw[a][:].rearrange("p j (m t) -> p m j t", t=PACK)
-            lower(dst[:, :, :, 0:PAIR], src[:, :, :, 0:PAIR])
-            upper(dst[:, :, :, PAIR:PACK], src[:, :, :, PAIR:PACK])
+            copy(
+                w1_bf[a, pair][:].rearrange("p (t m j) -> p m j t", t=PAIR, j=PACK),
+                src[:, :, :, PAIR * pair:PAIR * (pair + 1)],
+            )
 
-        def quantize_w1(a):
-            nc.vector.quantize_mx(out=w1_q[a][:].bitcast(FP8X4), scales=w1_sc[a][:], in_=w1_bf[a][:])
+        def quantize_w1(a, pair):
+            cols = slice(pair * CHUNK, (pair + 1) * CHUNK)
+            nc.vector.quantize_mx(
+                out=w1_q[a][:, cols].bitcast(FP8X4), scales=w1_sc[a][:, cols], in_=w1_bf[a, pair][:],
+            )
 
         def wb_part(g):
             first = min(g, 2)
@@ -157,7 +161,7 @@ def tile_list_wafer_drift_correction_kernel(
                 if (h, pair) == (0, 0):
                     for c in range(2):
                         if u == 0:
-                            rho_b[c, pair] = held("rho_b%d_0" % c, [P, 2, CHUNK], F32)
+                            rho_b[c, pair] = held("rho_b%d_0" % c, [P, 2, CHUNK], F32, tag=tags[c])
                         nc.scalar.activation(
                             rho_b[c, pair][:, u, :], b_ps[:, c * CHUNK:(c + 1) * CHUNK],
                             ACT.Copy, scale=rho_t[:, t:t + 1],
@@ -320,13 +324,16 @@ def tile_list_wafer_drift_correction_kernel(
             wr_sc[:].rearrange("p (t m) -> p t m", t=PACK),
             wr_sc_raw[:].rearrange("p (m t) -> p t m", t=PACK),
         )
-        round_w1(0, on_scalar, on_scalar)
-        quantize_w1(0)
-        round_w1(1, on_scalar, on_vector)
-        quantize_w1(1)
-        reference_product(0, range(2), None)
-        reference_product(1, range(PACK), ("w1_raw1", "w1_raw0"))
-        reference_product(0, range(2, PACK), (None, "w1_bf1"))
+        for pair in range(2):
+            round_w1(0, pair, on_scalar)
+        round_w1(1, 0, on_scalar)
+        round_w1(1, 1, on_vector)
+        for a, pair in ((0, 0), (0, 1), (1, 1), (1, 0)):
+            quantize_w1(a, pair)
+        reference_product(0, range(2), ("w1_raw0", "w1_bf0_1"))
+        reference_product(1, range(2), ("w1_raw1", None))
+        reference_product(0, range(2, PACK), (None, "w1_bf1_1"))
+        reference_product(1, range(2, PACK), (None, "w1_bf1_0"))
         for h in range(2):
             v[0, h] = held("v0_%d" % h, [P, HALF], U32)
             pick(0, h * HALF, HALF)
@@ -347,7 +354,7 @@ def tile_list_wafer_drift_correction_kernel(
         bound(0)
         weigh(0, nc.gpsimd, tag="wb_raw0")
         round_wb(1, on_scalar, tag="resid0")
-        v[1, 1] = held("v1_1", [P, HALF], U32, tag="rho_b0_0")
+        v[1, 1] = held("v1_1", [P, HALF], U32, tag="w1_raw0")
         for c in range(2, CHUNKS):
             pick(1, c * CHUNK, CHUNK)
             a_second(c, 1)
@@ -358,7 +365,7 @@ def tile_list_wafer_drift_correction_kernel(
             calibrate(0, n, FREED[n])
         quantize_wb(0, tag="w1_raw1")
         weigh(1, nc.vector)
-        quantize_z(0, tag="w1_raw0")
+        quantize_z(0, tag="w1_bf1_0")
         quantize_z(1)
         quantize_wb(1, tag="bounded1")
         round_wb(2, on_vector, tag="z_bf1")

@@ -229,10 +229,10 @@ def tile_list_wafer_drift_correction_kernel(
                 rhs=z_q[h][:].bitcast(FP8X4), rhs_scale=z_sc[h][:], start=opens, stop=True,
             )
 
-        def finish(h, n, copy):
+        def finish(h, n, copy, queue=nc.sync):
             result = held("result%d_%d" % (h, n), [P, HALF], F32)
             copy(result[:], o_ps[h, n][:])
-            nc.sync.dma_start(out=out[n * P:(n + 1) * P, h * HALF:(h + 1) * HALF], in_=result[:])
+            queue.dma_start(out=out[n * P:(n + 1) * P, h * HALF:(h + 1) * HALF], in_=result[:])
 
         def finish_last(h, n, copy):
             for u in range(2):
@@ -243,12 +243,12 @@ def tile_list_wafer_drift_correction_kernel(
                     out=out[n * P:(n + 1) * P, h * HALF + u * CHUNK:h * HALF + (u + 1) * CHUNK], in_=result[:],
                 )
 
-        def finish_pair(h, n, first):
+        def finish_pair(h, n, first, queue=nc.sync):
             result = held("result%d_%d" % (h, n), [P, 2, HALF], F32)
             first(result[:, 0, :], o_ps[h, n][:])
             on_scalar(result[:, 1, :], o_ps[h, n + 1][:])
             rows = out[n * P:(n + 2) * P, h * HALF:(h + 1) * HALF]
-            nc.sync.dma_start(out=rows.rearrange("(u p) j -> p u j", u=2), in_=result[:])
+            queue.dma_start(out=rows.rearrange("(u p) j -> p u j", u=2), in_=result[:])
 
         def residual(c):
             for pair in range(2):
@@ -385,17 +385,17 @@ def tile_list_wafer_drift_correction_kernel(
         weigh(3, nc.vector, tag="resid0")
         quantize_z(2)
         quantize_z(3)
-        for n in range(4, TILES, 2):
-            finish_pair(0, n, on_scalar)
+        finish_pair(0, 4, on_scalar)
+        finish_pair(0, 6, on_scalar, nc.scalar)
         for n in range(2, 4):
             calibrate(1, n, FREED[n])
         for n in range(4):
             correct(1, n)
         finish_pair(1, 0, on_vector)
-        finish_pair(1, 2, on_vector)
+        finish_pair(1, 2, on_vector, nc.scalar)
         for n in range(4, TILES):
             calibrate(1, n, FREED[n])
             correct(1, n)
         finish_pair(1, 4, on_vector)
         finish(1, 6, on_vector)
-        finish(1, 7, on_scalar)
+        finish(1, 7, on_scalar, nc.scalar)

@@ -74,7 +74,7 @@ def tile_list_wafer_drift_correction_kernel(
         z_sc = [held("z_sc%d" % h, [P, HALF], U8) for h in range(2)]
         wb_sc = [held("wb_sc%d" % g, [P, CHUNK], U8) for g in range(PARTS)]
         v, v2, rho_b, a_ps, resid, bounded, z_bf, wb_bf, o_ps = {}, {}, {}, {}, {}, {}, {}, {}, {}
-        aside, z_q, wb_q = {}, {}, {}
+        z_q, wb_q, p_ps = {}, {}, {}
 
         def load_words(tile, packed):
             nc.sync.dma_start(out=tile[:].bitcast(I32), in_=packed.rearrange("p c i -> p (c i)").bitcast(I32))
@@ -234,20 +234,31 @@ def tile_list_wafer_drift_correction_kernel(
             copy(result[:], o_ps[h, n][:])
             queue.dma_start(out=out[n * P:(n + 1) * P, h * HALF:(h + 1) * HALF], in_=result[:])
 
-        def finish_last(h, n, copy):
+        def calibrate_pair(c, g, index):
+            p_ps[c, g] = bank(index, [P, 2, CHUNK], "p_ps")
             for u in range(2):
-                cols = slice(u * CHUNK, (u + 1) * CHUNK)
-                result = held("result%d_%d_%d" % (h, n, u), [P, CHUNK], F32)
-                copy(result[:], o_ps[h, n][:, cols])
-                nc.sync.dma_start(
-                    out=out[n * P:(n + 1) * P, h * HALF + u * CHUNK:h * HALF + (u + 1) * CHUNK], in_=result[:],
+                n = 2 * g + u
+                for a in range(PASSES):
+                    nc.tensor.matmul_mx(
+                        out=p_ps[c, g][:, u, :], lhsT=wp[a][:, 2 * n * P:2 * (n + 1) * P].bitcast(FP4X4),
+                        lhsT_scale=wp_sc[:, a, n * P:(n + 1) * P],
+                        rhs=picked(a, c * CHUNK, CHUNK).bitcast(FP8X4), rhs_scale=v_sc[a][:, c * CHUNK:(c + 1) * CHUNK],
+                        start=(u == 0 and a == 0), stop=False,
+                    )
+
+        def correct_pair(c, g):
+            cols = slice((c % 2) * CHUNK, (c % 2 + 1) * CHUNK)
+            for u in range(2):
+                rows = slice(u * P, (u + 1) * P)
+                nc.tensor.matmul_mx(
+                    out=p_ps[c, g][:, u, :], lhsT=wb_q[g][:, rows].bitcast(FP8X4), lhsT_scale=wb_sc[g][:, rows],
+                    rhs=z_q[c // 2][:, cols].bitcast(FP8X4), rhs_scale=z_sc[c // 2][:, cols], start=False, stop=(u == 1),
                 )
 
-        def finish_pair(h, n, first, queue=nc.sync):
-            result = held("result%d_%d" % (h, n), [P, 2, HALF], F32)
-            first(result[:, 0, :], o_ps[h, n][:])
-            on_scalar(result[:, 1, :], o_ps[h, n + 1][:])
-            rows = out[n * P:(n + 2) * P, h * HALF:(h + 1) * HALF]
+        def finish_chunk(c, g, copy, queue=nc.sync):
+            result = held("part%d_%d" % (c, g), [P, 2, CHUNK], F32)
+            copy(result[:], p_ps[c, g][:])
+            rows = out[2 * g * P:2 * (g + 1) * P, c * CHUNK:(c + 1) * CHUNK]
             queue.dma_start(out=rows.rearrange("(u p) j -> p u j", u=2), in_=result[:])
 
         def residual(c):
@@ -262,18 +273,6 @@ def tile_list_wafer_drift_correction_kernel(
         def a_second(c, a):
             for pair in range(2):
                 a_pass(c, pair, a, False)
-
-        def set_aside(n, index):
-            calibrate(1, n, index, True)
-            aside[n] = held("aside%d" % n, [P, HALF], F32)
-            on_scalar(aside[n][:], o_ps[1, n][:])
-
-        def finish_aside(n, index):
-            o_ps[1, n] = bank(index, [P, HALF], "o_ps")
-            correct(1, n, True)
-            result = held("result1_%d" % n, [P, HALF], F32)
-            nc.vector.tensor_tensor(result[:], o_ps[1, n][:], aside[n][:], ALU.add)
-            nc.sync.dma_start(out=out[n * P:(n + 1) * P, HALF:S], in_=result[:])
 
         nc.gpsimd.memset(sc_win[:].bitcast(I32), 0)
         nc.vector.memset(sc2_win[:].bitcast(I32), 0)
@@ -361,41 +360,58 @@ def tile_list_wafer_drift_correction_kernel(
         for c in range(1, CHUNKS):
             residual(c)
             bound(c)
-        for n in range(TILES):
-            calibrate(0, n, FREED[n])
-        quantize_wb(0, tag="w1_raw1")
-        weigh(1, nc.vector)
-        quantize_z(0, tag="w1_bf1_0")
-        quantize_z(1)
-        quantize_wb(1, tag="bounded1")
-        round_wb(2, on_vector, tag="z_bf1")
-        quantize_wb(2)
-        round_wb(3, on_vector, tag="resid0")
-        for n in range(4):
-            correct(0, n)
-            finish(0, n, on_scalar)
-        quantize_wb(3)
-        weigh(2, nc.vector, tag="z_bf1")
-        calibrate(1, 0, FREED[0])
+        for c in range(2):
+            for g in range(2):
+                calibrate_pair(c, g, FREED[2 * c + g])
         for n in range(4, 6):
-            correct(0, n)
-        calibrate(1, 1, FREED[1])
+            calibrate(0, n, FREED[n])
+        quantize_wb(0, tag="w1_bf1_0")
+        quantize_z(0)
+        correct_pair(0, 0)
+        finish_chunk(0, 0, on_scalar)
         for n in range(6, TILES):
-            correct(0, n)
-        weigh(3, nc.vector, tag="resid0")
+            calibrate(0, n, FREED[n])
+        weigh(1, nc.vector, tag="wb_raw0")
+        quantize_wb(1, tag="bounded1")
+        quantize_z(1)
+        correct_pair(0, 1)
+        finish_chunk(0, 1, on_scalar)
+        calibrate_pair(2, 0, FREED[0])
+        for g in range(2):
+            correct_pair(1, g)
+            finish_chunk(1, g, on_scalar)
+        round_wb(2, on_vector, tag="wb_raw0")
+        round_wb(3, on_vector, tag="resid0")
+        quantize_wb(2)
+        quantize_wb(3)
+        calibrate_pair(2, 1, FREED[1])
+        for g in range(2):
+            for n in range(4 + 2 * g, 6 + 2 * g):
+                correct(0, n)
+            calibrate_pair(3, g, FREED[2 + g])
+        for n in range(4, 7):
+            finish(0, n, on_scalar)
+        weigh(2, nc.vector, tag="resid0")
         quantize_z(2)
+        for g in range(2):
+            correct_pair(2, g)
+        weigh(3, nc.vector, tag="resid0")
+        finish(0, 7, on_vector)
         quantize_z(3)
-        finish_pair(0, 4, on_scalar)
-        finish_pair(0, 6, on_scalar, nc.scalar)
-        for n in range(2, 4):
+        for g in range(2):
+            finish_chunk(2, g, on_scalar)
+        for n in range(4, 6):
             calibrate(1, n, FREED[n])
-        for n in range(4):
+        for g in range(2):
+            correct_pair(3, g)
+        finish_chunk(3, 0, on_vector)
+        finish_chunk(3, 1, on_scalar)
+        for n in range(4, 6):
             correct(1, n)
-        finish_pair(1, 0, on_vector)
-        finish_pair(1, 2, on_vector, nc.scalar)
-        for n in range(4, TILES):
+        finish(1, 4, on_vector)
+        finish(1, 5, on_scalar)
+        for n in range(6, TILES):
             calibrate(1, n, FREED[n])
             correct(1, n)
-        finish_pair(1, 4, on_vector)
         finish(1, 6, on_vector)
-        finish(1, 7, on_scalar, nc.scalar)
+        finish(1, 7, on_scalar)

@@ -365,14 +365,14 @@ def tile_list_wafer_drift_correction_kernel(
                 calibrate_pair(c, g, FREED[2 * c + g])
         for n in range(4, 6):
             calibrate(0, n, FREED[n])
-        quantize_wb(0, tag="w1_bf1_0")
         quantize_z(0)
+        quantize_wb(0, tag="bounded0")
         correct_pair(0, 0)
         finish_chunk(0, 0, on_scalar)
         for n in range(6, TILES):
             calibrate(0, n, FREED[n])
         weigh(1, nc.vector, tag="wb_raw0")
-        quantize_wb(1, tag="bounded1")
+        quantize_wb(1, tag="wb_bf0")
         quantize_z(1)
         correct_pair(0, 1)
         finish_chunk(0, 1, on_scalar)
@@ -380,38 +380,37 @@ def tile_list_wafer_drift_correction_kernel(
         for g in range(2):
             correct_pair(1, g)
             finish_chunk(1, g, on_scalar)
-        round_wb(2, on_vector, tag="wb_raw0")
+        round_wb(2, on_vector, tag="bounded1")
         round_wb(3, on_vector, tag="resid0")
         quantize_wb(2)
+        weigh(2, nc.vector, tag="wb_raw2")
         quantize_wb(3)
+        quantize_z(2)
+        weigh(3, nc.vector, tag="resid0")
+        quantize_z(3)
         calibrate_pair(2, 1, FREED[1])
         for g in range(2):
             for n in range(4 + 2 * g, 6 + 2 * g):
                 correct(0, n)
             calibrate_pair(3, g, FREED[2 + g])
-        for n in range(4, 7):
+        for n in range(4, TILES):
             finish(0, n, on_scalar)
-        weigh(2, nc.vector, tag="resid0")
-        quantize_z(2)
         for g in range(2):
             correct_pair(2, g)
-        weigh(3, nc.vector, tag="resid0")
-        finish(0, 7, on_vector)
-        quantize_z(3)
-        for g in range(2):
-            finish_chunk(2, g, on_scalar)
+        finish_chunk(2, 0, on_scalar)
+        finish_chunk(2, 1, on_vector)
         for n in range(4, 6):
             calibrate(1, n, FREED[n])
         for g in range(2):
             correct_pair(3, g)
-        finish_chunk(3, 0, on_vector)
-        finish_chunk(3, 1, on_scalar)
+        finish_chunk(3, 0, on_scalar)
+        finish_chunk(3, 1, on_vector)
         for n in range(4, 6):
             correct(1, n)
-        finish(1, 4, on_vector)
-        finish(1, 5, on_scalar)
+        finish(1, 4, on_scalar)
+        finish(1, 5, on_vector)
         for n in range(6, TILES):
             calibrate(1, n, FREED[n])
             correct(1, n)
-        finish(1, 6, on_vector)
-        finish(1, 7, on_scalar)
+        finish(1, 6, on_scalar)
+        finish(1, 7, on_vector)

@@ -24,6 +24,7 @@ HALF = 512
 CHUNK = 256
 LIST_ROWS = 16
 PAIR = 2
+SHARE = 96
 PASSES, CHUNKS, PARTS, TILES = K // K_PASS, S // CHUNK, K // CHUNK, K // P
 FREED = (6, 7, 2, 3, 4, 5, 0, 1)
 WB_LOADS = {0: CHUNK, 1: CHUNK, 2: HALF}
@@ -138,8 +139,7 @@ def tile_list_wafer_drift_correction_kernel(
                 wb_part(g).rearrange("p j (g i) -> p g j i", i=PAIR),
             )
 
-        def round_wb_gpsimd(g, tag=None):
-            wb_bf[g] = held("wb_bf%d" % g, [P, CHUNK, PACK], BF16, tag=tag)
+        def round_wb_gpsimd(g):
             on_gpsimd(wb_bf[g][:], wb_part(g).rearrange("p j n -> p n j"))
 
         def quantize_wb(g, tag=None):
@@ -185,23 +185,26 @@ def tile_list_wafer_drift_correction_kernel(
                     start=(opens and u == 0), stop=(not opens and u == 1),
                 )
 
-        def subtract(c, pair):
+        def subtract(c, pair, cols=slice(0, CHUNK)):
             two = slice(2 * pair, 2 * pair + 2)
-            nc.vector.tensor_tensor(resid[c][:, two, :], rho_b[c, pair][:], a_ps[c, pair][:], ALU.subtract)
+            nc.vector.tensor_tensor(
+                resid[c][:, two, cols], rho_b[c, pair][:, :, cols], a_ps[c, pair][:, :, cols], ALU.subtract,
+            )
 
-        def bound(c):
-            bounded[c] = held("bounded%d" % c, [P, CHUNK, PACK], F32)
+        def bound(c, cols=slice(0, CHUNK)):
+            if cols.start == 0:
+                bounded[c] = held("bounded%d" % c, [P, CHUNK, PACK], F32)
             nc.scalar.activation(
-                bounded[c][:].rearrange("p (g i) t -> p g t i", i=PAIR),
-                resid[c][:].rearrange("p t (g i) -> p g t i", i=PAIR),
+                bounded[c][:, cols].rearrange("p (g i) t -> p g t i", i=PAIR),
+                resid[c][:, :, cols].rearrange("p t (g i) -> p g t i", i=PAIR),
                 ACT.Tanh,
             )
 
-        def weigh(c, engine, tag=None):
-            z_bf[c] = held("z_bf%d" % c, [P, CHUNK, PACK], BF16, tag=tag)
-            engine.tensor_tensor(
-                z_bf[c][:], bounded[c][:], gain_t[:].unsqueeze(1).to_broadcast([P, CHUNK, PACK]), ALU.mult,
-            )
+        def weigh(c, engine, tag=None, cols=slice(0, CHUNK)):
+            if c not in z_bf:
+                z_bf[c] = held("z_bf%d" % c, [P, CHUNK, PACK], BF16, tag=tag)
+            spread = gain_t[:].unsqueeze(1).to_broadcast([P, cols.stop - cols.start, PACK])
+            engine.tensor_tensor(z_bf[c][:, cols], bounded[c][:, cols], spread, ALU.mult)
 
         def quantize_z(c, tag=None):
             if c % 2 == 0:
@@ -347,17 +350,25 @@ def tile_list_wafer_drift_correction_kernel(
         a_second(1, 0)
         for c in range(CHUNKS):
             resid[c] = held("resid%d" % c, [P, PACK, CHUNK], F32)
+        stage = held("stage", [P, SHARE + CHUNK, PACK], BF16)
+        z_bf[1], wb_bf[0] = stage[:, 0:CHUNK], stage[:, SHARE:SHARE + CHUNK]
         round_wb_gpsimd(0)
-        residual(0)
+        for cols in (slice(0, P), slice(P, CHUNK)):
+            for pair in range(2):
+                subtract(0, pair, cols)
+            bound(0, cols)
+            weigh(0, nc.gpsimd, "wb_raw0", cols)
         a_first(3, 0, 0)
-        bound(0)
-        weigh(0, nc.gpsimd, tag="wb_raw0")
         round_wb(1, on_scalar, tag="resid0")
         v[1, 1] = held("v1_1", [P, HALF], U32, tag="w1_raw0")
         for c in range(2, CHUNKS):
             pick(1, c * CHUNK, CHUNK)
             a_second(c, 1)
-        for c in range(1, CHUNKS):
+        residual(1)
+        bound(1, slice(0, SHARE))
+        weigh(1, nc.gpsimd, None, slice(0, SHARE))
+        bound(1, slice(SHARE, CHUNK))
+        for c in range(2, CHUNKS):
             residual(c)
             bound(c)
         for c in range(2):
@@ -365,14 +376,14 @@ def tile_list_wafer_drift_correction_kernel(
                 calibrate_pair(c, g, FREED[2 * c + g])
         for n in range(4, 6):
             calibrate(0, n, FREED[n])
-        quantize_z(0)
         quantize_wb(0, tag="bounded0")
+        quantize_z(0)
         correct_pair(0, 0)
         finish_chunk(0, 0, on_scalar)
         for n in range(6, TILES):
             calibrate(0, n, FREED[n])
-        weigh(1, nc.vector, tag="wb_raw0")
-        quantize_wb(1, tag="wb_bf0")
+        weigh(1, nc.vector, None, slice(SHARE, CHUNK))
+        quantize_wb(1, tag="wb_raw0")
         quantize_z(1)
         correct_pair(0, 1)
         finish_chunk(0, 1, on_scalar)
@@ -385,8 +396,8 @@ def tile_list_wafer_drift_correction_kernel(
         quantize_wb(2)
         weigh(2, nc.vector, tag="wb_raw2")
         quantize_wb(3)
+        weigh(3, nc.vector, tag="bounded1")
         quantize_z(2)
-        weigh(3, nc.vector, tag="resid0")
         quantize_z(3)
         calibrate_pair(2, 1, FREED[1])
         for g in range(2):

@@ -380,17 +380,15 @@ def tile_list_wafer_drift_correction_kernel(
         quantize_z(0)
         correct_pair(0, 0)
         finish_chunk(0, 0, on_scalar)
-        for n in range(6, TILES):
-            calibrate(0, n, FREED[n])
+        calibrate(0, 6, FREED[6])
         weigh(1, nc.vector, None, slice(SHARE, CHUNK))
         quantize_wb(1, tag="wb_raw0")
         quantize_z(1)
-        correct_pair(0, 1)
-        finish_chunk(0, 1, on_scalar)
+        for c, g in ((0, 1), (1, 0), (1, 1)):
+            correct_pair(c, g)
+            finish_chunk(c, g, on_scalar)
+        calibrate(0, 7, FREED[7])
         calibrate_pair(2, 0, FREED[0])
-        for g in range(2):
-            correct_pair(1, g)
-            finish_chunk(1, g, on_scalar)
         round_wb(2, on_vector, tag="bounded1")
         round_wb(3, on_vector, tag="resid0")
         quantize_wb(2)
@@ -399,29 +397,21 @@ def tile_list_wafer_drift_correction_kernel(
         weigh(3, nc.vector, tag="bounded1")
         quantize_z(2)
         quantize_z(3)
-        calibrate_pair(2, 1, FREED[1])
         for g in range(2):
             for n in range(4 + 2 * g, 6 + 2 * g):
                 correct(0, n)
-            calibrate_pair(3, g, FREED[2 + g])
-        for n in range(4, TILES):
-            finish(0, n, on_scalar)
+                finish(0, n, on_scalar)
+            calibrate_pair(2 + g, 1 - g, FREED[1 + g])
         for g in range(2):
             correct_pair(2, g)
         finish_chunk(2, 0, on_scalar)
         finish_chunk(2, 1, on_vector)
-        for n in range(4, 6):
-            calibrate(1, n, FREED[n])
+        calibrate_pair(3, 1, FREED[3])
         for g in range(2):
             correct_pair(3, g)
         finish_chunk(3, 0, on_scalar)
         finish_chunk(3, 1, on_vector)
-        for n in range(4, 6):
-            correct(1, n)
-        finish(1, 4, on_scalar)
-        finish(1, 5, on_vector)
-        for n in range(6, TILES):
+        for n in range(4, TILES):
             calibrate(1, n, FREED[n])
             correct(1, n)
-        finish(1, 6, on_scalar)
-        finish(1, 7, on_vector)
+            finish(1, n, on_vector if n % 2 else on_scalar)

@@ -26,6 +26,8 @@ LIST_ROWS = 16
 PAIR = 2
 SHARE = 96
 PASSES, CHUNKS, PARTS, TILES = K // K_PASS, S // CHUNK, K // CHUNK, K // P
+DUOS = 2
+WHOLE = 2 * DUOS
 FREED = (6, 7, 2, 3, 4, 5, 0, 1)
 WB_LOADS = {0: CHUNK, 1: CHUNK, 2: HALF}
 V2_FIRST, WR_FIRST = 8, 12
@@ -41,9 +43,6 @@ def tile_list_wafer_drift_correction_kernel(
         psum = ctx.enter_context(tc.psum_pool(name="psum", bufs=1))
         on_scalar, on_vector = nc.scalar.copy, nc.vector.tensor_copy
 
-        def on_gpsimd(dst, src):
-            nc.gpsimd.tensor_scalar(dst, src, 1.0, 0.0, ALU.mult, ALU.add)
-
         def held(name, shape, dtype, tag=None):
             return keep.tile(shape, dtype, name=name, tag=tag or name, align_bytes=256)
 
@@ -56,91 +55,91 @@ def tile_list_wafer_drift_correction_kernel(
         sc2_win = held("sc2_win", [P, T], U8)
         wr_sc_raw = held("wr_sc_raw", [P, H], U8)
         wp_sc = held("wp_sc", [P, PASSES, K], U8)
-        v_sc = [held("v_sc%d" % a, [P, S], U8) for a in range(PASSES)]
+        v_sc = [held("v_sc%d" % kp, [P, S], U8) for kp in range(PASSES)]
         rho_t = held("rho_t", [P, PACK], F32)
         gain_t = held("gain_t", [P, PACK], F32)
-        w1_raw = [held("w1_raw%d" % a, [P, PACK, H], F32) for a in range(PASSES)]
-        tab = [held("tab%d" % a, [P, T], U32) for a in range(PASSES)]
+        w1_raw = [held("w1_raw%d" % kp, [P, PACK, H], F32) for kp in range(PASSES)]
+        tab = [held("tab%d" % kp, [P, T], U32) for kp in range(PASSES)]
         tab2 = held("tab2", [P, T], U32)
         wr_raw = held("wr_raw", [P, H], U32)
-        wp = [held("wp%d" % a, [P, 2 * K], U8) for a in range(PASSES)]
+        wp = [held("wp%d" % kp, [P, 2 * K], U8) for kp in range(PASSES)]
         wb_raw = {g: held("wb_raw%d" % g, [P, PACK, width], F32) for g, width in WB_LOADS.items()}
         sc_picked = held("sc_picked", [P, S], U8)
         v2_sc = held("v2_sc", [P, S], U8)
-        w1_bf = {(a, pair): held("w1_bf%d_%d" % (a, pair), [P, PAIR * H], BF16) for a in range(PASSES) for pair in range(2)}
-        w1_q = [held("w1_q%d" % a, [P, H], U32) for a in range(PASSES)]
-        w1_sc = [held("w1_sc%d" % a, [P, H], U8) for a in range(PASSES)]
+        w1_bf = {(kp, pair): held("w1_bf%d_%d" % (kp, pair), [P, PAIR * H], BF16) for kp in range(PASSES) for pair in range(2)}
+        w1_q = [held("w1_q%d" % kp, [P, H], U32) for kp in range(PASSES)]
+        w1_sc = [held("w1_sc%d" % kp, [P, H], U8) for kp in range(PASSES)]
         wr_q = held("wr_q", [P, H], U32)
         wr_sc = held("wr_sc", [P, H], U8)
         z_sc = [held("z_sc%d" % h, [P, HALF], U8) for h in range(2)]
         wb_sc = [held("wb_sc%d" % g, [P, CHUNK], U8) for g in range(PARTS)]
         v, v2, rho_b, a_ps, resid, bounded, z_bf, wb_bf, o_ps = {}, {}, {}, {}, {}, {}, {}, {}, {}
-        z_q, wb_q, p_ps = {}, {}, {}
+        z_q, wb_q, duo_ps = {}, {}, {}
 
         def load_words(tile, packed):
             nc.sync.dma_start(out=tile[:].bitcast(I32), in_=packed.rearrange("p c i -> p (c i)").bitcast(I32))
 
         def load_plane(plane, rows, first, which):
-            for r in which:
-                nc.sync.dma_start(out=plane[:].bitcast(I32)[first + r:P:QUADRANT], in_=rows[r].bitcast(I32))
+            for e in which:
+                nc.sync.dma_start(out=plane[:].bitcast(I32)[first + e:P:QUADRANT], in_=rows[e].bitcast(I32))
 
         def load_by_slice(tile, vec):
             nc.sync.dma_start(out=tile[:], in_=vec.rearrange("(p t) -> p t", t=PACK))
 
-        def load_w1(a):
-            rows = w1[a * K_PASS:(a + 1) * K_PASS, :]
-            nc.sync.dma_start(out=w1_raw[a][:], in_=rows.rearrange("(p j) r -> p j r", j=PACK))
+        def load_w1(kp):
+            rows = w1[kp * K_PASS:(kp + 1) * K_PASS, :]
+            nc.sync.dma_start(out=w1_raw[kp][:], in_=rows.rearrange("(p j) r -> p j r", j=PACK))
 
-        def load_wp(a):
-            nc.sync.dma_start(out=wp[a][:].bitcast(I32), in_=wp_words[a].bitcast(I32))
+        def load_wp(kp):
+            nc.sync.dma_start(out=wp[kp][:].bitcast(I32), in_=wp_words[kp].bitcast(I32))
 
         def load_wb(g):
             cols = wb[:, g * CHUNK:g * CHUNK + WB_LOADS[g]]
             nc.sync.dma_start(out=wb_raw[g][:], in_=cols.rearrange("(p j) n -> p j n", j=PACK))
 
-        def place_scales(a):
-            for r in range(PACK):
+        def place_scales(kp):
+            for e in range(PACK):
                 nc.sync.dma_start(
-                    out=v_sc[a][:].bitcast(I32)[r:P:QUADRANT],
-                    in_=sc_picked[:].bitcast(I32)[8 * r + 4 * a:P:QUADRANT],
+                    out=v_sc[kp][:].bitcast(I32)[e:P:QUADRANT],
+                    in_=sc_picked[:].bitcast(I32)[8 * e + 4 * kp:P:QUADRANT],
                 )
 
         def gather(dst, window, offsets, entry, count):
             cols = slice(entry // LIST_ROWS, (entry + count) // LIST_ROWS)
             nc.vector.tensor_copy(dst, window[:].indirect(offsets[:, cols]))
 
-        def picked(a, entry, count):
-            return v[a, entry // HALF][:, entry % HALF:entry % HALF + count]
+        def picked(kp, entry, count):
+            return v[kp, entry // HALF][:, entry % HALF:entry % HALF + count]
 
-        def pick(a, entry, count):
-            gather(picked(a, entry, count), tab[a], lists, entry, count)
+        def pick(kp, entry, count):
+            gather(picked(kp, entry, count), tab[kp], lists, entry, count)
 
-        def round_w1(a, pair, copy):
-            src = w1_raw[a][:].rearrange("p j (m t) -> p m j t", t=PACK)
+        def round_w1(kp, pair, copy):
+            src = w1_raw[kp][:].rearrange("p j (m t) -> p m j t", t=PACK)
             copy(
-                w1_bf[a, pair][:].rearrange("p (t m j) -> p m j t", t=PAIR, j=PACK),
+                w1_bf[kp, pair][:].rearrange("p (t m j) -> p m j t", t=PAIR, j=PACK),
                 src[:, :, :, PAIR * pair:PAIR * (pair + 1)],
             )
 
-        def quantize_w1(a, pair):
+        def quantize_w1(kp, pair):
             cols = slice(pair * CHUNK, (pair + 1) * CHUNK)
             nc.vector.quantize_mx(
-                out=w1_q[a][:, cols].bitcast(FP8X4), scales=w1_sc[a][:, cols], in_=w1_bf[a, pair][:],
+                out=w1_q[kp][:, cols].bitcast(FP8X4), scales=w1_sc[kp][:, cols], in_=w1_bf[kp, pair][:],
             )
 
         def wb_part(g):
-            first = min(g, 2)
+            first = max(load for load in WB_LOADS if load <= g)
             return wb_raw[first][:, :, (g - first) * CHUNK:(g - first + 1) * CHUNK]
 
-        def round_wb(g, copy, tag=None):
+        def round_wb(g, copy, tag):
             wb_bf[g] = held("wb_bf%d" % g, [P, CHUNK, PACK], BF16, tag=tag)
             copy(
-                wb_bf[g][:].rearrange("p (g i) j -> p g j i", i=PAIR),
-                wb_part(g).rearrange("p j (g i) -> p g j i", i=PAIR),
+                wb_bf[g][:].rearrange("p (m i) j -> p m j i", i=PAIR),
+                wb_part(g).rearrange("p j (m i) -> p m j i", i=PAIR),
             )
 
         def round_wb_gpsimd(g):
-            on_gpsimd(wb_bf[g][:], wb_part(g).rearrange("p j n -> p n j"))
+            nc.gpsimd.tensor_scalar(wb_bf[g][:], wb_part(g).rearrange("p j n -> p n j"), 1.0, 0.0, ALU.mult, ALU.add)
 
         def quantize_wb(g, tag=None):
             wb_q[g] = held("wb_q%d" % g, [P, CHUNK], U32, tag=tag)
@@ -175,13 +174,13 @@ def tile_list_wafer_drift_correction_kernel(
                         both[:, :, u, :], b_ps[:].rearrange("p (c j) -> p c j", c=2), ACT.Copy, scale=rho_t[:, t:t + 1],
                     )
 
-        def a_pass(c, pair, a, opens):
+        def a_pass(c, pair, kp, opens):
             for u in range(2):
                 rows = slice((2 * pair + u) * P, (2 * pair + u + 1) * P)
                 nc.tensor.matmul_mx(
-                    out=a_ps[c, pair][:, u, :], lhsT=w1_q[a][:, rows].bitcast(FP8X4), lhsT_scale=w1_sc[a][:, rows],
-                    rhs=picked(a, c * CHUNK, CHUNK).bitcast(FP8X4),
-                    rhs_scale=v_sc[a][:, c * CHUNK:(c + 1) * CHUNK],
+                    out=a_ps[c, pair][:, u, :], lhsT=w1_q[kp][:, rows].bitcast(FP8X4), lhsT_scale=w1_sc[kp][:, rows],
+                    rhs=picked(kp, c * CHUNK, CHUNK).bitcast(FP8X4),
+                    rhs_scale=v_sc[kp][:, c * CHUNK:(c + 1) * CHUNK],
                     start=(opens and u == 0), stop=(not opens and u == 1),
                 )
 
@@ -195,8 +194,8 @@ def tile_list_wafer_drift_correction_kernel(
             if cols.start == 0:
                 bounded[c] = held("bounded%d" % c, [P, CHUNK, PACK], F32)
             nc.scalar.activation(
-                bounded[c][:, cols].rearrange("p (g i) t -> p g t i", i=PAIR),
-                resid[c][:, :, cols].rearrange("p t (g i) -> p g t i", i=PAIR),
+                bounded[c][:, cols].rearrange("p (m i) t -> p m t i", i=PAIR),
+                resid[c][:, :, cols].rearrange("p t (m i) -> p m t i", i=PAIR),
                 ACT.Tanh,
             )
 
@@ -206,97 +205,98 @@ def tile_list_wafer_drift_correction_kernel(
             spread = gain_t[:].unsqueeze(1).to_broadcast([P, cols.stop - cols.start, PACK])
             engine.tensor_tensor(z_bf[c][:, cols], bounded[c][:, cols], spread, ALU.mult)
 
-        def quantize_z(c, tag=None):
+        def quantize_z(c):
             if c % 2 == 0:
-                z_q[c // 2] = held("z_q%d" % (c // 2), [P, HALF], U32, tag=tag)
+                z_q[c // 2] = held("z_q%d" % (c // 2), [P, HALF], U32)
             cols = slice((c % 2) * CHUNK, (c % 2 + 1) * CHUNK)
             nc.vector.quantize_mx(
                 out=z_q[c // 2][:, cols].bitcast(FP8X4), scales=z_sc[c // 2][:, cols],
                 in_=z_bf[c][:].rearrange("p j t -> p (j t)"),
             )
 
-        def calibrate(h, n, index, closes=False):
+        def calibrate(h, n, index):
             o_ps[h, n] = bank(index, [P, HALF], "o_ps")
-            for a in range(PASSES):
+            for kp in range(PASSES):
                 nc.tensor.matmul_mx(
-                    out=o_ps[h, n][:], lhsT=wp[a][:, 2 * n * P:2 * (n + 1) * P].bitcast(FP4X4),
-                    lhsT_scale=wp_sc[:, a, n * P:(n + 1) * P],
-                    rhs=picked(a, h * HALF, HALF).bitcast(FP8X4), rhs_scale=v_sc[a][:, h * HALF:(h + 1) * HALF],
-                    start=(a == 0), stop=(closes and a == PASSES - 1),
+                    out=o_ps[h, n][:], lhsT=wp[kp][:, 2 * n * P:2 * (n + 1) * P].bitcast(FP4X4),
+                    lhsT_scale=wp_sc[:, kp, n * P:(n + 1) * P],
+                    rhs=picked(kp, h * HALF, HALF).bitcast(FP8X4), rhs_scale=v_sc[kp][:, h * HALF:(h + 1) * HALF],
+                    start=(kp == 0), stop=False,
                 )
 
-        def correct(h, n, opens=False):
+        def correct(h, n):
             g, rows = n // 2, slice((n % 2) * P, (n % 2 + 1) * P)
             nc.tensor.matmul_mx(
                 out=o_ps[h, n][:], lhsT=wb_q[g][:, rows].bitcast(FP8X4), lhsT_scale=wb_sc[g][:, rows],
-                rhs=z_q[h][:].bitcast(FP8X4), rhs_scale=z_sc[h][:], start=opens, stop=True,
+                rhs=z_q[h][:].bitcast(FP8X4), rhs_scale=z_sc[h][:], start=False, stop=True,
             )
 
-        def finish(h, n, copy, queue=nc.sync):
+        def finish(h, n, copy):
             result = held("result%d_%d" % (h, n), [P, HALF], F32)
             copy(result[:], o_ps[h, n][:])
-            queue.dma_start(out=out[n * P:(n + 1) * P, h * HALF:(h + 1) * HALF], in_=result[:])
+            nc.sync.dma_start(out=out[n * P:(n + 1) * P, h * HALF:(h + 1) * HALF], in_=result[:])
 
-        def calibrate_pair(c, g, index):
-            p_ps[c, g] = bank(index, [P, 2, CHUNK], "p_ps")
+        def calibrate_duo(c, g, index):
+            duo_ps[c, g] = bank(index, [P, 2, CHUNK], "p_ps")
             for u in range(2):
                 n = 2 * g + u
-                for a in range(PASSES):
+                for kp in range(PASSES):
                     nc.tensor.matmul_mx(
-                        out=p_ps[c, g][:, u, :], lhsT=wp[a][:, 2 * n * P:2 * (n + 1) * P].bitcast(FP4X4),
-                        lhsT_scale=wp_sc[:, a, n * P:(n + 1) * P],
-                        rhs=picked(a, c * CHUNK, CHUNK).bitcast(FP8X4), rhs_scale=v_sc[a][:, c * CHUNK:(c + 1) * CHUNK],
-                        start=(u == 0 and a == 0), stop=False,
+                        out=duo_ps[c, g][:, u, :], lhsT=wp[kp][:, 2 * n * P:2 * (n + 1) * P].bitcast(FP4X4),
+                        lhsT_scale=wp_sc[:, kp, n * P:(n + 1) * P],
+                        rhs=picked(kp, c * CHUNK, CHUNK).bitcast(FP8X4), rhs_scale=v_sc[kp][:, c * CHUNK:(c + 1) * CHUNK],
+                        start=(u == 0 and kp == 0), stop=False,
                     )
 
-        def correct_pair(c, g):
+        def correct_duo(c, g):
             cols = slice((c % 2) * CHUNK, (c % 2 + 1) * CHUNK)
             for u in range(2):
                 rows = slice(u * P, (u + 1) * P)
                 nc.tensor.matmul_mx(
-                    out=p_ps[c, g][:, u, :], lhsT=wb_q[g][:, rows].bitcast(FP8X4), lhsT_scale=wb_sc[g][:, rows],
+                    out=duo_ps[c, g][:, u, :], lhsT=wb_q[g][:, rows].bitcast(FP8X4), lhsT_scale=wb_sc[g][:, rows],
                     rhs=z_q[c // 2][:, cols].bitcast(FP8X4), rhs_scale=z_sc[c // 2][:, cols], start=False, stop=(u == 1),
                 )
 
-        def finish_chunk(c, g, copy, queue=nc.sync):
+        def finish_duo(c, g, copy):
             result = held("part%d_%d" % (c, g), [P, 2, CHUNK], F32)
-            copy(result[:], p_ps[c, g][:])
+            copy(result[:], duo_ps[c, g][:])
             rows = out[2 * g * P:2 * (g + 1) * P, c * CHUNK:(c + 1) * CHUNK]
-            queue.dma_start(out=rows.rearrange("(u p) j -> p u j", u=2), in_=result[:])
+            nc.sync.dma_start(out=rows.rearrange("(u p) j -> p u j", u=2), in_=result[:])
 
         def residual(c):
             for pair in range(2):
                 subtract(c, pair)
 
-        def a_first(c, a, index):
+        def a_first(c, kp, index):
             for pair in range(2):
                 a_ps[c, pair] = bank(index + pair, [P, 2, CHUNK], "a_ps")
-                a_pass(c, pair, a, True)
+                a_pass(c, pair, kp, True)
 
-        def a_second(c, a):
+        def a_second(c, kp):
             for pair in range(2):
-                a_pass(c, pair, a, False)
+                a_pass(c, pair, kp, False)
 
         nc.gpsimd.memset(sc_win[:].bitcast(I32), 0)
         nc.vector.memset(sc2_win[:].bitcast(I32), 0)
         nc.vector.memset(wr_sc_raw[:].bitcast(I32), 0)
-        for a in range(PASSES):
-            nc.vector.memset(v_sc[a][:].bitcast(I32), 0)
+        for kp in range(PASSES):
+            nc.vector.memset(v_sc[kp][:].bitcast(I32), 0)
         nc.vector.memset(wp_sc[:].bitcast(I32), 0)
 
-        wr_rows = wr_scales[0].rearrange("(d r) c -> r d c", r=PACK)
-        wp_rows = wp_scales.rearrange("a (d r) c -> r d a c", r=PACK)
+        wr_rows = wr_scales[0].rearrange("(d e) c -> e d c", e=PACK)
+        wp_rows = wp_scales.rearrange("kp (d e) c -> e d kp c", e=PACK)
+        v2_rows = tab2_scales[0].rearrange("(d e) t -> e d t", e=PACK)
         nc.sync.dma_start(lists[:], offs)
         load_words(wr_raw, wr_words[0])
         load_by_slice(rho_t, rho)
         nc.sync.dma_start(lists2[:], offs2)
         nc.sync.dma_start(
-            out=sc_win[:].bitcast(I32)[0:P:4, :],
-            in_=tab_scales.rearrange("a q t -> q a t").bitcast(I32),
+            out=sc_win[:].bitcast(I32)[0:P:PACK, :],
+            in_=tab_scales.rearrange("kp q t -> q kp t").bitcast(I32),
         )
-        load_plane(sc2_win, tab2_scales[0].rearrange("(d r) t -> r d t", r=PACK), V2_FIRST, range(2))
+        load_plane(sc2_win, v2_rows, V2_FIRST, range(2))
         load_words(tab2, tab2_words[0])
-        load_plane(sc2_win, tab2_scales[0].rearrange("(d r) t -> r d t", r=PACK), V2_FIRST, range(2, PACK))
+        load_plane(sc2_win, v2_rows, V2_FIRST, range(2, PACK))
         load_plane(wr_sc_raw, wr_rows, WR_FIRST, range(2))
         load_w1(0)
         load_plane(wr_sc_raw, wr_rows, WR_FIRST, range(2, PACK))
@@ -330,8 +330,8 @@ def tile_list_wafer_drift_correction_kernel(
             round_w1(0, pair, on_scalar)
         round_w1(1, 0, on_scalar)
         round_w1(1, 1, on_vector)
-        for a, pair in ((0, 0), (0, 1), (1, 1), (1, 0)):
-            quantize_w1(a, pair)
+        for kp, pair in ((0, 0), (0, 1), (1, 1), (1, 0)):
+            quantize_w1(kp, pair)
         reference_product(0, range(2), ("w1_raw0", "w1_bf0_1"))
         reference_product(1, range(2), ("w1_raw1", None))
         reference_product(0, range(2, PACK), (None, "w1_bf1_1"))
@@ -353,7 +353,7 @@ def tile_list_wafer_drift_correction_kernel(
         stage = held("stage", [P, SHARE + CHUNK, PACK], BF16)
         z_bf[1], wb_bf[0] = stage[:, 0:CHUNK], stage[:, SHARE:SHARE + CHUNK]
         round_wb_gpsimd(0)
-        for cols in (slice(0, P), slice(P, CHUNK)):
+        for cols in (slice(0, CHUNK // 2), slice(CHUNK // 2, CHUNK)):
             for pair in range(2):
                 subtract(0, pair, cols)
             bound(0, cols)
@@ -371,47 +371,49 @@ def tile_list_wafer_drift_correction_kernel(
         for c in range(2, CHUNKS):
             residual(c)
             bound(c)
+
         for c in range(2):
-            for g in range(2):
-                calibrate_pair(c, g, FREED[2 * c + g])
-        for n in range(4, 6):
+            for g in range(DUOS):
+                calibrate_duo(c, g, FREED[DUOS * c + g])
+        for n in range(WHOLE, WHOLE + 2):
             calibrate(0, n, FREED[n])
         quantize_wb(0, tag="bounded0")
         quantize_z(0)
-        correct_pair(0, 0)
-        finish_chunk(0, 0, on_scalar)
-        calibrate(0, 6, FREED[6])
+        correct_duo(0, 0)
+        finish_duo(0, 0, on_scalar)
+        calibrate(0, TILES - 2, FREED[TILES - 2])
         weigh(1, nc.vector, None, slice(SHARE, CHUNK))
         quantize_wb(1, tag="wb_raw0")
         quantize_z(1)
         for c, g in ((0, 1), (1, 0), (1, 1)):
-            correct_pair(c, g)
-            finish_chunk(c, g, on_scalar)
-        calibrate(0, 7, FREED[7])
-        calibrate_pair(2, 0, FREED[0])
+            correct_duo(c, g)
+            finish_duo(c, g, on_scalar)
+        calibrate(0, TILES - 1, FREED[TILES - 1])
+        calibrate_duo(2, 0, FREED[0])
         round_wb(2, on_vector, tag="bounded1")
         round_wb(3, on_vector, tag="resid0")
         quantize_wb(2)
-        weigh(2, nc.vector, tag="wb_raw2")
         quantize_wb(3)
+        weigh(2, nc.vector, tag="wb_raw2")
         weigh(3, nc.vector, tag="bounded1")
         quantize_z(2)
         quantize_z(3)
-        for g in range(2):
-            for n in range(4 + 2 * g, 6 + 2 * g):
+        for g, (next_c, next_g) in ((2, (2, 1)), (3, (3, 0))):
+            for n in (2 * g, 2 * g + 1):
                 correct(0, n)
                 finish(0, n, on_scalar)
-            calibrate_pair(2 + g, 1 - g, FREED[1 + g])
-        for g in range(2):
-            correct_pair(2, g)
-        finish_chunk(2, 0, on_scalar)
-        finish_chunk(2, 1, on_vector)
-        calibrate_pair(3, 1, FREED[3])
-        for g in range(2):
-            correct_pair(3, g)
-        finish_chunk(3, 0, on_scalar)
-        finish_chunk(3, 1, on_vector)
-        for n in range(4, TILES):
+            calibrate_duo(next_c, next_g, FREED[g - 1])
+
+        for g in range(DUOS):
+            correct_duo(2, g)
+        finish_duo(2, 0, on_scalar)
+        finish_duo(2, 1, on_vector)
+        calibrate_duo(3, 1, FREED[3])
+        for g in range(DUOS):
+            correct_duo(3, g)
+        finish_duo(3, 0, on_scalar)
+        finish_duo(3, 1, on_vector)
+        for n in range(WHOLE, TILES):
             calibrate(1, n, FREED[n])
             correct(1, n)
             finish(1, n, on_vector if n % 2 else on_scalar)

@@ -389,7 +389,7 @@ def tile_list_wafer_drift_correction_kernel(
             correct_duo(c, g)
             finish_duo(c, g, on_scalar)
         calibrate(0, TILES - 1, FREED[TILES - 1])
-        calibrate_duo(2, 0, FREED[0])
+        calibrate(1, 0, FREED[0])
         round_wb(2, on_vector, tag="bounded1")
         round_wb(3, on_vector, tag="resid0")
         quantize_wb(2)
@@ -398,22 +398,15 @@ def tile_list_wafer_drift_correction_kernel(
         weigh(3, nc.vector, tag="bounded1")
         quantize_z(2)
         quantize_z(3)
-        for g, (next_c, next_g) in ((2, (2, 1)), (3, (3, 0))):
+        for g in (2, 3):
             for n in (2 * g, 2 * g + 1):
                 correct(0, n)
                 finish(0, n, on_scalar)
-            calibrate_duo(next_c, next_g, FREED[g - 1])
+            calibrate(1, g - 1, FREED[g - 1])
+        calibrate(1, 3, FREED[3])
 
-        for g in range(DUOS):
-            correct_duo(2, g)
-        finish_duo(2, 0, on_scalar)
-        finish_duo(2, 1, on_vector)
-        calibrate_duo(3, 1, FREED[3])
-        for g in range(DUOS):
-            correct_duo(3, g)
-        finish_duo(3, 0, on_scalar)
-        finish_duo(3, 1, on_vector)
-        for n in range(WHOLE, TILES):
-            calibrate(1, n, FREED[n])
+        for n in range(TILES):
+            if n >= WHOLE:
+                calibrate(1, n, FREED[n])
             correct(1, n)
             finish(1, n, on_vector if n % 2 else on_scalar)

from contextlib import ExitStack

import concourse.mybir as mybir

K, K2, H, T, S = 1024, 512, 512, 2048, 1024
FLOPS = 2 * S * (K * H + K2 * H + K * K + H * K)

F32 = mybir.dt.float32
BF16 = mybir.dt.bfloat16
I32 = mybir.dt.int32
U32 = mybir.dt.uint32
U16 = mybir.dt.uint16
U8 = mybir.dt.uint8
FP8X4 = mybir.dt.float8_e4m3fn_x4
FP4X4 = mybir.dt.float4_e2m1fn_x4
ACT = mybir.ActivationFunctionType
ALU = mybir.AluOpType

P = 128
PACK = 4
QUADRANT = 32
K_PASS = P * PACK
HALF = 512
CHUNK = 256
LIST_ROWS = 16
PAIR = 2
SHARE = 96
PASSES, CHUNKS, PARTS, TILES = K // K_PASS, S // CHUNK, K // CHUNK, K // P
DUOS = 2
WHOLE = 2 * DUOS
FREED = (6, 7, 2, 3, 4, 5, 0, 1)
WB_LOADS = {0: CHUNK, 1: CHUNK, 2: HALF}
V2_FIRST, WR_FIRST = 8, 12


def tile_list_wafer_drift_correction_kernel(
    tc, tab_words, tab_scales, offs, tab2_words, tab2_scales, offs2, w1,
    wr_words, wr_scales, rho, gain, wb, wp_words, wp_scales, out,
):
    nc = tc.nc
    with ExitStack() as ctx:
        keep = ctx.enter_context(tc.tile_pool(name="keep", bufs=1))
        psum = ctx.enter_context(tc.psum_pool(name="psum", bufs=1))
        on_scalar, on_vector = nc.scalar.copy, nc.vector.tensor_copy

        def held(name, shape, dtype, tag=None):
            return keep.tile(shape, dtype, name=name, tag=tag or name, align_bytes=256)

        def bank(index, shape, name):
            return psum.tile(shape, F32, name=name, tag="bank%d" % index)

        lists = keep.tile([P, S // LIST_ROWS], U16, name="lists")
        lists2 = keep.tile([P, S // LIST_ROWS], U16, name="lists2")
        sc_win = held("sc_win", [P, T], U8)
        sc2_win = held("sc2_win", [P, T], U8)
        wr_sc_raw = held("wr_sc_raw", [P, H], U8)
        wp_sc = held("wp_sc", [P, PASSES, K], U8)
        v_sc = [held("v_sc%d" % kp, [P, S], U8) for kp in range(PASSES)]
        rho_t = held("rho_t", [P, PACK], F32)
        gain_t = held("gain_t", [P, PACK], F32)
        w1_raw = [held("w1_raw%d" % kp, [P, PACK, H], F32) for kp in range(PASSES)]
        tab = [held("tab%d" % kp, [P, T], U32) for kp in range(PASSES)]
        tab2 = held("tab2", [P, T], U32)
        wr_raw = held("wr_raw", [P, H], U32)
        wp = [held("wp%d" % kp, [P, 2 * K], U8) for kp in range(PASSES)]
        wb_raw = {g: held("wb_raw%d" % g, [P, PACK, width], F32) for g, width in WB_LOADS.items()}
        sc_picked = held("sc_picked", [P, S], U8)
        v2_sc = held("v2_sc", [P, S], U8)
        w1_bf = {(kp, pair): held("w1_bf%d_%d" % (kp, pair), [P, PAIR * H], BF16) for kp in range(PASSES) for pair in range(2)}
        w1_q = [held("w1_q%d" % kp, [P, H], U32) for kp in range(PASSES)]
        w1_sc = [held("w1_sc%d" % kp, [P, H], U8) for kp in range(PASSES)]
        wr_q = held("wr_q", [P, H], U32)
        wr_sc = held("wr_sc", [P, H], U8)
        z_sc = [held("z_sc%d" % h, [P, HALF], U8) for h in range(2)]
        wb_sc = [held("wb_sc%d" % g, [P, CHUNK], U8) for g in range(PARTS)]
        v, v2, rho_b, a_ps, resid, bounded, z_bf, wb_bf, o_ps = {}, {}, {}, {}, {}, {}, {}, {}, {}
        z_q, wb_q, duo_ps = {}, {}, {}

        def load_words(tile, packed):
            nc.sync.dma_start(out=tile[:].bitcast(I32), in_=packed.rearrange("p c i -> p (c i)").bitcast(I32))

        def load_plane(plane, rows, first, which):
            for e in which:
                nc.sync.dma_start(out=plane[:].bitcast(I32)[first + e:P:QUADRANT], in_=rows[e].bitcast(I32))

        def load_by_slice(tile, vec):
            nc.sync.dma_start(out=tile[:], in_=vec.rearrange("(p t) -> p t", t=PACK))

        def load_w1(kp):
            rows = w1[kp * K_PASS:(kp + 1) * K_PASS, :]
            nc.sync.dma_start(out=w1_raw[kp][:], in_=rows.rearrange("(p j) r -> p j r", j=PACK))

        def load_wp(kp):
            nc.sync.dma_start(out=wp[kp][:].bitcast(I32), in_=wp_words[kp].bitcast(I32))

        def load_wb(g):
            cols = wb[:, g * CHUNK:g * CHUNK + WB_LOADS[g]]
            nc.sync.dma_start(out=wb_raw[g][:], in_=cols.rearrange("(p j) n -> p j n", j=PACK))

        def place_scales(kp):
            for e in range(PACK):
                nc.sync.dma_start(
                    out=v_sc[kp][:].bitcast(I32)[e:P:QUADRANT],
                    in_=sc_picked[:].bitcast(I32)[8 * e + 4 * kp:P:QUADRANT],
                )

        def gather(dst, window, offsets, entry, count):
            cols = slice(entry // LIST_ROWS, (entry + count) // LIST_ROWS)
            nc.vector.tensor_copy(dst, window[:].indirect(offsets[:, cols]))

        def picked(kp, entry, count):
            return v[kp, entry // HALF][:, entry % HALF:entry % HALF + count]

        def pick(kp, entry, count):
            gather(picked(kp, entry, count), tab[kp], lists, entry, count)

        def round_w1(kp, pair, copy):
            src = w1_raw[kp][:].rearrange("p j (m t) -> p m j t", t=PACK)
            copy(
                w1_bf[kp, pair][:].rearrange("p (t m j) -> p m j t", t=PAIR, j=PACK),
                src[:, :, :, PAIR * pair:PAIR * (pair + 1)],
            )

        def quantize_w1(kp, pair):
            cols = slice(pair * CHUNK, (pair + 1) * CHUNK)
            nc.vector.quantize_mx(
                out=w1_q[kp][:, cols].bitcast(FP8X4), scales=w1_sc[kp][:, cols], in_=w1_bf[kp, pair][:],
            )

        def wb_part(g):
            first = max(load for load in WB_LOADS if load <= g)
            return wb_raw[first][:, :, (g - first) * CHUNK:(g - first + 1) * CHUNK]

        def round_wb(g, copy, tag):
            wb_bf[g] = held("wb_bf%d" % g, [P, CHUNK, PACK], BF16, tag=tag)
            copy(
                wb_bf[g][:].rearrange("p (m i) j -> p m j i", i=PAIR),
                wb_part(g).rearrange("p j (m i) -> p m j i", i=PAIR),
            )

        def round_wb_gpsimd(g):
            nc.gpsimd.tensor_scalar(wb_bf[g][:], wb_part(g).rearrange("p j n -> p n j"), 1.0, 0.0, ALU.mult, ALU.add)

        def quantize_wb(g, tag=None):
            wb_q[g] = held("wb_q%d" % g, [P, CHUNK], U32, tag=tag)
            nc.vector.quantize_mx(
                out=wb_q[g][:].bitcast(FP8X4), scales=wb_sc[g][:], in_=wb_bf[g][:].rearrange("p n j -> p (n j)"),
            )

        def reference_product(h, slices, tags):
            for t in slices:
                pair, u = divmod(t, 2)
                b_ps = bank(PACK * h + t, [P, HALF], "b_ps")
                rows = slice(t * P, (t + 1) * P)
                nc.tensor.matmul_mx(
                    out=b_ps[:], lhsT=wr_q[:, rows].bitcast(FP8X4), lhsT_scale=wr_sc[WR_FIRST:P, rows],
                    rhs=v2[h][:].bitcast(FP8X4), rhs_scale=v2_sc[V2_FIRST:P, h * HALF:(h + 1) * HALF],
                    start=True, stop=True,
                )
                if (h, pair) == (0, 0):
                    for c in range(2):
                        if u == 0:
                            rho_b[c, pair] = held("rho_b%d_0" % c, [P, 2, CHUNK], F32, tag=tags[c])
                        nc.scalar.activation(
                            rho_b[c, pair][:, u, :], b_ps[:, c * CHUNK:(c + 1) * CHUNK],
                            ACT.Copy, scale=rho_t[:, t:t + 1],
                        )
                else:
                    if u == 0:
                        both = held("rho_b_half%d_%d" % (h, pair), [P, 2, 2, CHUNK], F32, tag=tags[pair])
                        for c in range(2):
                            rho_b[2 * h + c, pair] = both[:, c]
                    nc.scalar.activation(
                        both[:, :, u, :], b_ps[:].rearrange("p (c j) -> p c j", c=2), ACT.Copy, scale=rho_t[:, t:t + 1],
                    )

        def a_pass(c, pair, kp, opens):
            for u in range(2):
                rows = slice((2 * pair + u) * P, (2 * pair + u + 1) * P)
                nc.tensor.matmul_mx(
                    out=a_ps[c, pair][:, u, :], lhsT=w1_q[kp][:, rows].bitcast(FP8X4), lhsT_scale=w1_sc[kp][:, rows],
                    rhs=picked(kp, c * CHUNK, CHUNK).bitcast(FP8X4),
                    rhs_scale=v_sc[kp][:, c * CHUNK:(c + 1) * CHUNK],
                    start=(opens and u == 0), stop=(not opens and u == 1),
                )

        def subtract(c, pair, cols=slice(0, CHUNK)):
            two = slice(2 * pair, 2 * pair + 2)
            nc.vector.tensor_tensor(
                resid[c][:, two, cols], rho_b[c, pair][:, :, cols], a_ps[c, pair][:, :, cols], ALU.subtract,
            )

        def bound(c, cols=slice(0, CHUNK)):
            if cols.start == 0:
                bounded[c] = held("bounded%d" % c, [P, CHUNK, PACK], F32)
            nc.scalar.activation(
                bounded[c][:, cols].rearrange("p (m i) t -> p m t i", i=PAIR),
                resid[c][:, :, cols].rearrange("p t (m i) -> p m t i", i=PAIR),
                ACT.Tanh,
            )

        def weigh(c, engine, tag=None, cols=slice(0, CHUNK)):
            if c not in z_bf:
                z_bf[c] = held("z_bf%d" % c, [P, CHUNK, PACK], BF16, tag=tag)
            spread = gain_t[:].unsqueeze(1).to_broadcast([P, cols.stop - cols.start, PACK])
            engine.tensor_tensor(z_bf[c][:, cols], bounded[c][:, cols], spread, ALU.mult)

        def quantize_z(c):
            if c % 2 == 0:
                z_q[c // 2] = held("z_q%d" % (c // 2), [P, HALF], U32)
            cols = slice((c % 2) * CHUNK, (c % 2 + 1) * CHUNK)
            nc.vector.quantize_mx(
                out=z_q[c // 2][:, cols].bitcast(FP8X4), scales=z_sc[c // 2][:, cols],
                in_=z_bf[c][:].rearrange("p j t -> p (j t)"),
            )

        def calibrate(h, n, index):
            o_ps[h, n] = bank(index, [P, HALF], "o_ps")
            for kp in range(PASSES):
                nc.tensor.matmul_mx(
                    out=o_ps[h, n][:], lhsT=wp[kp][:, 2 * n * P:2 * (n + 1) * P].bitcast(FP4X4),
                    lhsT_scale=wp_sc[:, kp, n * P:(n + 1) * P],
                    rhs=picked(kp, h * HALF, HALF).bitcast(FP8X4), rhs_scale=v_sc[kp][:, h * HALF:(h + 1) * HALF],
                    start=(kp == 0), stop=False,
                )

        def correct(h, n):
            g, rows = n // 2, slice((n % 2) * P, (n % 2 + 1) * P)
            nc.tensor.matmul_mx(
                out=o_ps[h, n][:], lhsT=wb_q[g][:, rows].bitcast(FP8X4), lhsT_scale=wb_sc[g][:, rows],
                rhs=z_q[h][:].bitcast(FP8X4), rhs_scale=z_sc[h][:], start=False, stop=True,
            )

        def finish(h, n, copy):
            result = held("result%d_%d" % (h, n), [P, HALF], F32)
            copy(result[:], o_ps[h, n][:])
            nc.sync.dma_start(out=out[n * P:(n + 1) * P, h * HALF:(h + 1) * HALF], in_=result[:])

        def calibrate_duo(c, g, index):
            duo_ps[c, g] = bank(index, [P, 2, CHUNK], "p_ps")
            for u in range(2):
                n = 2 * g + u
                for kp in range(PASSES):
                    nc.tensor.matmul_mx(
                        out=duo_ps[c, g][:, u, :], lhsT=wp[kp][:, 2 * n * P:2 * (n + 1) * P].bitcast(FP4X4),
                        lhsT_scale=wp_sc[:, kp, n * P:(n + 1) * P],
                        rhs=picked(kp, c * CHUNK, CHUNK).bitcast(FP8X4), rhs_scale=v_sc[kp][:, c * CHUNK:(c + 1) * CHUNK],
                        start=(u == 0 and kp == 0), stop=False,
                    )

        def correct_duo(c, g):
            cols = slice((c % 2) * CHUNK, (c % 2 + 1) * CHUNK)
            for u in range(2):
                rows = slice(u * P, (u + 1) * P)
                nc.tensor.matmul_mx(
                    out=duo_ps[c, g][:, u, :], lhsT=wb_q[g][:, rows].bitcast(FP8X4), lhsT_scale=wb_sc[g][:, rows],
                    rhs=z_q[c // 2][:, cols].bitcast(FP8X4), rhs_scale=z_sc[c // 2][:, cols], start=False, stop=(u == 1),
                )

        def finish_duo(c, g, copy):
            result = held("part%d_%d" % (c, g), [P, 2, CHUNK], F32)
            copy(result[:], duo_ps[c, g][:])
            rows = out[2 * g * P:2 * (g + 1) * P, c * CHUNK:(c + 1) * CHUNK]
            nc.sync.dma_start(out=rows.rearrange("(u p) j -> p u j", u=2), in_=result[:])

        def residual(c):
            for pair in range(2):
                subtract(c, pair)

        def a_first(c, kp, index):
            for pair in range(2):
                a_ps[c, pair] = bank(index + pair, [P, 2, CHUNK], "a_ps")
                a_pass(c, pair, kp, True)

        def a_second(c, kp):
            for pair in range(2):
                a_pass(c, pair, kp, False)

        nc.gpsimd.memset(sc_win[:].bitcast(I32), 0)
        nc.vector.memset(sc2_win[:].bitcast(I32), 0)
        nc.vector.memset(wr_sc_raw[:].bitcast(I32), 0)
        for kp in range(PASSES):
            nc.vector.memset(v_sc[kp][:].bitcast(I32), 0)
        nc.vector.memset(wp_sc[:].bitcast(I32), 0)

        wr_rows = wr_scales[0].rearrange("(d e) c -> e d c", e=PACK)
        wp_rows = wp_scales.rearrange("kp (d e) c -> e d kp c", e=PACK)
        v2_rows = tab2_scales[0].rearrange("(d e) t -> e d t", e=PACK)
        nc.sync.dma_start(lists[:], offs)
        load_words(wr_raw, wr_words[0])
        load_by_slice(rho_t, rho)
        nc.sync.dma_start(lists2[:], offs2)
        nc.sync.dma_start(
            out=sc_win[:].bitcast(I32)[0:P:PACK, :],
            in_=tab_scales.rearrange("kp q t -> q kp t").bitcast(I32),
        )
        load_plane(sc2_win, v2_rows, V2_FIRST, range(2))
        load_words(tab2, tab2_words[0])
        load_plane(sc2_win, v2_rows, V2_FIRST, range(2, PACK))
        load_plane(wr_sc_raw, wr_rows, WR_FIRST, range(2))
        load_w1(0)
        load_plane(wr_sc_raw, wr_rows, WR_FIRST, range(2, PACK))
        load_w1(1)
        load_words(tab[0], tab_words[0])
        gather(sc_picked[:], sc_win, lists, 0, S)
        place_scales(0)
        load_words(tab[1], tab_words[1])
        place_scales(1)
        load_wb(0)
        load_wb(1)
        load_by_slice(gain_t, gain)
        load_wp(0)
        load_plane(wp_sc, wp_rows, 0, range(PACK))
        load_wp(1)
        load_wb(2)

        gather(v2_sc[:], sc2_win, lists2, 0, S)
        for h in range(2):
            v2[h] = held("v2_%d" % h, [P, HALF], U32)
            gather(v2[h][:], tab2, lists2, h * HALF, HALF)
        nc.gpsimd.tensor_copy(
            wr_q[:].bitcast(I32).rearrange("p (t m) -> p t m", t=PACK),
            wr_raw[:].bitcast(I32).rearrange("p (m t) -> p t m", t=PACK),
        )
        nc.gpsimd.tensor_copy(
            wr_sc[:].rearrange("p (t m) -> p t m", t=PACK),
            wr_sc_raw[:].rearrange("p (m t) -> p t m", t=PACK),
        )
        for pair in range(2):
            round_w1(0, pair, on_scalar)
        round_w1(1, 0, on_scalar)
        round_w1(1, 1, on_vector)
        for kp, pair in ((0, 0), (0, 1), (1, 1), (1, 0)):
            quantize_w1(kp, pair)
        reference_product(0, range(2), ("w1_raw0", "w1_bf0_1"))
        reference_product(1, range(2), ("w1_raw1", None))
        reference_product(0, range(2, PACK), (None, "w1_bf1_1"))
        reference_product(1, range(2, PACK), (None, "w1_bf1_0"))
        for h in range(2):
            v[0, h] = held("v0_%d" % h, [P, HALF], U32)
            pick(0, h * HALF, HALF)
        for c in (0, 2):
            a_first(c, 0, 2 * c)

        v[1, 0] = held("v1_0", [P, HALF], U32)
        for c in range(2):
            pick(1, c * CHUNK, CHUNK)
        a_second(0, 1)
        a_first(1, 1, 2)
        a_second(1, 0)
        for c in range(CHUNKS):
            resid[c] = held("resid%d" % c, [P, PACK, CHUNK], F32)
        stage = held("stage", [P, SHARE + CHUNK, PACK], BF16)
        z_bf[1], wb_bf[0] = stage[:, 0:CHUNK], stage[:, SHARE:SHARE + CHUNK]
        round_wb_gpsimd(0)
        for cols in (slice(0, CHUNK // 2), slice(CHUNK // 2, CHUNK)):
            for pair in range(2):
                subtract(0, pair, cols)
            bound(0, cols)
            weigh(0, nc.gpsimd, "wb_raw0", cols)
        a_first(3, 0, 0)
        round_wb(1, on_scalar, tag="resid0")
        v[1, 1] = held("v1_1", [P, HALF], U32, tag="w1_raw0")
        for c in range(2, CHUNKS):
            pick(1, c * CHUNK, CHUNK)
            a_second(c, 1)
        residual(1)
        bound(1, slice(0, SHARE))
        weigh(1, nc.gpsimd, None, slice(0, SHARE))
        bound(1, slice(SHARE, CHUNK))
        for c in range(2, CHUNKS):
            residual(c)
            bound(c)

        for c in range(2):
            for g in range(DUOS):
                calibrate_duo(c, g, FREED[DUOS * c + g])
        for n in range(WHOLE, WHOLE + 2):
            calibrate(0, n, FREED[n])
        quantize_wb(0, tag="bounded0")
        quantize_z(0)
        correct_duo(0, 0)
        finish_duo(0, 0, on_scalar)
        calibrate(0, TILES - 2, FREED[TILES - 2])
        weigh(1, nc.vector, None, slice(SHARE, CHUNK))
        quantize_wb(1, tag="wb_raw0")
        quantize_z(1)
        for c, g in ((0, 1), (1, 0), (1, 1)):
            correct_duo(c, g)
            finish_duo(c, g, on_scalar)
        calibrate(0, TILES - 1, FREED[TILES - 1])
        calibrate(1, 0, FREED[0])
        round_wb(2, on_vector, tag="bounded1")
        round_wb(3, on_vector, tag="resid0")
        quantize_wb(2)
        quantize_wb(3)
        weigh(2, nc.vector, tag="wb_raw2")
        weigh(3, nc.vector, tag="bounded1")
        quantize_z(2)
        quantize_z(3)
        for g in (2, 3):
            for n in (2 * g, 2 * g + 1):
                correct(0, n)
                finish(0, n, on_scalar)
            calibrate(1, g - 1, FREED[g - 1])
        calibrate(1, 3, FREED[3])

        for n in range(TILES):
            if n >= WHOLE:
                calibrate(1, n, FREED[n])
            correct(1, n)
            finish(1, n, on_vector if n % 2 else on_scalar)
